import numpy as np, ml_dtypes
CORES = [6,15,38,47]
N = 4
BF = ml_dtypes.bfloat16
def gentries(a):
    return np.ascontiguousarray(a.reshape(8, 16, -1).transpose(0, 2, 1)).reshape(8, -1)
def gtable(e):
    e = np.asarray(e); return np.ascontiguousarray(e.reshape(8, -1, 16).transpose(0, 2, 1)).reshape(128, -1).astype(np.int32)
W, I, J, A, B, P, RO = 4096, 2048, 1536, 8, 8, 128, 4
def column(i, j):
    return ((((2 * i + 1) * (2 * j + 1)) >> 5) + 37 * i + j) & (W - 1)
def sized(rng, n, lo, hi, noise):
    b = np.exp2(lo + (hi - lo) * rng.random((N, 8, 1, n), dtype=np.float32))
    return (b * np.exp2(noise * (2 * rng.random((N, 8, 16, n), dtype=np.float32) - 1))).astype(np.int64)
def parts(rng):
    v = np.minimum(np.maximum(sized(rng, W, 2.6, 6.8, 0.5), 1), 127)
    rl = rng.integers(0, J, (N, 8, 16, I)); cl = rng.integers(0, I, (N, 8, 16, J))
    i = rng.integers(0, I, (N, 8, P)); j = rng.integers(0, J, (N, 8, P))
    return v, rl, cl, i, j, np.minimum(sized(rng, P, 1.0, 6.0, 0.5), 127)
def pack(v, rl, cl, i, j, z):
    return {"fig": np.ascontiguousarray(v.reshape(N, 128, W)).astype(np.float32).astype(BF), "rmate": np.ascontiguousarray(rl.reshape(N, 128, I)).astype(np.int32), "cmate": np.ascontiguousarray(cl.reshape(N, 128, J)).astype(np.int32),
            "prow": np.stack([gtable(a) for a in i]), "pcol": np.stack([gtable(a) for a in j]), "need": np.ascontiguousarray(z.reshape(N, 128, P)).astype(np.float32).astype(BF)}
def some(rng, good, free):
    n = np.flatnonzero(good & free)
    if len(n) == 0: n = np.flatnonzero(free)
    return n[rng.integers(0, len(n), 128)]
def fill(rng, v, rl, cl, i, j, z, g):
    v[:, g] = 40 + np.argsort(rng.random((N, 16, W)), axis=1); z[:, g] = 0
    seen = np.zeros((N, W), bool); rows = np.zeros((N, I), bool); cols = np.zeros((N, J), bool); ai = np.arange(I); aj = np.arange(J)
    for q in range(N):
        i[q, g] = rng.permutation(I)[:P]; j[q, g] = rng.permutation(J)[:P]; rows[q, i[q, g]] = True; cols[q, j[q, g]] = True
    x = np.array(i[:, g]); y = np.array(j[:, g])
    for t in range(RO):
        if t == RO - 1: rows[:] = False; cols[:] = False
        nx = np.zeros_like(x); ny = np.zeros_like(y)
        for q in range(N):
            to = (q + 1 + t % 3) % N
            for k in range(P):
                a, b = int(x[q, k]), int(y[q, k])
                u = some(rng, ~seen[q][column(a, aj)], ~cols[to]); w = some(rng, ~seen[q][column(ai, b)], ~rows[to])
                c = np.stack([column(a, u), column(w, b), column(w, u)])
                n = int(np.argmax(~seen[q][c[2]] & (c[0] != c[1]) & (c[0] != c[2]) & (c[1] != c[2])))
                seen[q, c[:, n]] = True; cols[to, u[n]] = True; rows[to, w[n]] = True
                rl[q, g, :, a] = u[n]; cl[q, g, :, b] = w[n]; nx[to, k] = w[n]; ny[to, k] = u[n]
        x, y = nx, ny
def setup_inputs(rng):
    return pack(*parts(rng))
def setup_inputs_ties(rng):
    v, rl, cl, i, j, z = parts(rng)
    v = rng.choice(np.array([8, 16, 32, 64]), (N, 8, 1, W)) + np.zeros((1, 1, 16, 1), np.int64)
    low = (rng.random((N, 8, 1, W)) < 0.3) & (np.arange(16)[:, None] == rng.integers(0, 16, (N, 8, 1, W)))
    z = rng.choice(np.array([0, 1, 8, 9, 16, 32, 33, 64, 65]), (N, 8, 1, P)) + np.zeros((1, 1, 16, 1), np.int64)
    v = v - low; fill(rng, v, rl, cl, i, j, z, 3)
    return pack(v, rl, cl, i, j, z)
def setup_inputs_none(rng):
    v, rl, cl, i, j, z = parts(rng)
    h = int(rng.integers(0, 8)); z[int(rng.integers(0, N))] = 0; z[:, h] = 127; v[:, h] = np.minimum(v[:, h], 126)
    for g, a, b in (((h + 1) % 8, A - 1, B - 1), ((h + 2) % 8, 0, 0)):
        v[:, g] = np.minimum(v[:, g], 10); z[:, g] = rng.integers(20, 30, (N, 16, P))
        for q in range(N):
            for k in range(8):
                x, y = int(i[q, g, k]), int(j[q, g, k]); u, w = int(rl[q, g, a, x]), int(cl[q, g, b, y])
                for c in (column(x, u), column(w, y), column(w, u)): v[q, g, :, c] = 127
    return pack(v, rl, cl, i, j, z)
def setup_inputs_alike(rng):
    v, rl, cl, i, j, z = parts(rng); z = z // 4
    i[:, [0, 4]] = i[:, [0, 4], :1]; j[:, [0, 4]] = j[:, [0, 4], :1]; z[:, [0, 4]] = z[:, [0, 4], :, :1]
    rl[:, [1, 5]] = rng.choice(np.array([0, 5, J - 1]), (N, 2, 16, I)); cl[:, [1, 5]] = rng.choice(np.array([0, 7, I - 1]), (N, 2, 16, J))
    i[:, 2] = rng.choice(np.array([0, 1, I // 2, I - 1]), (N, P)); j[:, 2] = rng.choice(np.array([0, 1, J // 2, J - 1]), (N, P))
    rl[:, 6] = rl[:, 6, :1]; cl[:, 6] = cl[:, 6, :1]
    for q in range(N):
        rl[q, 7, 0, i[q, 7]] = j[q, 7]; cl[q, 7, 0, j[q, 7]] = i[q, 7]
        cl[q, 4, :, int(j[q, 4, 0])] = int(i[q, 4, 0])
    z[:, 4] = 0
    rl[:, 3] = np.where(rng.random((N, 16, I)) < 0.5, rng.choice(np.array([0, J - 1]), (N, 16, I)), rl[:, 3])
    cl[:, 3] = np.where(rng.random((N, 16, J)) < 0.5, rng.choice(np.array([0, I - 1]), (N, 16, J)), cl[:, 3])
    i[:, 3] = np.where(rng.random((N, P)) < 0.5, rng.choice(np.array([0, I - 1]), (N, P)), i[:, 3])
    j[:, 3] = np.where(rng.random((N, P)) < 0.5, rng.choice(np.array([0, J - 1]), (N, P)), j[:, 3])
    return pack(v, rl, cl, i, j, z)
def setup_inputs_late(rng):
    v, rl, cl, i, j, z = parts(rng); z = z // 4
    for g in range(8):
        s = rng.permutation(16)
        for q in range(N):
            a, b = int(s[q % 2]), int(s[1 - q % 2])
            v[q, g, a] = np.minimum(v[q, g, a], 12); z[q, g, a] = rng.integers(13, 30, P); z[q, g, b] = np.minimum(z[q, g, b], 6)
    return pack(v, rl, cl, i, j, z)
def setup_inputs_spread(rng):
    v, rl, cl, i, j, z = parts(rng)
    v = np.minimum(np.maximum(sized(rng, W, 0.0, 7.3, 0.3), 1), 127)
    z = np.minimum(sized(rng, P, -1.0, 7.2, 0.2), 127)
    v[:, 2] = rng.integers(123, 128, (N, 16, W)); z[:, 2] = np.minimum(z[:, 2], 60)
    v[:, 5] = np.where(rng.random((N, 1, W)) < 0.5, 127, 1); z[:, 5] = 127
    return pack(v, rl, cl, i, j, z)
def check_inputs(d):
    bad = []
    for k, lo, hi in (("fig", 1, 127), ("rmate", 0, J - 1), ("cmate", 0, I - 1), ("prow", 0, I - 1), ("pcol", 0, J - 1), ("need", 0, 127)):
        v = np.asarray(d[k]).astype(np.float64)
        if not (np.all(v >= lo) and np.all(v <= hi) and np.all(v == np.floor(v))): bad.append("range of " + k)
    return bad
def look(h, c, z):
    m = c.shape[1]; v = np.take_along_axis(h, c.reshape(8, 1, m * P), 2).reshape(8, 16, m, P)
    return np.all(np.abs(v) >= z[:, :, None, :], axis=1), np.sum(np.maximum(v, 0), axis=1)
def reference(fig, rmate, cmate, prow, pcol, need):
    h = fig.astype(np.float32).astype(np.int32).reshape(N, 8, 16, W); z = need.astype(np.float32).astype(np.int32).reshape(N, 8, 16, P)
    rm = rmate.astype(np.int64).reshape(N, 8, 16, I); cm = cmate.astype(np.int64).reshape(N, 8, 16, J)
    i = np.stack([gentries(a) for a in prow]).astype(np.int64); j = np.stack([gentries(a) for a in pcol]).astype(np.int64)
    cost = np.zeros((N, 8, RO, P), np.float32); gi = np.arange(8)[:, None] + np.zeros((1, P), np.int64)
    for t in range(RO):
        ra = A * (t % (16 // A)); rb = B * (t % (16 // B)); sh = 1 + t % 3
        ni, nj, nz = [None] * N, [None] * N, [None] * N
        for q in range(N):
            x, y = i[q], j[q]
            jm = np.take_along_axis(rm[q][:, ra:ra + A], x[:, None, :], 2)
            im = np.take_along_axis(cm[q][:, rb:rb + B], y[:, None, :], 2)
            ok1, c1 = look(h[q], column(x[:, None, :], jm), z[q]); ok2, c2 = look(h[q], column(im, y[:, None, :]), z[q])
            ok3, c3 = look(h[q], column(im[:, None, :, :], jm[:, :, None, :]).reshape(8, A * B, P), z[q])
            ok = (ok1[:, :, None, :] & ok2[:, None, :, :]).reshape(8, A * B, P) & ok3
            total = (c1[:, :, None, :] + c2[:, None, :, :]).reshape(8, A * B, P) + c3
            total = np.where(ok, total, 2 ** 20)
            best = np.argmin(total, axis=1); good = np.any(ok, axis=1)
            cost[q, :, t] = np.where(good, np.take_along_axis(total, best[:, None, :], 1)[:, 0], -1)
            u = np.take_along_axis(jm, (best // B)[:, None, :], 1)[:, 0]; w = np.take_along_axis(im, (best % B)[:, None, :], 1)[:, 0]
            far = column(w, u); hit = np.zeros((8, W), bool)
            for c in (column(x, u), column(w, y), far): hit[gi[good], c[good]] = True
            size = np.abs(h[q]); fresh = np.take_along_axis(size, far[:, None, :], 2) >> 1
            h[q] = np.where(hit[:, None, :], -size, h[q])
            to = (q + sh) % N
            ni[to] = np.where(good, w, x); nj[to] = np.where(good, u, y); nz[to] = np.where(good[:, None, :], fresh, z[q])
        i = np.stack(ni); j = np.stack(nj); z = np.stack(nz)
    yp = np.stack([gtable(np.concatenate([i[q], j[q]], axis=1)) for q in range(N)])
    return {"yf": h.reshape(N, 128, W).astype(np.float32).astype(BF), "yp": yp.astype(np.float32), "yz": z.reshape(N, 128, P).astype(np.float32).astype(BF), "yc": cost.reshape(N, 8, RO * P)}

@@ -1,0 +1,519 @@
+from concourse.mybir import AluOpType as A, ActivationFunctionType as F
+
+ROT = 315
+W, NI, NJ = 4096, 2048, 1536
+BAD = float(2 ** 20)
+CLIP = float(2 ** 20 - 64)
+PC = 17704.5
+ROUNDS = 4
+NS = [4, 4, 4, 6]
+NSM = 6
+
+SB = {}
+POOL = {}
+USED = {"poolF": 0, "poolI": 0}
+
+
+def _sb(names, shape, dtype="float32"):
+    for n in names.split():
+        SB[n] = ("sbuf", [128] + shape, dtype)
+
+
+def _small(names, width, dtype="float32"):
+    p = "poolF" if dtype == "float32" else "poolI"
+    for n in names.split():
+        POOL[n] = (p, USED[p], width)
+        USED[p] += width
+
+
+_small("rhoI Pi far2 FC3", 8, "int32")
+_small("KJ k0 k1 gn PP t8 kj P8 MB", 8)
+_small("mki cI", 8 * ROUNDS, "int32")
+_small("G cf cst", 8 * ROUNDS)
+_small("XYi", 16, "int32")
+_small("XYf UWO UWN T16 H16 PH YP", 16)
+_small("QC", 24, "int32")
+_small("HLi", 48, "int32")
+_small("HLf", 48)
+_small("SP SN", NSM)
+_small("T32 MA", 32)
+_small("M2", 64)
+_small("PI P15i", 1, "int32")
+_small("PF P15 G16 SLO SHI SCA BIA SCB BIB CWT CW2 PKC PM PMA QA QB QB8 QJ1 QJ2 QJ3", 1)
+_sb("poolF", [USED["poolF"]])
+_sb("poolI", [USED["poolI"]], "int32")
+_sb("prowI pcolI", [8], "int32")
+_sb("rhoU farU", [8], "uint16")
+for _t in range(ROUNDS + 1):
+    _sb("XY%d" % _t, [16], "uint16")
+    _sb("Z%d" % _t, [128], "bfloat16")
+_sb("XYs", [16], "uint16")
+_sb("Zs", [128], "bfloat16")
+_sb("XM0 XM1", [NI], "int32")
+_sb("MW", [W + 128], "bfloat16")
+_sb("CW YF", [W], "bfloat16")
+_sb("IOTA", [NI])
+_sb("ONE BT BB OFF C16 C8 CAL MI NPC", [128])
+_sb("C16b IDb HIO", [128], "bfloat16")
+_sb("sJ0 sJ1 sJ2 sJ3 sA sB sI PK IDf DMK", [128])
+_sb("SEL SELC EXPM", [16, 128], "bfloat16")
+_sb("RHO", [512], "bfloat16")
+_sb("RST", [256])
+_sb("M1", [512])
+_sb("OHA OHB T64", [64])
+_sb("OHW", [80])
+_sb("LIO SG", [256], "bfloat16")
+_sb("R2 C2 U WN OT IPs MT2s NM NMm", [128])
+_sb("K2Y", [8, 16])
+_sb("K1s", [4, 8, 2])
+_sb("F12q F12i", [128], "int32")
+_sb("F12u", [128], "uint16")
+_sb("F3q F3i", [512], "int32")
+_sb("F3u", [512], "uint16")
+_sb("Zr E12v E12c", [2048], "bfloat16")
+_sb("E3v E3c", [8192], "bfloat16")
+_sb("HOH", [24, 128], "bfloat16")
+_sb("LOH", [24, 256], "bfloat16")
+_sb("ST1 ST2", [NSM, 256], "bfloat16")
+_sb("CSi HCi LCi", [256], "int32")
+_sb("HLC", [2, 256], "bfloat16")
+_sb("YZ", [128], "bfloat16")
+for _n in ("pJP", "pM", "pM2", "pA", "pB", "pN", "pH"):
+    SB[_n] = ("psum", [128, 512], "float32")
+SB["pK"] = ("psum", [128, 8, 16], "float32")
+PSUMS = ("pJP", "pM", "pM2", "pA", "pB", "pN", "pH", "pK")
+SCRATCH = SB
+NDMA = 60
+SEMAPHORES = ["qv", "qt", "qs", "qg"] + ["d%d" % k for k in range(NDMA)] + \
+    [p + "%d" % k for p in ("rn", "rz", "ln", "lz") for k in range(ROUNDS)]
+
+
+def rank_program(g, core, T, topo):
+    rank = T.rank_of(core)
+    if rank is None:
+        return
+    queues = {"v": g.vector, "t": g.tensor, "s": g.scalar, "g": g, "y": g.sync}
+    count = {}
+    known = {q: {} for q in queues}
+    past = {}
+    ndma = [0]
+
+    def need_waits(q, reads, writes, is_dma):
+        deps = []
+        for regs, w in ((reads, False), (writes, True)):
+            for (n, lo, hi) in regs:
+                bank = n in PSUMS
+                for (plo, phi, pw, pq, sem, val, kn) in past.get(n, ()):
+                    same = pq == q and not is_dma
+                    if bank:
+                        if same and not (pw or w):
+                            continue
+                    elif phi <= lo or plo >= hi or not (pw or w):
+                        continue
+                    if same and (q == "t" or not pw):
+                        continue
+                    deps.append((sem, val, kn))
+        for sem, val, kn in sorted(deps, key=lambda d: -d[1]):
+            if known[q].get(sem, 0) < val:
+                queues[q].wait_ge(T.sem[sem], val)
+                known[q][sem] = val
+                for s2, v2 in kn.items():
+                    if known[q].get(s2, 0) < v2:
+                        known[q][s2] = v2
+
+    def note(q, sem, val, reads, writes, kn):
+        for regs, w in ((reads, False), (writes, True)):
+            for (n, lo, hi) in regs:
+                lst = past.setdefault(n, [])
+                if n in PSUMS:
+                    lst[:] = [p for p in lst if not (p[3] == q and (w or not p[2]) and lo <= p[0] and p[1] <= hi)]
+                elif w:
+                    lst[:] = [p for p in lst if not (lo <= p[0] and p[1] <= hi)]
+                lst.append((lo, hi, w, q, sem, val, kn))
+
+    def regs_of(*refs):
+        out = []
+        for r in refs:
+            if isinstance(r, tuple):
+                out += r[1]
+        return out
+
+    def emit(q, call, reads, writes):
+        sem = "q" + q
+        need_waits(q, reads, writes, False)
+        inst = call()
+        count[sem] = count.get(sem, 0) + 1
+        inst.then_inc(T.sem[sem], 1)
+        note(q, sem, count[sem], reads, writes, dict(known[q]))
+
+    def dma(q, out, in_):
+        sem = "d%d" % ndma[0]
+        ndma[0] += 1
+        need_waits(q, in_[1], out[1], True)
+        queues[q].dma_start(out[0], in_[0]).then_inc(T.sem[sem], 16)
+        count[sem] = 16
+        note(sem, sem, 16, in_[1], out[1], dict(known[q]))
+
+    def R(n, lo=0, hi=None, step=1):
+        if n in POOL:
+            p, base, width = POOL[n]
+            hi = width if hi is None else hi
+            n, lo, hi = p, base + lo, base + hi
+        elif hi is None:
+            hi = SB[n][1][1]
+        return (T[n][:, lo:hi:step] if step > 1 else T[n][:, lo:hi], [(n, lo, hi)])
+
+    def X(ap, n, lo=0, hi=1 << 20):
+        return (ap, [(n, lo, hi)])
+
+    def IND(win, offs):
+        return (win[0].indirect(offs[0]), win[1] + offs[1])
+
+    def val(x):
+        return x[0] if isinstance(x, tuple) else x
+
+    def TT(out, a, b, op):
+        emit("v", lambda: g.vector.tensor_tensor(out[0], a[0], b[0], op), regs_of(a, b), out[1])
+
+    def TS(out, a, s1, s2, op0, op1=None):
+        if op1 is None:
+            emit("v", lambda: g.vector.tensor_scalar(out[0], a[0], val(s1), None, op0), regs_of(a, s1), out[1])
+        else:
+            emit("v", lambda: g.vector.tensor_scalar(out[0], a[0], val(s1), val(s2), op0, op1), regs_of(a, s1, s2), out[1])
+
+    def TC(out, a):
+        emit("v", lambda: g.vector.tensor_copy(out[0], a[0]), regs_of(a), out[1])
+
+    def MS(out, c):
+        emit("v", lambda: g.vector.memset(out[0], c), [], out[1])
+
+    def SCAN(out, d0, d1, init, op0, op1):
+        emit("v", lambda: g.vector.tensor_tensor_scan(out[0], d0[0], d1[0], init, op0, op1), regs_of(d0, d1), out[1])
+
+    def ACT(out, a, func, bias=0.0, scale=1.0):
+        emit("s", lambda: g.scalar.activation(out[0], a[0], func, bias=val(bias), scale=val(scale)), regs_of(a, bias, scale), out[1])
+
+    def MM(out, pairs, start=True, stop=True):
+        def go():
+            inst = None
+            for k, (l, r) in enumerate(pairs):
+                inst = g.tensor.matmul(out[0], l[0], r[0], start and k == 0, stop and k == len(pairs) - 1)
+            return inst
+        emit("t", go, regs_of(*[r for p in pairs for r in p]), out[1])
+
+    def IOTA(out, pattern, base, cm, f=True):
+        if f:
+            emit("g", lambda: g.iota(out[0], pattern, base, cm, allow_small_or_imprecise_dtypes=True), [], out[1])
+        else:
+            emit("g", lambda: g.iota(out[0], pattern, base, cm), [], out[1])
+
+    def AFF(out, in_, pattern, op, fill, base, cm):
+        emit("g", lambda: g.affine_select(out[0], in_[0], pattern, op, fill, base, cm), in_[1], out[1])
+
+    def remote(t, kind, dst, src):
+        sh = 1 + t % 3
+        to = T.cores[(rank + sh) % 4]
+        rid, pid, _ = topo.addr(to)
+        ls, rs = "l%s%d" % (kind, t), "r%s%d" % (kind, t)
+        need_waits("g", src[1], [], True)
+        g.remote_dma(T[dst][:], src[0], T.sem[rs], T.sem[ls], pid, rid, topo.mask(core, to))
+        count[ls] = len(topo.engines(core, to))
+        note(ls, ls, count[ls], src[1], [], dict(known["g"]))
+        frm = T.cores[(rank - sh) % 4]
+        count[rs] = len(topo.engines(frm, core))
+        note(rs, rs, count[rs], [], [(dst, 0, SB[dst][1][1])], {})
+
+    eq, ge, SHR, AND = A.is_equal, A.is_ge, A.arith_shift_right, A.bitwise_and
+    EXT = []
+
+    def mates(h, qs):
+        n = "XM%d" % h
+        for k in range(8):
+            dma(qs[k % 2], X(T[n][16 * k:16 * k + 8, 0:NI], n, k, k + 1), (T.rmate[16 * k + 8 * h:16 * k + 8 * h + 8, :], EXT))
+        for k in range(8):
+            dma(qs[k % 2], X(T[n][16 * k + 8:16 * k + 16, 0:NJ], n, 8 + k, 9 + k), (T.cmate[16 * k + 8 * h:16 * k + 8 * h + 8, :], EXT))
+    dma("y", R("prowI"), (T.prow[:], EXT))
+    dma("s", R("pcolI"), (T.pcol[:], EXT))
+    dma("y", R("MW", ROT, W), (T.fig[:, 0:W - ROT], EXT))
+    dma("s", R("MW", 0, ROT), (T.fig[:, W - ROT:W], EXT))
+    MS(X(T.XM0[:, NJ:NI], "XM0"), 0)
+    mates(0, "ys")
+    dma("s", R("Z0"), (T.need[:], EXT))
+
+    MS(R("ONE"), 1.0)
+    MS(R("CW"), 0.0)
+    IOTA(R("PI"), [[1, 1]], 0, 1, False)
+    AFF(R("BT"), R("ONE"), [[-16, 8], [0, 16]], ge, 0.0, 0, 1)
+    AFF(R("BB"), R("BT"), [[16, 8], [0, 16]], ge, 0.0, 15, -1)
+    IOTA(R("C16"), [[0, 8], [1, 16]], 0, 0)
+    IOTA(R("C8"), [[0, 16], [1, 8]], 0, 0)
+    IOTA(R("CAL"), [[0, 8], [1, 2], [0, 8]], 0, 0)
+    IOTA(R("IOTA"), [[1, NI]], 0, 0)
+    IOTA(R("MI"), [[1, 128]], 0, 0)
+    IOTA(R("LIO"), [[1, 256]], 0, 0)
+    IOTA(R("RHO"), [[16, 4], [0, 8], [1, 16]], 0, 0)
+    IOTA(R("OHA"), [[1, 8], [0, 8]], 0, 0)
+    IOTA(R("OHB"), [[0, 8], [1, 8]], 8, 0)
+    IOTA(R("DMK"), [[1, 8], [0, 8], [8, 2]], 0, 0)
+    IOTA(R("KJ"), [[16, 8]], W, 0)
+    IOTA(R("H16"), [[1, 16]], 0, 0)
+    IOTA(R("RST"), [[0, 32], [1, 8]], 0, 0)
+
+    TS(R("P15i"), R("PI"), 15, None, AND)
+    TC(R("PF"), R("PI"))
+    TC(R("P15"), R("P15i"))
+    TS(R("OFF"), R("BB"), -999.0, 999.0, A.mult, A.add)
+    TT(R("C16"), R("C16"), R("OFF"), A.add)
+    TC(R("C16b"), R("C16"))
+    for c in range(16):
+        TS(X(T.SEL[:, c, :], "SEL", c, c + 1), R("C16b"), float(c), BAD, eq, A.mult)
+    TS(R("SLO"), R("P15"), 8.0, None, A.is_lt)
+    TS(R("SHI"), R("P15"), 8.0, None, ge)
+    TS(R("SCA"), R("SLO"), 2.0, None, A.mult)
+    TS(R("BIA"), R("SLO"), 17.0, None, A.mult)
+    TS(R("SCB"), R("SHI"), 2.0, None, A.mult)
+    TS(R("BIB"), R("SHI"), 593.0, None, A.mult)
+    TS(R("PM"), R("SHI"), -50.0, None, A.mult)
+    TT(R("QA"), R("P15"), R("PM"), A.add)
+    TS(R("PMA"), R("SLO"), -50.0, -8.0, A.mult, A.add)
+    TT(R("QB"), R("P15"), R("PMA"), A.add)
+    TS(R("QB8"), R("QB"), 8.0, None, A.add)
+    for a in range(1, 4):
+        TS(R("QJ%d" % a), R("QA"), -2.0 * a, None, A.add)
+    for n in ("C8", "CAL"):
+        TT(R(n), R(n), R("OFF"), A.add)
+    TS(R("sA"), R("C16"), R("QA"), None, eq)
+    TS(R("sB"), R("C16"), R("QB8"), None, eq)
+    TS(R("sI"), R("C8"), R("QB"), None, eq)
+    for a in range(4):
+        TS(R("sJ%d" % a), R("CAL"), R("QJ%d" % a if a else "QA"), None, eq)
+    TC(R("XY0", 0, 8), R("prowI"))
+    TC(R("XY0", 8, 16), R("pcolI"))
+
+    def sums():
+        for h in range(16):
+            MM(R("pH", 0, 256), [(X(T.SEL[:, h, :], "SEL", h, h + 1), R("MW", 256 * h, 256 * h + 256))], h == 0, h == 15)
+        TS(R("CSi"), R("pH", 0, 256), 1.0 / BAD, None, A.mult)
+        TS(R("HCi"), R("CSi"), 4, None, SHR)
+        TS(R("LCi"), R("CSi"), 15, None, AND)
+        TC(X(T.HLC[:, 0, :], "HLC", 0, 256), R("HCi"))
+        TC(X(T.HLC[:, 1, :], "HLC", 256, 512), R("LCi"))
+
+    def spread_sums():
+        for k in range(2):
+            dma("y", X(T.CW[k::16, :], "CW", k, k + 1), X(T.HLC[:, k, :], "HLC", 256 * k, 256 * k + 256))
+
+    sums()
+    spread_sums()
+    MS(X(T.XM1[:, NJ:NI], "XM1"), 0)
+    mates(1, "yy")
+    MS(R("OHW"), 0.0)
+    MS(R("NPC"), -PC)
+    TS(R("CWT"), R("P15"), 0.0, 2048.0 / BAD, eq, A.mult)
+    TS(R("CW2"), R("P15"), 1.0, 128.0 / BAD, eq, A.mult)
+    TT(R("CWT"), R("CWT"), R("CW2"), A.add)
+    TS(X(T.SELC[:], "SELC"), X(T.SEL[:], "SEL"), R("CWT"), None, A.mult)
+    TS(R("IDb"), R("MI"), R("PF"), None, eq)
+    TS(R("IDf"), R("MI"), R("PF"), None, eq)
+
+    def late_constants():
+        TS(R("PKC"), R("SHI"), 1023.5, 0.5, A.mult, A.add)
+        TS(R("PK"), R("BB"), R("PKC"), None, A.mult)
+        TS(R("RST"), R("RST"), 0.0, 1e9, eq, A.mult)
+        TS(R("OHA"), R("OHA"), R("P15"), None, eq)
+        TS(R("OHB"), R("OHB"), R("P15"), None, eq)
+        TT(R("OHW", 0, 64), R("OHA"), R("OHB"), A.add)
+        TS(R("DMK"), R("DMK"), R("P15"), None, eq)
+        TS(R("KJ"), R("KJ"), R("P15"), None, A.add)
+        TT(R("G16"), R("PF"), R("P15"), A.subtract)
+        TS(R("HIO"), R("MI"), R("G16"), None, A.subtract)
+        TS(R("PH"), R("H16"), R("P15"), None, eq)
+        for c in range(16):
+            TS(X(T.EXPM[:, c, :], "EXPM", c, c + 1), R("BB"), R("PH", c, c + 1), None, A.mult)
+
+    def suppress(ns):
+        first = 24 - ns
+        TS(R("SP", 0, ns), R("HLf", 24 + first, 48), -1.0, 0.5, A.mult, A.add)
+        TS(R("SN", 0, ns), R("HLf", 24 + first, 48), 0.5, None, A.add)
+        for k in range(ns):
+            ACT(X(T.ST1[:, k, :], "ST1", k, k + 1), R("LIO"), F.Sign, bias=R("SP", k, k + 1))
+            ACT(X(T.ST2[:, k, :], "ST2", k, k + 1), R("LIO"), F.Sign, bias=R("SN", k, k + 1), scale=-1.0)
+        order = list(range(0, 10)) + list(range(first, 24)) + list(range(10, first))
+        for n, e in enumerate(order):
+            hoh = X(T.HOH[:, e, :], "HOH", e, e + 1)
+            TS(hoh, R("HIO"), R("HLf", e, e + 1), R("gn", e % 8, e % 8 + 1), eq, A.mult)
+            if e < first:
+                loh = X(T.LOH[:, e, :], "LOH", e, e + 1)
+                TS(loh, R("LIO"), R("HLf", 24 + e, 25 + e), 2.0, eq, A.mult)
+                MM(R("pH", 0, 256), [(hoh, loh)], n == 0, n == 23)
+            else:
+                k = e - first
+                MM(R("pH", 0, 256), [(hoh, X(T.ST1[:, k, :], "ST1", k, k + 1)), (hoh, X(T.ST2[:, k, :], "ST2", k, k + 1))], False, n == 23)
+
+    for t in range(ROUNDS):
+        xy, z = "XY%d" % t, "Z%d" % t
+        zoff = 0.0 if t == 0 else -128.0
+        LX, LY = R(xy, 0, 8), R(xy, 8, 16)
+        XM = R("XM%d" % (t % 2))
+        TS(R("R2"), IND(XM, LX), 2.0, 593.0, A.mult, A.add)
+        ACT(R("U"), IND(R("IOTA"), LX), F.Identity, bias=R("BIA"), scale=R("SCA"))
+        ACT(R("WN"), IND(R("IOTA"), LY), F.Identity, bias=R("BIB"), scale=R("SCB"))
+        TS(R("C2"), IND(XM, LY), 2.0, 17.0, A.mult, A.add)
+        if t:
+            for k in range(2):
+                hl = X(T.HLC[:, k, :], "HLC", 256 * k, 256 * k + 256)
+                TT(hl, hl, R("pH", 0, 256), A.subtract)
+            spread_sums()
+        MM(R("pM", 0, 128), [(R("sA"), R("R2"))], True, False)
+        MM(R("pM", 0, 128), [(R("sB"), R("C2"))], False, True)
+        MM(R("pN", 0, 128), [(R("sI"), R("C2"))])
+        JP = [R(("pJP", "pA")[a // 2], 128 * (a % 2), 128 * (a % 2) + 128) for a in range(4)]
+        for a in range(4):
+            MM(JP[a], [(R("sJ%d" % a), R("R2"))])
+        for k in range(16):
+            if k == 12:
+                ACT(R("IPs"), R("pN", 0, 128), F.Copy)
+            ACT(X(T.Zr[:, k:2048:16], "Zr", k, k + 1), R(z), F.Copy, bias=zoff)
+        ACT(X(T.MW[:, W:W + 128], "MW", W, W + 128), R(z), F.Copy, bias=2 * zoff, scale=2.0)
+        TT(R("OT"), R("U"), R("WN"), A.add)
+        TC(R("XYf"), R(xy))
+        TS(R("UWO", 0, 8), R("XYf", 0, 8), 2.0, 17.0, A.mult, A.add)
+        TS(R("UWO", 8, 16), R("XYf", 8, 16), 2.0, 593.0, A.mult, A.add)
+        TS(R("t8"), R("XYf", 0, 8), 2048.0, PC, A.mult, A.add)
+        TT(R("PP"), R("t8"), R("XYf", 8, 16), A.add)
+        TT(R("F12q"), R("pM", 0, 128), R("OT"), A.mult)
+        TS(R("F12i"), R("F12q"), 5, W - 1, SHR, AND)
+        TC(R("F12u"), R("F12i"))
+        for a in range(4):
+            TT(R("F3q", 128 * a, 128 * a + 128), JP[a], R("IPs"), A.mult)
+        TS(R("F3i"), R("F3q"), 5, W - 1, SHR, AND)
+        TC(R("F3u"), R("F3i"))
+
+        def look_v(e, lo, f, flo, n):
+            TT(R(e, lo, lo + 16 * n), IND(R("MW", 0, W), R(f, flo, flo + n)), X(T.Zr[:, lo % 2048:lo % 2048 + 16 * n], "Zr"), A.is_lt)
+
+        def look_c(e, lo, f, flo, n):
+            ACT(R(e, lo, lo + 16 * n), IND(R("CW"), R(f, flo, flo + n)), F.Relu)
+
+        def chunk(out, e, off, sel, start, stop, c0=0, c1=16):
+            for c in range(c0, c1):
+                MM(out, [(X(T[sel][:, c, :], sel, c, c + 1), R(e, off + 128 * c, off + 128 * c + 128))], start and c == 0, stop and c == 15)
+        PKR = X(T.pK[:], "pK")
+        look_c("E12c", 0, "F12u", 0, 128)
+        look_v("E12v", 0, "F12u", 0, 128)
+        for b, nm in enumerate(("pA", "pB")):
+            MM(R(nm, 0, 256), [(R("IDb"), R("RHO", 256 * b, 256 * b + 256))], True, False)
+        for k in range(8):
+            MM(R("pM2", 16 * k, 16 * k + 16), [(R("sA"), R("R2", k, 128, 8)), (R("sB"), R("C2", k, 128, 8))])
+        chunk(PKR, "E12v", 0, "SEL", True, False)
+        banks = [R(("pA", "pB")[a // 2], 128 * (a % 2), 128 * (a % 2) + 128) for a in range(4)]
+        for a in range(4):
+            lo = 2048 * a
+            parts = ((0, 128),) if a < 3 else ((0, 64), (64, 32), (96, 32))
+            for (p, n) in parts:
+                look_v("E3v", lo + 16 * p, "F3u", 128 * a + p, n)
+                look_c("E3c", lo + 16 * p, "F3u", 128 * a + p, n)
+            if a == 0:
+                chunk(PKR, "E12c", 0, "SELC", False, True)
+                if t == 0:
+                    late_constants()
+            if a == 1:
+                ACT(R("MT2s"), R("pM2", 0, 128), F.Copy)
+                for l in range(2):
+                    ACT(X(T.K2Y[:, :, 8 * l:8 * l + 8], "K2Y", l, l + 1), X(T.pK[:, :, 8:16], "pK"), F.Copy)
+                for x in range(4):
+                    ACT(X(T.K1s[:, x, :, :], "K1s", x, x + 1), X(T.pK[:, :, 2 * x:2 * x + 2], "pK"), F.Copy)
+                for x in range(2):
+                    MM(banks[x], [(R("IDf"), X(T.K2Y[:], "K2Y"))], False, False)
+            if a == 2:
+                for x in range(2):
+                    MM(banks[2 + x], [(R("IDf"), X(T.K2Y[:], "K2Y"))], False, False)
+                MM(R("pN", 0, 128), [(R("IDf"), R("NPC"))], True, False)
+            for (p, n) in parts:
+                chunk(banks[a], "E3c", lo, "SELC", False, False, p // 8, (p + n) // 8)
+                chunk(banks[a], "E3v", lo, "SEL", False, a % 2 == 1, p // 8, (p + n) // 8)
+        for b, nm in enumerate(("pA", "pB")):
+            SCAN(R("M1", 256 * b, 256 * b + 256), R("RST"), R(nm, 0, 256), 0.0, A.max, A.min)
+            m = R("M2", 32 * b, 32 * b + 32)
+            TT(m, R("M1", 256 * b + 7, 256 * b + 256, 8), X(T.K1s[:, 2 * b:2 * b + 2, :, :], "K1s", 2 * b, 2 * b + 2), A.add)
+            TT(R("MA", 16 * b, 16 * b + 16), R("M2", 32 * b, 32 * b + 16), R("M2", 32 * b + 16, 32 * b + 32), A.min)
+        TT(R("MA", 0, 16), R("MA", 0, 16), R("MA", 16, 32), A.min)
+        TT(R("MB"), R("MA", 0, 16, 2), R("MA", 1, 16, 2), A.min)
+        mk = R("mki", 8 * t, 8 * t + 8)
+        TS(mk, R("MB"), CLIP, None, A.min)
+        TS(R("rhoI"), mk, 127, None, AND)
+        TC(R("rhoU"), R("rhoI"))
+        TT(R("NM"), IND(R("OHW"), R("rhoU")), R("MT2s"), A.mult)
+        MM(R("pN", 0, 128), [(R("PK"), R("NM"))], False, True)
+        if t == ROUNDS - 1:
+            TS(R("cI"), R("mki"), 7, None, SHR)
+            TS(R("G"), R("mki"), CLIP, None, A.is_lt)
+            TS(R("cf"), R("cI"), 1.0, None, A.add)
+        TT(R("NMm"), R("pN", 0, 128), R("DMK"), A.mult)
+        TT(R("T64"), R("NMm", 0, 64), R("NMm", 64, 128), A.add)
+        TT(R("T32"), R("T64", 0, 32), R("T64", 32, 64), A.add)
+        TT(R("T16"), R("T32", 0, 16), R("T32", 16, 32), A.add)
+        TT(R("P8"), R("T16", 0, 16, 2), R("T16", 1, 16, 2), A.add)
+        TS(R("k0"), R("P8"), 0.0, None, A.is_lt)
+        TT(R("k1"), R("k0"), R("PP"), A.mult)
+        TT(R("Pi"), R("P8"), R("k1"), A.add)
+        TS(R("XYi", 0, 8), R("Pi"), 11, None, SHR)
+        TS(R("XYi", 8, 16), R("Pi"), 2047, None, AND)
+
+        def pass_names():
+            TC(R("XYs"), R("XYi"))
+            remote(t, "n", "XY%d" % (t + 1), R("XYs"))
+
+        def pass_needs():
+            TT(R("kj"), R("k0"), R("KJ"), A.mult)
+            TS(R("FC3"), R("QC", 16, 24), 5, W - 1, SHR, AND)
+            TT(R("far2"), R("FC3"), R("kj"), A.max)
+            TC(R("farU"), R("far2"))
+            TS(R("Zs"), IND(R("MW"), R("farU")), 0.5, 127.75, A.mult, A.add)
+            remote(t, "z", "Z%d" % (t + 1), R("Zs"))
+        if t < ROUNDS - 1:
+            pass_names()
+        TS(R("UWN", 0, 8), R("XYi", 0, 8), 2.0, 17.0, A.mult, A.add)
+        TS(R("UWN", 8, 16), R("XYi", 8, 16), 2.0, 593.0, A.mult, A.add)
+        TT(R("QC", 16, 24), R("UWN", 0, 8), R("UWN", 8, 16), A.mult)
+        if t < ROUNDS - 1:
+            pass_needs()
+        TT(R("QC", 0, 8), R("UWO", 0, 8), R("UWN", 8, 16), A.mult)
+        TT(R("QC", 8, 16), R("UWN", 0, 8), R("UWO", 8, 16), A.mult)
+        TS(R("gn"), R("k0"), 0.0, 64.0, eq, A.mult)
+        TS(R("HLi", 0, 24), R("QC"), 13, 15, SHR, AND)
+        TS(R("HLi", 24, 48), R("QC"), 5, 255, SHR, AND)
+        TC(R("HLf"), R("HLi"))
+        suppress(NS[t])
+        if t == ROUNDS - 1:
+            pass_names()
+            pass_needs()
+            TT(R("SG"), X(T.HLC[:, 0, :], "HLC", 0, 256), R("pH", 0, 256), A.subtract)
+            TS(R("SG"), R("SG"), 0.0, 2.0, A.is_gt, A.mult)
+            TS(R("SG"), R("SG"), -1.0, None, A.add)
+
+    e = ROUNDS
+    banks = ("pA", "pB", "pJP", "pM")
+    for k in range(8):
+        nm = banks[k % 4]
+        for x in range(2):
+            MM(R(nm, 256 * x, 256 * x + 256), [(X(T.EXPM[:, 2 * k + x, :], "EXPM"), R("SG"))])
+        TT(R("YF", 512 * k, 512 * k + 512), R("MW", 512 * k, 512 * k + 512), R(nm, 0, 512), A.mult)
+        if k == 0:
+            dma("s", (T.yf[:, 0:512 - ROT], EXT), R("YF", ROT, 512))
+            dma("y", (T.yf[:, W - ROT:W], EXT), R("YF", 0, ROT))
+            TT(R("cst"), R("cf"), R("G"), A.mult)
+            TS(R("cst"), R("cst"), -1.0, None, A.add)
+            for x in range(ROUNDS):
+                dma(("s", "y")[x % 2], (T.yc[:, 128 * x:128 * x + 128], EXT), R("cst", 8 * x, 8 * x + 8))
+        elif k % 2 == 0:
+            dma(("s", "y")[k // 2 % 2], (T.yf[:, 512 * (k - 1) - ROT:512 * (k + 1) - ROT], EXT), R("YF", 512 * (k - 1), 512 * (k + 1)))
+        if k == 5:
+            TC(R("YP"), R("XY%d" % e))
+            dma("y", (T.yp[:], EXT), R("YP"))
+    dma("s", (T.yf[:, 3584 - ROT:W - ROT], EXT), R("YF", 3584, W))
+    TS(R("YZ"), R("Z%d" % e), -128.0, None, A.add)
+    dma("y", (T.yz[:], EXT), R("YZ"))
+    for s, n in sorted(count.items()):
+        if known["g"].get(s, 0) < n:
+            g.wait_ge(T.sem[s], n)

@@ -2,12 +2,18 @@ from concourse.mybir import AluOpType as A, ActivationFunctionType as F
 
 ROT = 315
 W, NI, NJ = 4096, 2048, 1536
-BAD = float(2 ** 20)
-CLIP = float(2 ** 20 - 64)
-PC = 17704.5
+JO = 288
+EPS, SIG = 1.0 / 64, 1.0 / 256
+MAGIC = 1.5 * 2 ** 23
+CLIP = float(128 * 6144 + 64)
 ROUNDS = 4
-NS = [4, 4, 4, 6]
-NSM = 6
+NV = 9
+NS = 16 - NV
+NPER = (40 * NV + 15) // 16
+NSE = [5, 5, 5, 6]
+CHUNKS = {"VA": ("pA", 0, 2), "VB": ("pB", 2, 4), "VC": ("pA", 4, 5), "SA": ("pC", 0, 4), "SB": ("pD", 4, 6), "SC": ("pC", 6, 7)}
+ORDER = ("gs0 gs1 gs2 gs3 gs4 gs5 gs6 ms0 gv0 mv0 ms1 gv1 mv1 ms2 gv2 rVA mv2 dVA ms3 gv3 kVA rSA eVA dSA mv3 ms4 gv4 kSA rVB mv4 dVB ms5 "
+         "rVC rSB dVC dSB kVB eVB ms6 kVC kSB eVC rSC dSC kSC").split()
 
 SB = {}
 POOL = {}
@@ -26,20 +32,20 @@ def _small(names, width, dtype="float32"):
         USED[p] += width
 
 
-_small("rhoI Pi far2 FC3", 8, "int32")
-_small("KJ k0 k1 gn PP t8 kj P8 MB", 8)
+_small("hiI loI QC", 24, "int32")
+_small("rhoI q3 FC far", 8, "int32")
 _small("mki cI", 8 * ROUNDS, "int32")
-_small("G cf cst", 8 * ROUNDS)
-_small("XYi", 16, "int32")
-_small("XYf UWO UWN T16 H16 PH YP", 16)
-_small("QC", 24, "int32")
-_small("HLi", 48, "int32")
-_small("HLf", 48)
-_small("SP SN", NSM)
-_small("T32 MA", 32)
-_small("M2", 64)
+_small("repI", 8 * NV + 48, "int32")
 _small("PI P15i", 1, "int32")
-_small("PF P15 G16 SLO SHI SCA BIA SCB BIB CWT CW2 PKC PM PMA QA QB QB8 QJ1 QJ2 QJ3", 1)
+_small("KJ kj mkf val ST1", 8)
+_small("G cf cst", 8 * ROUNDS)
+_small("UW YP NEW", 16)
+_small("Asb nlo", 24)
+_small("sO cK", 56)
+_small("DM", 8 * NS)
+_small("FU", 2 * NPER)
+_small("FUa FUb", NPER)
+_small("P15 SLO SHI S2L S2H R2B C2B BIA BIB CKR CKC T1 T2 QA QB QB8 QJ1 QJ2 QJ3 P7", 1)
 _sb("poolF", [USED["poolF"]])
 _sb("poolI", [USED["poolI"]], "int32")
 _sb("prowI pcolI", [8], "int32")
@@ -48,42 +54,51 @@ for _t in range(ROUNDS + 1):
     _sb("XY%d" % _t, [16], "uint16")
     _sb("Z%d" % _t, [128], "bfloat16")
 _sb("XYs", [16], "uint16")
-_sb("Zs", [128], "bfloat16")
+_sb("repU", [8 * NV + 48], "uint16")
+_sb("Zs Zin YZ IDb C128", [128], "bfloat16")
+_sb("BBb", [8, 16], "bfloat16")
 _sb("XM0 XM1", [NI], "int32")
 _sb("MW", [W + 128], "bfloat16")
-_sb("CW YF", [W], "bfloat16")
+_sb("WF", [W + 128])
+_sb("YF", [W], "bfloat16")
 _sb("IOTA", [NI])
-_sb("ONE BT BB OFF C16 C8 CAL MI NPC", [128])
-_sb("C16b IDb HIO", [128], "bfloat16")
-_sb("sJ0 sJ1 sJ2 sJ3 sA sB sI PK IDf DMK", [128])
-_sb("SEL SELC EXPM", [16, 128], "bfloat16")
-_sb("RHO", [512], "bfloat16")
-_sb("RST", [256])
-_sb("M1", [512])
-_sb("OHA OHB T64", [64])
-_sb("OHW", [80])
-_sb("LIO SG", [256], "bfloat16")
-_sb("R2 C2 U WN OT IPs MT2s NM NMm", [128])
-_sb("K2Y", [8, 16])
-_sb("K1s", [4, 8, 2])
-_sb("F12q F12i", [128], "int32")
-_sb("F12u", [128], "uint16")
-_sb("F3q F3i", [512], "int32")
-_sb("F3u", [512], "uint16")
-_sb("Zr E12v E12c", [2048], "bfloat16")
-_sb("E3v E3c", [8192], "bfloat16")
-_sb("HOH", [24, 128], "bfloat16")
+_sb("ONE BT BB OFF C16 C8 CAL IDf NIDf OHW U WN OT IPs MT NZf CT", [128])
+_sb("sJ0 sJ1 sJ2 sJ3 sA sB sI PK0 PK1 IDh I15 I16 SELI CD R2 C2 NM", [128], "float16")
+_sb("sN", [56], "float16")
+_sb("mo", [16], "float16")
+_sb("RZ", [8, NS], "float16")
+_sb("SEL0 SEL1", [512], "float16")
+_sb("SELJ", [128], "float16")
+_sb("MKB", [256], "float16")
+_sb("RB DB", [640], "float16")
+_sb("KV KS", [5, 8, 16], "float16")
+_sb("RHO ZEb", [512], "bfloat16")
+_sb("SELa SELb SELc SELd", [8, 2, 32], "bfloat16")
+_sb("SELe", [128], "bfloat16")
+_sb("ONEb EXPM", [16, 128], "bfloat16")
+_sb("NEG RST M1", [512])
+_sb("RS16 NSC MKI", [256])
+_sb("OHA OHB", [64])
+_sb("LIO NIO SG FL B16", [256], "bfloat16")
+_sb("BP W0", [256])
+_sb("HIO HOH", [768], "bfloat16")
 _sb("LOH", [24, 256], "bfloat16")
-_sb("ST1 ST2", [NSM, 256], "bfloat16")
-_sb("CSi HCi LCi", [256], "int32")
-_sb("HLC", [2, 256], "bfloat16")
-_sb("YZ", [128], "bfloat16")
-for _n in ("pJP", "pM", "pM2", "pA", "pB", "pN", "pH"):
-    SB[_n] = ("psum", [128, 512], "float32")
-SB["pK"] = ("psum", [128, 8, 16], "float32")
-PSUMS = ("pJP", "pM", "pM2", "pA", "pB", "pN", "pH", "pK")
+_sb("AB", [6, 256], "bfloat16")
+_sb("Fq", [8, 16, 5], "int32")
+_sb("FiS", [8, NS, 5], "int32")
+_sb("FiV", [40 * NV], "int32")
+_sb("perU", [NPER + NPER % 2], "uint16")
+_sb("FS", [8, NS, 6], "uint16")
+_sb("FV", [16 * NPER], "uint16")
+_sb("Zr", [128 * NV])
+_sb("EV", [5, 128 * NV])
+_sb("ES", [NS, 640])
+for _n, _s in (("pA", [2, 2, 8, 16]), ("pB", [2, 2, 8, 16]), ("pC", [8, 2, 8, 4]), ("pD", [8, 2, 8, 4]), ("pE", [512]),
+               ("pH", [512]), ("pJ", [512]), ("pM", [512])):
+    SB[_n] = ("psum", [128] + _s, "float32")
+PSUMS = ("pA", "pB", "pC", "pD", "pE", "pH", "pJ", "pM")
 SCRATCH = SB
-NDMA = 60
+NDMA = 70
 SEMAPHORES = ["qv", "qt", "qs", "qg"] + ["d%d" % k for k in range(NDMA)] + \
     [p + "%d" % k for p in ("rn", "rz", "ln", "lz") for k in range(ROUNDS)]
 
@@ -110,7 +125,7 @@ def rank_program(g, core, T, topo):
                             continue
                     elif phi <= lo or plo >= hi or not (pw or w):
                         continue
-                    if same and (q == "t" or not pw):
+                    if same and q == "t":
                         continue
                     deps.append((sem, val, kn))
         for sem, val, kn in sorted(deps, key=lambda d: -d[1]):
@@ -126,9 +141,11 @@ def rank_program(g, core, T, topo):
             for (n, lo, hi) in regs:
                 lst = past.setdefault(n, [])
                 if n in PSUMS:
-                    lst[:] = [p for p in lst if not (p[3] == q and (w or not p[2]) and lo <= p[0] and p[1] <= hi)]
+                    lst[:] = [p for p in lst if p[3] != q or (p[2] and not w)]
                 elif w:
                     lst[:] = [p for p in lst if not (lo <= p[0] and p[1] <= hi)]
+                else:
+                    lst[:] = [p for p in lst if not (p[3] == q and not p[2] and lo <= p[0] and p[1] <= hi)]
                 lst.append((lo, hi, w, q, sem, val, kn))
 
     def regs_of(*refs):
@@ -146,10 +163,10 @@ def rank_program(g, core, T, topo):
         inst.then_inc(T.sem[sem], 1)
         note(q, sem, count[sem], reads, writes, dict(known[q]))
 
-    def dma(q, out, in_):
+    def dma(q, out, in_, after=()):
         sem = "d%d" % ndma[0]
         ndma[0] += 1
-        need_waits(q, in_[1], out[1], True)
+        need_waits(q, in_[1] + list(after), out[1], True)
         queues[q].dma_start(out[0], in_[0]).then_inc(T.sem[sem], 16)
         count[sem] = 16
         note(sem, sem, 16, in_[1], out[1], dict(known[q]))
@@ -165,6 +182,9 @@ def rank_program(g, core, T, topo):
 
     def X(ap, n, lo=0, hi=1 << 20):
         return (ap, [(n, lo, hi)])
+
+    def ALL(n):
+        return X(T[n][:], n)
 
     def IND(win, offs):
         return (win[0].indirect(offs[0]), win[1] + offs[1])
@@ -193,13 +213,16 @@ def rank_program(g, core, T, topo):
     def ACT(out, a, func, bias=0.0, scale=1.0):
         emit("s", lambda: g.scalar.activation(out[0], a[0], func, bias=val(bias), scale=val(scale)), regs_of(a, bias, scale), out[1])
 
-    def MM(out, pairs, start=True, stop=True):
+    def MM(items):
         def go():
             inst = None
-            for k, (l, r) in enumerate(pairs):
-                inst = g.tensor.matmul(out[0], l[0], r[0], start and k == 0, stop and k == len(pairs) - 1)
+            for (o, l, r, st, sp) in items:
+                inst = g.tensor.matmul(o[0], l[0], r[0], st, sp)
             return inst
-        emit("t", go, regs_of(*[r for p in pairs for r in p]), out[1])
+        emit("t", go, regs_of(*[r for it in items for r in it[1:3]]), regs_of(*[it[0] for it in items]))
+
+    def ACC(out, pairs, start=True, stop=True):
+        MM([(out, l, r, start and k == 0, stop and k == len(pairs) - 1) for k, (l, r) in enumerate(pairs)])
 
     def IOTA(out, pattern, base, cm, f=True):
         if f:
@@ -223,296 +246,324 @@ def rank_program(g, core, T, topo):
         count[rs] = len(topo.engines(frm, core))
         note(rs, rs, count[rs], [], [(dst, 0, SB[dst][1][1])], {})
 
-    eq, ge, SHR, AND = A.is_equal, A.is_ge, A.arith_shift_right, A.bitwise_and
+    eq, ge, SHR, AND, mul, add = A.is_equal, A.is_ge, A.arith_shift_right, A.bitwise_and, A.mult, A.add
     EXT = []
 
-    def mates(h, qs):
+    def blank(h):
+        n = "XM%d" % h
+        MS(X(T[n][:, 0:JO], n, 0, 8), 0)
+        MS(X(T[n][:, JO + NJ:NI], n, 0, 8), 0)
+
+    def mates(h, qs, after=()):
         n = "XM%d" % h
         for k in range(8):
-            dma(qs[k % 2], X(T[n][16 * k:16 * k + 8, 0:NI], n, k, k + 1), (T.rmate[16 * k + 8 * h:16 * k + 8 * h + 8, :], EXT))
+            dma(qs[k % 2], X(T[n][16 * k + 8:16 * k + 16, JO:JO + NJ], n, 8 + k, 9 + k), (T.cmate[16 * k + 8 * h:16 * k + 8 * h + 8, :], EXT), after)
         for k in range(8):
-            dma(qs[k % 2], X(T[n][16 * k + 8:16 * k + 16, 0:NJ], n, 8 + k, 9 + k), (T.cmate[16 * k + 8 * h:16 * k + 8 * h + 8, :], EXT))
+            dma(qs[k % 2], X(T[n][16 * k:16 * k + 8, 0:NI], n, k, k + 1), (T.rmate[16 * k + 8 * h:16 * k + 8 * h + 8, :], EXT), after)
+    blank(0)
     dma("y", R("prowI"), (T.prow[:], EXT))
     dma("s", R("pcolI"), (T.pcol[:], EXT))
+    mates(0, "ys")
+    dma("s", R("Zin"), (T.need[:], EXT))
     dma("y", R("MW", ROT, W), (T.fig[:, 0:W - ROT], EXT))
     dma("s", R("MW", 0, ROT), (T.fig[:, W - ROT:W], EXT))
-    MS(X(T.XM0[:, NJ:NI], "XM0"), 0)
-    mates(0, "ys")
-    dma("s", R("Z0"), (T.need[:], EXT))
 
     MS(R("ONE"), 1.0)
-    MS(R("CW"), 0.0)
+    MS(R("FU"), 0.0)
     IOTA(R("PI"), [[1, 1]], 0, 1, False)
-    AFF(R("BT"), R("ONE"), [[-16, 8], [0, 16]], ge, 0.0, 0, 1)
-    AFF(R("BB"), R("BT"), [[16, 8], [0, 16]], ge, 0.0, 15, -1)
     IOTA(R("C16"), [[0, 8], [1, 16]], 0, 0)
     IOTA(R("C8"), [[0, 16], [1, 8]], 0, 0)
     IOTA(R("CAL"), [[0, 8], [1, 2], [0, 8]], 0, 0)
+    AFF(R("BT"), R("ONE"), [[-16, 8], [0, 16]], ge, 0.0, 0, 1)
+    AFF(R("BB"), R("BT"), [[16, 8], [0, 16]], ge, 0.0, 15, -1)
+    AFF(R("IDf"), R("ONE"), [[-1, 128]], eq, 0.0, 0, 1)
+    IOTA(R("repI", 0, 8 * NV), [[1, NV], [16, 8]], 0, 0, False)
+    IOTA(R("FU", 0, 5 * NV), [[1, 5], [5, NV]], 0, 0)
     IOTA(R("IOTA"), [[1, NI]], 0, 0)
-    IOTA(R("MI"), [[1, 128]], 0, 0)
-    IOTA(R("LIO"), [[1, 256]], 0, 0)
-    IOTA(R("RHO"), [[16, 4], [0, 8], [1, 16]], 0, 0)
+    IOTA(R("repI", 8 * NV, 8 * NV + 48), [[1, 24], [0, 2]], 0, 0, False)
+    IOTA(R("DM"), [[0, 8], [1, NS]], NV, 0)
+    IOTA(R("RHO"), [[0, 8], [1, 16], [16, 4]], 0, 0)
+    IOTA(R("MKI"), [[0, 16], [1, 16]], 0, 0)
     IOTA(R("OHA"), [[1, 8], [0, 8]], 0, 0)
     IOTA(R("OHB"), [[0, 8], [1, 8]], 8, 0)
-    IOTA(R("DMK"), [[1, 8], [0, 8], [8, 2]], 0, 0)
     IOTA(R("KJ"), [[16, 8]], W, 0)
-    IOTA(R("H16"), [[1, 16]], 0, 0)
-    IOTA(R("RST"), [[0, 32], [1, 8]], 0, 0)
 
+    blank(1)
+    MS(R("NEG"), -1e9)
+    MS(R("ZEb"), 0.0)
+    MS(R("C128"), 128.0)
+    MS(R("OHW", 0, 64), 0.0)
+    MS(R("sO"), 0.0)
+    MS(R("cK"), 0.0)
+    for lo, hi in ((8, 32), (40, 48)):
+        MS(R("cK", lo, hi), 4113.0 / 128)
     TS(R("P15i"), R("PI"), 15, None, AND)
-    TC(R("PF"), R("PI"))
     TC(R("P15"), R("P15i"))
-    TS(R("OFF"), R("BB"), -999.0, 999.0, A.mult, A.add)
-    TT(R("C16"), R("C16"), R("OFF"), A.add)
-    TC(R("C16b"), R("C16"))
-    for c in range(16):
-        TS(X(T.SEL[:, c, :], "SEL", c, c + 1), R("C16b"), float(c), BAD, eq, A.mult)
     TS(R("SLO"), R("P15"), 8.0, None, A.is_lt)
     TS(R("SHI"), R("P15"), 8.0, None, ge)
-    TS(R("SCA"), R("SLO"), 2.0, None, A.mult)
-    TS(R("BIA"), R("SLO"), 17.0, None, A.mult)
-    TS(R("SCB"), R("SHI"), 2.0, None, A.mult)
-    TS(R("BIB"), R("SHI"), 593.0, None, A.mult)
-    TS(R("PM"), R("SHI"), -50.0, None, A.mult)
-    TT(R("QA"), R("P15"), R("PM"), A.add)
-    TS(R("PMA"), R("SLO"), -50.0, -8.0, A.mult, A.add)
-    TT(R("QB"), R("P15"), R("PMA"), A.add)
-    TS(R("QB8"), R("QB"), 8.0, None, A.add)
+    TS(R("S2L"), R("SLO"), 2.0, None, mul)
+    TS(R("S2H"), R("SHI"), 2.0, None, mul)
+    TS(R("BIA"), R("SLO"), 17.0, None, mul)
+    TS(R("BIB"), R("SHI"), 17.0, None, mul)
+    TS(R("R2B"), R("SLO"), 2.0 * (JO - 2048) - 1, 1.0, mul, add)
+    TS(R("C2B"), R("SHI"), -4097.0, 1.0, mul, add)
+    for n, r in (("CKR", 8.0), ("CKC", 0.0)):
+        TS(R("T1"), R("P15"), r, 512.0, eq, mul)
+        TS(R("T2"), R("P15"), r + 1, 2.125, eq, mul)
+        TT(R(n), R("T1"), R("T2"), add)
+    TS(R("QA"), R("SHI"), -50.0, R("P15"), mul, add)
+    TS(R("QB8"), R("SLO"), -50.0, R("P15"), mul, add)
+    TS(R("QB"), R("QB8"), -8.0, None, add)
     for a in range(1, 4):
-        TS(R("QJ%d" % a), R("QA"), -2.0 * a, None, A.add)
-    for n in ("C8", "CAL"):
-        TT(R(n), R(n), R("OFF"), A.add)
-    TS(R("sA"), R("C16"), R("QA"), None, eq)
+        TS(R("QJ%d" % a), R("QA"), -2.0 * a, None, add)
+    TS(R("OFF"), R("BB"), -999.0, 999.0, mul, add)
+    for n in ("C16", "C8", "CAL"):
+        TT(R(n), R(n), R("OFF"), add)
+    TS(R("sA"), R("C16"), R("QA"), R("CKR"), eq, add)
     TS(R("sB"), R("C16"), R("QB8"), None, eq)
-    TS(R("sI"), R("C8"), R("QB"), None, eq)
+    TS(R("sI"), R("C8"), R("QB"), R("CKC"), eq, add)
     for a in range(4):
-        TS(R("sJ%d" % a), R("CAL"), R("QJ%d" % a if a else "QA"), None, eq)
+        TS(R("sJ%d" % a), R("CAL"), R("QJ%d" % a if a else "QA"), R("CKR"), eq, add)
     TC(R("XY0", 0, 8), R("prowI"))
-    TC(R("XY0", 8, 16), R("pcolI"))
-
-    def sums():
-        for h in range(16):
-            MM(R("pH", 0, 256), [(X(T.SEL[:, h, :], "SEL", h, h + 1), R("MW", 256 * h, 256 * h + 256))], h == 0, h == 15)
-        TS(R("CSi"), R("pH", 0, 256), 1.0 / BAD, None, A.mult)
-        TS(R("HCi"), R("CSi"), 4, None, SHR)
-        TS(R("LCi"), R("CSi"), 15, None, AND)
-        TC(X(T.HLC[:, 0, :], "HLC", 0, 256), R("HCi"))
-        TC(X(T.HLC[:, 1, :], "HLC", 256, 512), R("LCi"))
-
-    def spread_sums():
-        for k in range(2):
-            dma("y", X(T.CW[k::16, :], "CW", k, k + 1), X(T.HLC[:, k, :], "HLC", 256 * k, 256 * k + 256))
-
-    sums()
-    spread_sums()
-    MS(X(T.XM1[:, NJ:NI], "XM1"), 0)
-    mates(1, "yy")
-    MS(R("OHW"), 0.0)
-    MS(R("NPC"), -PC)
-    TS(R("CWT"), R("P15"), 0.0, 2048.0 / BAD, eq, A.mult)
-    TS(R("CW2"), R("P15"), 1.0, 128.0 / BAD, eq, A.mult)
-    TT(R("CWT"), R("CWT"), R("CW2"), A.add)
-    TS(X(T.SELC[:], "SELC"), X(T.SEL[:], "SEL"), R("CWT"), None, A.mult)
-    TS(R("IDb"), R("MI"), R("PF"), None, eq)
-    TS(R("IDf"), R("MI"), R("PF"), None, eq)
+    TS(R("XY0", 8, 16), R("pcolI"), float(JO), None, add)
+    ACT(R("Z0"), R("Zin"), F.Copy, bias=-128.0, scale=-1.0)
+    TC(R("repU", 0, 8 * NV), R("repI", 0, 8 * NV))
+    TS(R("P7"), R("SHI"), -8.0, R("P15"), mul, add)
+    TS(R("P7"), R("P7"), 5.0 * NV, None, mul)
+    TS(R("FUa"), R("FU", 0, 2 * NPER, 2), R("SLO"), R("P7"), mul, add)
+    TS(R("FUb"), R("FU", 1, 2 * NPER, 2), R("SHI"), None, mul)
+    TT(R("FUa"), R("FUa"), R("FUb"), add)
+    TC(R("perU", 0, NPER), R("FUa"))
+    G8 = R("BB", 0, 128, 16)
+    TC(R("ST1"), G8)
+    for n, c in (("IDb", 1.0), ("IDh", 1.0), ("I15", 2.0 ** 15), ("I16", 1.0 / 16), ("SELI", 2048.0), ("NIDf", -1.0)):
+        TS(R(n), R("IDf"), c, None, mul)
+    TC(ALL("BBb"), R("BB"))
+    for c in range(8):
+        TS(R("CD", c, 128, 8), R("BB", 16 * c, 16 * c + 16), -1.0 / 16, None, mul)
+    for n in ("KV", "KS"):
+        TS(ALL(n), R("IOTA", 0, 640), 0.0, None, mul)
+    TS(R("PK0"), R("BB"), R("SHI"), None, mul)
+    TS(R("PK1"), R("BB"), R("SLO"), None, mul)
+    TS(R("T1"), R("P15"), 0.0, None, eq)
+    TS(R("T2"), R("P15"), 8.0, None, eq)
+    TS(R("sO", 0, 8), G8, R("T1"), None, mul)
+    TS(R("sO", 32, 40), G8, R("T2"), None, mul)
+    for k, s in enumerate((0.0, "S2H", "S2H", "S2L", 0.0, "S2L", "SHI")):
+        TS(R("sN", 8 * k, 8 * k + 8), G8, R(s) if s else s, None, mul)
 
     def late_constants():
-        TS(R("PKC"), R("SHI"), 1023.5, 0.5, A.mult, A.add)
-        TS(R("PK"), R("BB"), R("PKC"), None, A.mult)
-        TS(R("RST"), R("RST"), 0.0, 1e9, eq, A.mult)
+        AFF(R("RST"), R("NEG"), [[0, 8], [1, 64]], A.not_equal, 1e9, 0, 0)
+        AFF(R("RS16"), R("NEG", 0, 256), [[0, 16], [1, 16]], A.not_equal, 1e9, 0, 0)
+        for n1, n2, sc, se in (("SELa", "SELb", 16, 1), ("SELc", "SELd", 1, 8)):
+            for h in range(2):
+                AFF(X(T[n1][:, :, h, :], n1, h, h + 1), R("ZEb", 0, 256), [[-sc, 8], [0, 8], [-2 * se, 4]], A.not_equal, 2048.0, -h * se, 1)
+                AFF(X(T[n2][:, :, h, :], n2, h, h + 1), X(T[n1][:, :, h, :], n1, h, h + 1), [[-sc, 8], [-se, 8], [0, 4]], A.not_equal, 2048.0, -8 * se, 1)
+        AFF(R("SELe"), R("ZEb", 0, 128), [[-1, 8], [-8, 16]], A.not_equal, 2048.0, 0, 1)
+        IOTA(ALL("HIO"), [[0, 12], [-16, 2], [1, 32]], 0, 0)
+        IOTA(R("LIO"), [[1, 256]], 0, 0)
+        IOTA(R("NIO"), [[-1, 256]], 0, 0)
+        TC(R("repU", 8 * NV, 8 * NV + 48), R("repI", 8 * NV, 8 * NV + 48))
+        TS(R("DM"), R("DM"), R("P15"), None, eq)
+        TS(ALL("MKB"), R("MKI"), R("P15"), 4096.0, A.not_equal, mul)
         TS(R("OHA"), R("OHA"), R("P15"), None, eq)
         TS(R("OHB"), R("OHB"), R("P15"), None, eq)
-        TT(R("OHW", 0, 64), R("OHA"), R("OHB"), A.add)
-        TS(R("DMK"), R("DMK"), R("P15"), None, eq)
-        TS(R("KJ"), R("KJ"), R("P15"), None, A.add)
-        TT(R("G16"), R("PF"), R("P15"), A.subtract)
-        TS(R("HIO"), R("MI"), R("G16"), None, A.subtract)
-        TS(R("PH"), R("H16"), R("P15"), None, eq)
-        for c in range(16):
-            TS(X(T.EXPM[:, c, :], "EXPM", c, c + 1), R("BB"), R("PH", c, c + 1), None, A.mult)
+        TT(R("OHW", 64, 128), R("OHA"), R("OHB"), add)
+        TS(R("KJ"), R("KJ"), R("P15"), None, add)
+    late_constants()
+    figs = R("MW", 0, W)[1]
+    dma("y", R("B16"), X(T.MW[0::16, 0:W], "MW", 0, W))
+    dma("g", R("WF", ROT, W), (T.fig[:, 0:W - ROT], EXT), figs)
+    dma("g", R("WF", 0, ROT), (T.fig[:, W - ROT:W], EXT), figs)
+    mates(1, "yy", figs)
 
-    def suppress(ns):
+    def suppress(ns, between):
         first = 24 - ns
-        TS(R("SP", 0, ns), R("HLf", 24 + first, 48), -1.0, 0.5, A.mult, A.add)
-        TS(R("SN", 0, ns), R("HLf", 24 + first, 48), 0.5, None, A.add)
+
+        def count_in(e):
+            q = 32 * (e % 8 // 2)
+            MM([(X(T.pH[q:q + 32, 0:256], "pH"), R("HOH", 32 * e, 32 * e + 32), X(T.LOH[:, e, :], "LOH", e, e + 1), False, e > 16 and e % 2 == 1)])
         for k in range(ns):
-            ACT(X(T.ST1[:, k, :], "ST1", k, k + 1), R("LIO"), F.Sign, bias=R("SP", k, k + 1))
-            ACT(X(T.ST2[:, k, :], "ST2", k, k + 1), R("LIO"), F.Sign, bias=R("SN", k, k + 1), scale=-1.0)
-        order = list(range(0, 10)) + list(range(first, 24)) + list(range(10, first))
-        for n, e in enumerate(order):
-            hoh = X(T.HOH[:, e, :], "HOH", e, e + 1)
-            TS(hoh, R("HIO"), R("HLf", e, e + 1), R("gn", e % 8, e % 8 + 1), eq, A.mult)
-            if e < first:
-                loh = X(T.LOH[:, e, :], "LOH", e, e + 1)
-                TS(loh, R("LIO"), R("HLf", 24 + e, 25 + e), 2.0, eq, A.mult)
-                MM(R("pH", 0, 256), [(hoh, loh)], n == 0, n == 23)
-            else:
-                k = e - first
-                MM(R("pH", 0, 256), [(hoh, X(T.ST1[:, k, :], "ST1", k, k + 1)), (hoh, X(T.ST2[:, k, :], "ST2", k, k + 1))], False, n == 23)
+            ACT(X(T.AB[:, k, :], "AB", k, k + 1), R("LIO"), F.Abs, bias=R("nlo", first + k, first + k + 1))
+        for k in range(ns):
+            e = first + k
+            ACT(X(T.LOH[:, e, :], "LOH", e, e + 1), X(T.AB[:, k, :], "AB", k, k + 1), F.Relu, bias=R("val", e % 8, e % 8 + 1), scale=-1.0)
+        TT(ALL("HOH"), IND(R("hiI"), R("repU", 8 * NV, 8 * NV + 48)), ALL("HIO"), eq)
+        for e in range(first):
+            TS(X(T.LOH[:, e, :], "LOH", e, e + 1), R("NIO"), R("nlo", e, e + 1), R("val", e % 8, e % 8 + 1), eq, mul)
+            count_in(e)
+        for e in range(first, 24):
+            count_in(e)
+        between()
 
     for t in range(ROUNDS):
         xy, z = "XY%d" % t, "Z%d" % t
-        zoff = 0.0 if t == 0 else -128.0
+        win = "WF" if t else "MW"
         LX, LY = R(xy, 0, 8), R(xy, 8, 16)
         XM = R("XM%d" % (t % 2))
-        TS(R("R2"), IND(XM, LX), 2.0, 593.0, A.mult, A.add)
-        ACT(R("U"), IND(R("IOTA"), LX), F.Identity, bias=R("BIA"), scale=R("SCA"))
-        ACT(R("WN"), IND(R("IOTA"), LY), F.Identity, bias=R("BIB"), scale=R("SCB"))
-        TS(R("C2"), IND(XM, LY), 2.0, 17.0, A.mult, A.add)
-        if t:
-            for k in range(2):
-                hl = X(T.HLC[:, k, :], "HLC", 256 * k, 256 * k + 256)
-                TT(hl, hl, R("pH", 0, 256), A.subtract)
-            spread_sums()
-        MM(R("pM", 0, 128), [(R("sA"), R("R2"))], True, False)
-        MM(R("pM", 0, 128), [(R("sB"), R("C2"))], False, True)
-        MM(R("pN", 0, 128), [(R("sI"), R("C2"))])
-        JP = [R(("pJP", "pA")[a // 2], 128 * (a % 2), 128 * (a % 2) + 128) for a in range(4)]
+        TS(R("C2"), IND(XM, LY), R("S2H"), R("C2B"), mul, add)
+        TS(R("R2"), IND(XM, LX), R("S2L"), R("R2B"), mul, add)
+        ACT(R("U"), IND(R("IOTA"), LX), F.Identity, bias=R("BIA"), scale=R("S2L"))
+        ACT(R("WN"), IND(R("IOTA"), LY), F.Identity, bias=R("BIB"), scale=R("S2H"))
+        TS(R("mo"), R(xy), -2048.0, None, add)
+        ACC(R("pM", 256, 384), [(R("sI"), R("C2"))])
+        ACT(R("IPs"), R("pM", 256, 384), F.Copy)
+        JP = [R("pJ", 128 * a, 128 * a + 128) for a in range(4)]
+        MM([(JP[a], R("sJ%d" % a), R("R2"), True, True) for a in range(4)])
+        ACC(R("pM", 128, 256), [(R("IDf"), R("U")), (R("IDf"), R("WN"))])
+        ACT(R("OT"), R("pM", 128, 256), F.Copy)
+        ACC(R("pM", 0, 128), [(R("sA"), R("R2")), (R("sB"), R("C2"))])
         for a in range(4):
-            MM(JP[a], [(R("sJ%d" % a), R("R2"))])
-        for k in range(16):
-            if k == 12:
-                ACT(R("IPs"), R("pN", 0, 128), F.Copy)
-            ACT(X(T.Zr[:, k:2048:16], "Zr", k, k + 1), R(z), F.Copy, bias=zoff)
-        ACT(X(T.MW[:, W:W + 128], "MW", W, W + 128), R(z), F.Copy, bias=2 * zoff, scale=2.0)
-        TT(R("OT"), R("U"), R("WN"), A.add)
-        TC(R("XYf"), R(xy))
-        TS(R("UWO", 0, 8), R("XYf", 0, 8), 2.0, 17.0, A.mult, A.add)
-        TS(R("UWO", 8, 16), R("XYf", 8, 16), 2.0, 593.0, A.mult, A.add)
-        TS(R("t8"), R("XYf", 0, 8), 2048.0, PC, A.mult, A.add)
-        TT(R("PP"), R("t8"), R("XYf", 8, 16), A.add)
-        TT(R("F12q"), R("pM", 0, 128), R("OT"), A.mult)
-        TS(R("F12i"), R("F12q"), 5, W - 1, SHR, AND)
-        TC(R("F12u"), R("F12i"))
-        for a in range(4):
-            TT(R("F3q", 128 * a, 128 * a + 128), JP[a], R("IPs"), A.mult)
-        TS(R("F3i"), R("F3q"), 5, W - 1, SHR, AND)
-        TC(R("F3u"), R("F3i"))
+            TT(X(T.Fq[:, :, :, 1 + a], "Fq", 1 + a, 2 + a), JP[a], R("IPs"), mul)
+        TT(X(T.Fq[:, :, :, 0], "Fq", 0, 1), R("pM", 0, 128), R("OT"), mul)
+        ACT(R("NZf"), R(z), F.Copy, bias=128.0 + EPS)
+        ACT(R("Zr"), IND(R(z), R("repU", 0, 8 * NV)), F.Copy, bias=-128.0 - EPS, scale=-1.0)
+        ACT(R("MT"), R("pM", 0, 128), F.Copy, bias=-2056.5, scale=0.5)
+        TS(ALL("FiS"), X(T.Fq[:, :, NV:16, :], "Fq"), 5, W - 1, SHR, AND)
+        TS(R("FiV"), X(T.Fq[:, :, 0:NV, :], "Fq"), 5, W - 1, SHR, AND)
+        TC(X(T.FS[:, :, :, 0:5], "FS"), ALL("FiS"))
+        TC(R("FV"), IND(R("FiV"), R("perU", 0, NPER)))
+        bs = X(T.BBb[:, :, NV:16], "BBb")
+        ACC(R("pM", 0, 8 * NS), [(R(z), bs), (R("C128"), bs)])
+        TT(ALL("RZ"), R("pM", 0, 8 * NS), R("DM"), mul)
+        ACC(R("pM", 0, 56), [(R("OT"), R("sO")), (R("ONE"), R("cK"))], True, False)
+        if t == 0:
+            TC(R("SEL0"), ALL("SELb"))
+            TC(R("SEL1"), ALL("SELd"))
+            TC(R("SELJ"), R("SELe"))
+            TS(R("BP"), R("B16"), SIG, None, add)
+        ACC(R("pH", 0, 256), [(R("IDf"), R("W0")) if t else (R("IDb"), R("B16"))], True, False)
+        ACC(ALL("pE"), [(R("IDb"), R("RHO"))], True, False)
+        MM([(R("pJ", 0, 256), R("IDh"), R("MKB"), True, False), (R("pJ", 256, 272), R("IDh"), R("mo"), False, False)])
 
-        def look_v(e, lo, f, flo, n):
-            TT(R(e, lo, lo + 16 * n), IND(R("MW", 0, W), R(f, flo, flo + n)), X(T.Zr[:, lo % 2048:lo % 2048 + 16 * n], "Zr"), A.is_lt)
+        def rectangles(kp, xs, sel0, sel):
+            reg = (lambda x: (x, x + 1)) if kp == "KV" else (lambda x: (0, NS))
+            MM([(R("pE", x - 1, 512, 4) if x else ALL("pE"), X(T[kp][:, x], kp, *reg(x)), R(sel if x else sel0), False, kp == "KS" and x == 4) for x in xs])
 
-        def look_c(e, lo, f, flo, n):
-            ACT(R(e, lo, lo + 16 * n), IND(R("CW"), R(f, flo, flo + n)), F.Relu)
-
-        def chunk(out, e, off, sel, start, stop, c0=0, c1=16):
-            for c in range(c0, c1):
-                MM(out, [(X(T[sel][:, c, :], sel, c, c + 1), R(e, off + 128 * c, off + 128 * c + 128))], start and c == 0, stop and c == 15)
-        PKR = X(T.pK[:], "pK")
-        look_c("E12c", 0, "F12u", 0, 128)
-        look_v("E12v", 0, "F12u", 0, 128)
-        for b, nm in enumerate(("pA", "pB")):
-            MM(R(nm, 0, 256), [(R("IDb"), R("RHO", 256 * b, 256 * b + 256))], True, False)
-        for k in range(8):
-            MM(R("pM2", 16 * k, 16 * k + 16), [(R("sA"), R("R2", k, 128, 8)), (R("sB"), R("C2", k, 128, 8))])
-        chunk(PKR, "E12v", 0, "SEL", True, False)
-        banks = [R(("pA", "pB")[a // 2], 128 * (a % 2), 128 * (a % 2) + 128) for a in range(4)]
-        for a in range(4):
-            lo = 2048 * a
-            parts = ((0, 128),) if a < 3 else ((0, 64), (64, 32), (96, 32))
-            for (p, n) in parts:
-                look_v("E3v", lo + 16 * p, "F3u", 128 * a + p, n)
-                look_c("E3c", lo + 16 * p, "F3u", 128 * a + p, n)
-            if a == 0:
-                chunk(PKR, "E12c", 0, "SELC", False, True)
-                if t == 0:
-                    late_constants()
-            if a == 1:
-                ACT(R("MT2s"), R("pM2", 0, 128), F.Copy)
-                for l in range(2):
-                    ACT(X(T.K2Y[:, :, 8 * l:8 * l + 8], "K2Y", l, l + 1), X(T.pK[:, :, 8:16], "pK"), F.Copy)
-                for x in range(4):
-                    ACT(X(T.K1s[:, x, :, :], "K1s", x, x + 1), X(T.pK[:, :, 2 * x:2 * x + 2], "pK"), F.Copy)
-                for x in range(2):
-                    MM(banks[x], [(R("IDf"), X(T.K2Y[:], "K2Y"))], False, False)
-            if a == 2:
-                for x in range(2):
-                    MM(banks[2 + x], [(R("IDf"), X(T.K2Y[:], "K2Y"))], False, False)
-                MM(R("pN", 0, 128), [(R("IDf"), R("NPC"))], True, False)
-            for (p, n) in parts:
-                chunk(banks[a], "E3c", lo, "SELC", False, False, p // 8, (p + n) // 8)
-                chunk(banks[a], "E3v", lo, "SEL", False, a % 2 == 1, p // 8, (p + n) // 8)
-        for b, nm in enumerate(("pA", "pB")):
-            SCAN(R("M1", 256 * b, 256 * b + 256), R("RST"), R(nm, 0, 256), 0.0, A.max, A.min)
-            m = R("M2", 32 * b, 32 * b + 32)
-            TT(m, R("M1", 256 * b + 7, 256 * b + 256, 8), X(T.K1s[:, 2 * b:2 * b + 2, :, :], "K1s", 2 * b, 2 * b + 2), A.add)
-            TT(R("MA", 16 * b, 16 * b + 16), R("M2", 32 * b, 32 * b + 16), R("M2", 32 * b + 16, 32 * b + 32), A.min)
-        TT(R("MA", 0, 16), R("MA", 0, 16), R("MA", 16, 32), A.min)
-        TT(R("MB"), R("MA", 0, 16, 2), R("MA", 1, 16, 2), A.min)
+        def step(s):
+            k = s[2:]
+            if s[:2] == "gv":
+                x = int(k)
+                TT(X(T.EV[:, x], "EV", x, x + 1), IND(R(win, 0, W), R("FV", 8 * NV * x, 8 * NV * (x + 1))), R("Zr"), A.max)
+            elif s[:2] == "gs":
+                q = int(k)
+                for c in range(8):
+                    j = 16 * c + NV + q
+                    ACT(X(T.ES[:, q, c:640:8], "ES", 8 * q + c, 8 * q + c + 1), IND(R(win, 0, W), X(T.FS[:, c, q, 0:5], "FS")), F.Relu, bias=R("NZf", j, j + 1))
+            elif s[:2] == "mv":
+                x = int(k)
+                b, lo, hi = [c for n, c in CHUNKS.items() if n[0] == "V" and c[1] <= x < c[2]][0]
+                MM([(X(T[b][:, x - lo, 0, :, p], b), X(T.EV[:, x, 128 * p:128 * p + 128], "EV", x, x + 1), R("ST1"), x == lo and p == 0,
+                     x == hi - 1 and p == NV - 1) for p in range(NV)])
+            elif s[:2] == "ms":
+                q = int(k)
+                b, lo, hi = [c for n, c in CHUNKS.items() if n[0] == "S" and c[1] <= q < c[2]][0]
+                MM([(X(T[b][:, x, 0, :, q - lo], b), X(T.ES[:, q, 128 * x:128 * x + 128], "ES", 8 * q, 8 * q + 8), R("ST1"), q == lo and x == 0,
+                     q == hi - 1 and x == 4) for x in range(5)])
+            else:
+                b, lo, hi = CHUNKS[s[1:]]
+                if s[1] == "V":
+                    part = [X(T[b][:, 0:hi - lo, w, :, 0:NV], b) for w in range(2)]
+                    rb = R("RB", 8 * NV * lo, 8 * NV * hi)
+                    kp = X(T.KV[:, lo:hi, :, 0:NV], "KV", lo, hi)
+                else:
+                    part = [X(T[b][:, 0:5, w, :, 0:hi - lo], b) for w in range(2)]
+                    rb = R("RB", 40 * (NV + lo), 40 * (NV + hi))
+                    kp = X(T.KS[:, :, :, NV + lo:NV + hi], "KS", lo, hi)
+                if s[0] == "r":
+                    TS(rb, part[0], MAGIC, -MAGIC, add, add)
+                elif s[0] == "d":
+                    db = R("DB", *rb[1][0][1:])
+                    TT(db, rb, part[0], A.subtract)
+                    more = [(X(T[b][:, x, 1, :, 0:hi - lo], b), R("CD"), X(T.RZ[:, :, lo:hi], "RZ"), False, False) for x in range(5)] if s[1] == "S" else []
+                    MM([(part[1], R("I16"), rb, True, False)] + more + [(part[1], R("I15"), db, False, True)])
+                elif s[0] == "e":
+                    rectangles("KV", range(lo, hi), "SEL0", "SELI")
+                else:
+                    TS(kp, part[1], 8192.0 if s[1] == "S" else 0.0, 0.0, add, A.max)
+        for s in ORDER:
+            step(s)
+        ACT(R(win, W, W + 128), R(z), F.Copy, bias=-256.0, scale=-2.0)
+        rectangles("KS", range(5), "SEL1", "SELJ")
+        SCAN(R("M1"), R("RST"), ALL("pE"), 0.0, A.max, A.min)
         mk = R("mki", 8 * t, 8 * t + 8)
-        TS(mk, R("MB"), CLIP, None, A.min)
+        TS(mk, R("M1", 63, 512, 64), CLIP, -CLIP, A.min, add)
+        TS(R("mkf"), R("M1", 63, 512, 64), CLIP, -CLIP, A.min, add)
         TS(R("rhoI"), mk, 127, None, AND)
+        MM([(R("pJ", 256 + 8 * w, 264 + 8 * w), R("NIDf"), R("mkf"), False, False) for w in range(2)])
         TC(R("rhoU"), R("rhoI"))
-        TT(R("NM"), IND(R("OHW"), R("rhoU")), R("MT2s"), A.mult)
-        MM(R("pN", 0, 128), [(R("PK"), R("NM"))], False, True)
-        if t == ROUNDS - 1:
-            TS(R("cI"), R("mki"), 7, None, SHR)
-            TS(R("G"), R("mki"), CLIP, None, A.is_lt)
-            TS(R("cf"), R("cI"), 1.0, None, A.add)
-        TT(R("NMm"), R("pN", 0, 128), R("DMK"), A.mult)
-        TT(R("T64"), R("NMm", 0, 64), R("NMm", 64, 128), A.add)
-        TT(R("T32"), R("T64", 0, 32), R("T64", 32, 64), A.add)
-        TT(R("T16"), R("T32", 0, 16), R("T32", 16, 32), A.add)
-        TT(R("P8"), R("T16", 0, 16, 2), R("T16", 1, 16, 2), A.add)
-        TS(R("k0"), R("P8"), 0.0, None, A.is_lt)
-        TT(R("k1"), R("k0"), R("PP"), A.mult)
-        TT(R("Pi"), R("P8"), R("k1"), A.add)
-        TS(R("XYi", 0, 8), R("Pi"), 11, None, SHR)
-        TS(R("XYi", 8, 16), R("Pi"), 2047, None, AND)
+        TT(R("NM"), IND(R("OHW"), R("rhoU")), R("MT"), mul)
+        MM([(R("pJ", 128 * w, 128 * w + 128), R("PK%d" % w), R("NM"), False, w == 1) for w in range(2)])
+        ACC(R("pM", 0, 56), [(R("NM"), R("sN"))], False)
+        TT(R("kj"), R("KJ"), R("mkf"), add)
+        NEW = R("NEW")
 
         def pass_names():
-            TC(R("XYs"), R("XYi"))
+            SCAN(R("NSC"), R("RS16"), R("pJ", 0, 256), 0.0, A.max, A.min)
+            TT(NEW, R("pJ", 256, 272), R("NSC", 15, 256, 16), A.min)
+            TS(R("XYs"), NEW, 2048.0, None, add)
             remote(t, "n", "XY%d" % (t + 1), R("XYs"))
 
+        def corners():
+            TC(R("Asb"), R("pM", 0, 24))
+            TS(R("val"), R("pM", 48, 56), 0.0, SIG, A.not_equal, mul)
+            TT(R("QC"), R("pM", 24, 48), R("Asb"), mul)
+            TS(R("loI"), R("QC"), 5, 255, SHR, AND)
+            TS(R("hiI"), R("QC"), 13, 15, SHR, AND)
+            TS(R("nlo"), R("loI"), -1.0, None, mul)
+
         def pass_needs():
-            TT(R("kj"), R("k0"), R("KJ"), A.mult)
-            TS(R("FC3"), R("QC", 16, 24), 5, W - 1, SHR, AND)
-            TT(R("far2"), R("FC3"), R("kj"), A.max)
-            TC(R("farU"), R("far2"))
-            TS(R("Zs"), IND(R("MW"), R("farU")), 0.5, 127.75, A.mult, A.add)
+            TS(R("UW"), NEW, 2.0, 4113.0, mul, add)
+            TT(R("q3"), R("UW", 0, 8), R("UW", 8, 16), mul)
+            TS(R("FC"), R("q3"), 5, W - 1, SHR, AND)
+            TT(R("far"), R("FC"), R("kj"), A.max)
+            TC(R("farU"), R("far"))
+            ACT(R("Zs"), IND(R(win), R("farU")), F.Copy, bias=-127.8, scale=-0.5)
             remote(t, "z", "Z%d" % (t + 1), R("Zs"))
         if t < ROUNDS - 1:
             pass_names()
-        TS(R("UWN", 0, 8), R("XYi", 0, 8), 2.0, 17.0, A.mult, A.add)
-        TS(R("UWN", 8, 16), R("XYi", 8, 16), 2.0, 593.0, A.mult, A.add)
-        TT(R("QC", 16, 24), R("UWN", 0, 8), R("UWN", 8, 16), A.mult)
-        if t < ROUNDS - 1:
             pass_needs()
-        TT(R("QC", 0, 8), R("UWO", 0, 8), R("UWN", 8, 16), A.mult)
-        TT(R("QC", 8, 16), R("UWN", 0, 8), R("UWO", 8, 16), A.mult)
-        TS(R("gn"), R("k0"), 0.0, 64.0, eq, A.mult)
-        TS(R("HLi", 0, 24), R("QC"), 13, 15, SHR, AND)
-        TS(R("HLi", 24, 48), R("QC"), 5, 255, SHR, AND)
-        TC(R("HLf"), R("HLi"))
-        suppress(NS[t])
-        if t == ROUNDS - 1:
-            pass_names()
+            corners()
+            suppress(NSE[t], lambda: None)
+            TT(R("W0"), R("pH", 0, 256), R("BP"), A.min)
+            dma("y", X(T.WF[0::16, 0:W], "WF", 0, W), R("W0"))
+            if t == 0:
+                IOTA(ALL("ONEb"), [[0, 2048]], 1, 0)
+                AFF(ALL("EXPM"), ALL("ONEb"), [[-1, 16], [-16, 8], [0, 16]], eq, 0.0, 0, 1)
+        else:
+            corners()
+            suppress(NSE[t], pass_names)
+            TT(R("FL"), R("pH", 0, 256), R("B16"), A.is_gt)
+            TS(R("SG"), R("FL"), -2.0, 1.0, mul, add)
             pass_needs()
-            TT(R("SG"), X(T.HLC[:, 0, :], "HLC", 0, 256), R("pH", 0, 256), A.subtract)
-            TS(R("SG"), R("SG"), 0.0, 2.0, A.is_gt, A.mult)
-            TS(R("SG"), R("SG"), -1.0, None, A.add)
 
     e = ROUNDS
-    banks = ("pA", "pB", "pJP", "pM")
+    banks = ("pA", "pB", "pC", "pD")
+    half = {"pA": 1, "pB": 1, "pC": 4, "pD": 4}
     for k in range(8):
         nm = banks[k % 4]
-        for x in range(2):
-            MM(R(nm, 256 * x, 256 * x + 256), [(X(T.EXPM[:, 2 * k + x, :], "EXPM"), R("SG"))])
-        TT(R("YF", 512 * k, 512 * k + 512), R("MW", 512 * k, 512 * k + 512), R(nm, 0, 512), A.mult)
+        MM([(X(T[nm][:, half[nm] * x:half[nm] * (x + 1)], nm), X(T.EXPM[:, 2 * k + x, :], "EXPM"), R("SG"), True, True) for x in range(2)])
+        TT(R("YF", 512 * k, 512 * k + 512), R("MW", 512 * k, 512 * k + 512), ALL(nm), mul)
         if k == 0:
             dma("s", (T.yf[:, 0:512 - ROT], EXT), R("YF", ROT, 512))
             dma("y", (T.yf[:, W - ROT:W], EXT), R("YF", 0, ROT))
-            TT(R("cst"), R("cf"), R("G"), A.mult)
-            TS(R("cst"), R("cst"), -1.0, None, A.add)
-            for x in range(ROUNDS):
-                dma(("s", "y")[x % 2], (T.yc[:, 128 * x:128 * x + 128], EXT), R("cst", 8 * x, 8 * x + 8))
+            TS(R("cI"), R("mki"), 64.0, None, add)
+            TS(R("G"), R("mki"), 0.0, None, A.is_lt)
+            TS(R("cI"), R("cI"), 7, None, SHR)
+            TS(R("cf"), R("cI"), 6145.0, None, add)
+            TT(R("cst"), R("cf"), R("G"), mul)
+            ACC(X(T.pM[0:32, 0:128], "pM"), [(R("cst"), R("IDf"))])
+            ACT(X(T.CT[0:32, :], "CT"), X(T.pM[0:32, 0:128], "pM"), F.Copy, bias=-1.0)
+            for x in range(8):
+                dma(("s", "y")[x % 2], (T.yc[x:x + 1, :], EXT), X(T.CT[0:32, 16 * x:16 * x + 16], "CT"))
         elif k % 2 == 0:
             dma(("s", "y")[k // 2 % 2], (T.yf[:, 512 * (k - 1) - ROT:512 * (k + 1) - ROT], EXT), R("YF", 512 * (k - 1), 512 * (k + 1)))
         if k == 5:
-            TC(R("YP"), R("XY%d" % e))
+            TC(R("YP", 0, 8), R("XY%d" % e, 0, 8))
+            TS(R("YP", 8, 16), R("XY%d" % e, 8, 16), -float(JO), None, add)
             dma("y", (T.yp[:], EXT), R("YP"))
     dma("s", (T.yf[:, 3584 - ROT:W - ROT], EXT), R("YF", 3584, W))
-    TS(R("YZ"), R("Z%d" % e), -128.0, None, A.add)
+    ACT(R("YZ"), R("Z%d" % e), F.Copy, bias=-128.0, scale=-1.0)
     dma("y", (T.yz[:], EXT), R("YZ"))
     for s, n in sorted(count.items()):
         if known["g"].get(s, 0) < n:

@@ -3,17 +3,20 @@ from concourse.mybir import AluOpType as A, ActivationFunctionType as F
 ROT = 315
 W, NI, NJ = 4096, 2048, 1536
 JO = 288
-EPS, SIG = 1.0 / 64, 1.0 / 256
+EPS, EPS0, SIG = 1.0 / 16, 1.0 / 4, 1.0 / 2
+BIGA, BIG0 = 2.0 ** 15, 2.0 ** 11
+LIFT = BIGA * 15 * EPS + BIG0 * EPS0
 MAGIC = 1.5 * 2 ** 23
 CLIP = float(128 * 6144 + 64)
 ROUNDS = 4
 NV = 9
 NS = 16 - NV
 NPER = (40 * NV + 15) // 16
-NSE = [5, 5, 5, 6]
+NSE = 7
+CUT = 5
 CHUNKS = {"VA": ("pA", 0, 2), "VB": ("pB", 2, 4), "VC": ("pA", 4, 5), "SA": ("pC", 0, 4), "SB": ("pD", 4, 6), "SC": ("pC", 6, 7)}
-ORDER = ("gs0 gs1 gs2 gs3 gs4 gs5 gs6 ms0 gv0 mv0 ms1 gv1 mv1 ms2 gv2 rVA mv2 dVA ms3 gv3 kVA rSA eVA dSA mv3 ms4 gv4 kSA rVB mv4 dVB ms5 "
-         "rVC rSB dVC dSB kVB eVB ms6 kVC kSB eVC rSC dSC kSC").split()
+ORDER = ("gs0 gs1 gs2 ms0 gv0 mv0 ms1 gv1 mv1 ms2 gv2 gs3 rVA mv2 ms3 gv3 gs4 KVA rSA eVA mv3 ms4 gv4 gs5 KSA rVB mv4 gv5 ms5 mv5 "
+         "gs6 rSB rVC kVB eVB ms6 kSB rSC kVC eVC kSC").split()
 
 SB = {}
 POOL = {}
@@ -37,15 +40,15 @@ _small("rhoI q3 FC far", 8, "int32")
 _small("mki cI", 8 * ROUNDS, "int32")
 _small("repI", 8 * NV + 48, "int32")
 _small("PI P15i", 1, "int32")
-_small("KJ kj mkf val ST1", 8)
-_small("G cf cst", 8 * ROUNDS)
+_small("KJ nm val", 8)
+_small("cf cn", 8 * ROUNDS)
 _small("UW YP NEW", 16)
 _small("Asb nlo", 24)
 _small("sO cK", 56)
 _small("DM", 8 * NS)
 _small("FU", 2 * NPER)
 _small("FUa FUb", NPER)
-_small("P15 SLO SHI S2L S2H R2B C2B BIA BIB CKR CKC T1 T2 QA QB QB8 QJ1 QJ2 QJ3 P7", 1)
+_small("P15 SLO SHI S2L S2H R2B C2B BIA BIB CKR CKC T0 T1 T8 T9 QA QB QB8 QJ1 QJ2 QJ3 P7 P45 CLP LFT R0 RA WX EN EZ", 1)
 _sb("poolF", [USED["poolF"]])
 _sb("poolI", [USED["poolI"]], "int32")
 _sb("prowI pcolI", [8], "int32")
@@ -55,35 +58,38 @@ for _t in range(ROUNDS + 1):
     _sb("Z%d" % _t, [128], "bfloat16")
 _sb("XYs", [16], "uint16")
 _sb("repU", [8 * NV + 48], "uint16")
-_sb("Zs Zin YZ IDb C128", [128], "bfloat16")
+_sb("Zs Zin YZ IDb C128 AVG", [128], "bfloat16")
+_sb("OFV", [2, 2, 8, NV], "bfloat16")
+_sb("OFS", [5, 2, 8, 4], "bfloat16")
+_sb("ST1", [16], "float16")
+_sb("ST2", [8], "float16")
 _sb("BBb", [8, 16], "bfloat16")
 _sb("XM0 XM1", [NI], "int32")
 _sb("MW", [W + 128], "bfloat16")
-_sb("WF", [W + 128])
 _sb("YF", [W], "bfloat16")
 _sb("IOTA", [NI])
-_sb("ONE BT BB OFF C16 C8 CAL IDf NIDf OHW U WN OT IPs MT NZf CT", [128])
-_sb("sJ0 sJ1 sJ2 sJ3 sA sB sI PK0 PK1 IDh I15 I16 SELI CD R2 C2 NM", [128], "float16")
+_sb("C16", [8, 16])
+_sb("ONE BB OFF C16m C8 C8m CAL IDf NIDf OHW OT IPs MT NZf CT", [128])
+_sb("sJ0 sJ1 sJ2 sJ3 sA sB sI PK0 PK1 IDh I15 I11 I16 SELI SELJ CD R2 C2 NM U WN", [128], "float16")
 _sb("sN", [56], "float16")
 _sb("mo", [16], "float16")
 _sb("RZ", [8, NS], "float16")
 _sb("SEL0 SEL1", [512], "float16")
-_sb("SELJ", [128], "float16")
 _sb("MKB", [256], "float16")
-_sb("RB DB", [640], "float16")
+for _n, (_b, _lo, _hi) in CHUNKS.items():
+    _sb("R" + _n, [_hi - _lo, 2, 8 * NV] if _n[0] == "V" else [5, 2, 8 * (_hi - _lo)], "float16")
 _sb("KV KS", [5, 8, 16], "float16")
 _sb("RHO ZEb", [512], "bfloat16")
 _sb("SELa SELb SELc SELd", [8, 2, 32], "bfloat16")
-_sb("SELe", [128], "bfloat16")
-_sb("ONEb EXPM", [16, 128], "bfloat16")
+_sb("SELe LIO NIO", [128], "bfloat16")
+_sb("EXPM", [32, 64], "bfloat16")
 _sb("NEG RST M1", [512])
-_sb("RS16 NSC MKI", [256])
+_sb("RS16 NSC", [256])
 _sb("OHA OHB", [64])
-_sb("LIO NIO SG FL B16", [256], "bfloat16")
-_sb("BP W0", [256])
+_sb("SG FL B32 BP W0", [256], "bfloat16")
 _sb("HIO HOH", [768], "bfloat16")
-_sb("LOH", [24, 256], "bfloat16")
-_sb("AB", [6, 256], "bfloat16")
+_sb("LOH", [24, 128], "bfloat16")
+_sb("AB", [NSE, 128], "bfloat16")
 _sb("Fq", [8, 16, 5], "int32")
 _sb("FiS", [8, NS, 5], "int32")
 _sb("FiV", [40 * NV], "int32")
@@ -91,8 +97,8 @@ _sb("perU", [NPER + NPER % 2], "uint16")
 _sb("FS", [8, NS, 6], "uint16")
 _sb("FV", [16 * NPER], "uint16")
 _sb("Zr", [128 * NV])
-_sb("EV", [5, 128 * NV])
-_sb("ES", [NS, 640])
+_sb("EV", [5, 128 * NV], "float16")
+_sb("ES", [NS, 640], "float16")
 for _n, _s in (("pA", [2, 2, 8, 16]), ("pB", [2, 2, 8, 16]), ("pC", [8, 2, 8, 4]), ("pD", [8, 2, 8, 4]), ("pE", [512]),
                ("pH", [512]), ("pJ", [512]), ("pM", [512])):
     SB[_n] = ("psum", [128] + _s, "float32")
@@ -163,13 +169,14 @@ def rank_program(g, core, T, topo):
         inst.then_inc(T.sem[sem], 1)
         note(q, sem, count[sem], reads, writes, dict(known[q]))
 
-    def dma(q, out, in_, after=()):
-        sem = "d%d" % ndma[0]
-        ndma[0] += 1
-        need_waits(q, in_[1] + list(after), out[1], True)
+    def dma(q, out, in_, after=(), skip=False):
+        ndma[0] += 0 if skip else 1
+        sem = "d%d" % (ndma[0] - 1)
+        if not skip:
+            need_waits(q, in_[1] + list(after), out[1], True)
         queues[q].dma_start(out[0], in_[0]).then_inc(T.sem[sem], 16)
-        count[sem] = 16
-        note(sem, sem, 16, in_[1], out[1], dict(known[q]))
+        count[sem] = count.get(sem, 0) + 16
+        note(sem, sem, count[sem], in_[1], out[1], dict(known[q]))
 
     def R(n, lo=0, hi=None, step=1):
         if n in POOL:
@@ -210,7 +217,7 @@ def rank_program(g, core, T, topo):
     def SCAN(out, d0, d1, init, op0, op1):
         emit("v", lambda: g.vector.tensor_tensor_scan(out[0], d0[0], d1[0], init, op0, op1), regs_of(d0, d1), out[1])
 
-    def ACT(out, a, func, bias=0.0, scale=1.0):
+    def ACT(out, a, func=F.Identity, bias=0.0, scale=1.0):
         emit("s", lambda: g.scalar.activation(out[0], a[0], func, bias=val(bias), scale=val(scale)), regs_of(a, bias, scale), out[1])
 
     def MM(items):
@@ -271,170 +278,189 @@ def rank_program(g, core, T, topo):
     MS(R("ONE"), 1.0)
     MS(R("FU"), 0.0)
     IOTA(R("PI"), [[1, 1]], 0, 1, False)
-    IOTA(R("C16"), [[0, 8], [1, 16]], 0, 0)
+    AFF(R("BB"), R("ONE"), [[-16, 8], [0, 16]], ge, 0.0, 0, 1)
+    AFF(R("BB"), R("BB"), [[16, 8], [0, 16]], ge, 0.0, 15, -1)
+    IOTA(ALL("C16"), [[0, 8], [1, 16]], 0, 0)
     IOTA(R("C8"), [[0, 16], [1, 8]], 0, 0)
     IOTA(R("CAL"), [[0, 8], [1, 2], [0, 8]], 0, 0)
-    AFF(R("BT"), R("ONE"), [[-16, 8], [0, 16]], ge, 0.0, 0, 1)
-    AFF(R("BB"), R("BT"), [[16, 8], [0, 16]], ge, 0.0, 15, -1)
+    IOTA(R("IOTA"), [[1, NI]], 0, 0)
     AFF(R("IDf"), R("ONE"), [[-1, 128]], eq, 0.0, 0, 1)
     IOTA(R("repI", 0, 8 * NV), [[1, NV], [16, 8]], 0, 0, False)
     IOTA(R("FU", 0, 5 * NV), [[1, 5], [5, NV]], 0, 0)
-    IOTA(R("IOTA"), [[1, NI]], 0, 0)
-    IOTA(R("repI", 8 * NV, 8 * NV + 48), [[1, 24], [0, 2]], 0, 0, False)
-    IOTA(R("DM"), [[0, 8], [1, NS]], NV, 0)
-    IOTA(R("RHO"), [[0, 8], [1, 16], [16, 4]], 0, 0)
-    IOTA(R("MKI"), [[0, 16], [1, 16]], 0, 0)
     IOTA(R("OHA"), [[1, 8], [0, 8]], 0, 0)
-    IOTA(R("OHB"), [[0, 8], [1, 8]], 8, 0)
+    IOTA(R("repI", 8 * NV, 8 * NV + 48), [[1, 24], [0, 2]], 0, 0, False)
+    IOTA(R("RHO"), [[0, 8], [1, 16], [16, 4]], 0, 0)
     IOTA(R("KJ"), [[16, 8]], W, 0)
 
-    blank(1)
+    TS(R("P15i"), R("PI"), 15, None, AND)
     MS(R("NEG"), -1e9)
+    TC(R("P15"), R("P15i"))
     MS(R("ZEb"), 0.0)
+    TS(R("SLO"), R("P15"), 8.0, None, A.is_lt)
+    TS(R("SHI"), R("P15"), 8.0, None, ge)
+    TS(R("S2L"), R("P15"), 8.0, 2.0, A.is_lt, mul)
+    TS(R("S2H"), R("P15"), 8.0, 2.0, ge, mul)
+    TS(R("BIA"), R("P15"), 8.0, -4096.0, A.is_lt, mul)
+    TS(R("BIB"), R("P15"), 8.0, -4096.0, ge, mul)
+    TS(R("R0"), R("P15"), 0.0, None, eq)
+    TS(R("RA"), R("P15"), 0.0, None, A.is_gt)
+    TS(R("WX"), R("R0"), BIGA - BIG0, -BIGA, mul, add)
+    TS(R("EN"), R("R0"), EPS0 - EPS, 128.0 + EPS, mul, add)
+    TS(R("EZ"), R("R0"), EPS - EPS0, -128.0 - EPS, mul, add)
+    for n, r, c in (("T0", 0.0, 512.0), ("T1", 1.0, 2.125), ("T8", 8.0, 512.0), ("T9", 9.0, 2.125)):
+        TS(R(n), R("P15"), r, c, eq, mul)
+    TS(R("R2B"), R("SLO"), 2.0 * (JO - 2048) - 1, 1.0, mul, add)
+    TS(R("C2B"), R("SHI"), -4097.0, 1.0, mul, add)
+    TS(R("QA"), R("SHI"), -50.0, R("P15"), mul, add)
+    TS(R("QB8"), R("SLO"), -50.0, R("P15"), mul, add)
+    TS(R("P7"), R("SHI"), -8.0, R("P15"), mul, add)
+    TT(R("CKR"), R("T8"), R("T9"), add)
+    TT(R("CKC"), R("T0"), R("T1"), add)
+    TS(R("OFF"), R("BB"), -999.0, 999.0, mul, add)
+    TS(R("QB"), R("QB8"), -8.0, None, add)
+    for a in range(1, 4):
+        TS(R("QJ%d" % a), R("QA"), -2.0 * a, None, add)
+    TS(R("P45"), R("P7"), 5.0 * NV, None, mul)
+    for n, m in (("C16m", "C16"), ("C8m", "C8"), ("CAL", "CAL")):
+        TT(R(n), ALL(m), R("OFF"), add)
+    TS(R("sI"), R("C8m"), R("QB"), R("CKC"), eq, add)
+    for a in range(4):
+        TS(R("sJ%d" % a), R("CAL"), R("QJ%d" % a if a else "QA"), R("CKR"), eq, add)
+    TS(R("sA"), R("C16m"), R("QA"), R("CKR"), eq, add)
+    TS(R("sB"), R("C16m"), R("QB8"), None, eq)
+    ACT(R("XY0", 0, 8), R("prowI"))
+    ACT(R("XY0", 8, 16), R("pcolI"), F.Copy, bias=float(JO))
+    G8 = R("BB", 0, 128, 16)
+    ACT(R("ST1", 0, 8), G8, scale=R("RA"))
+    ACT(R("ST1", 8, 16), G8, scale=R("R0"))
+    ACT(R("ST2"), G8, scale=R("WX"))
+    ACT(R("IDh"), R("IDf"))
+    ACT(ALL("BBb"), R("BB"))
+    for w, s in enumerate(("SHI", "SLO")):
+        ACT(R("PK%d" % w), R("BB"), scale=R(s))
+    for c in range(8):
+        ACT(R("CD", c, 128, 8), R("BB", 16 * c, 16 * c + 16), scale=-1.0 / 16)
+    for k, s in enumerate((0.0, "S2H", "S2H", "S2L", 0.0, "S2L", "SHI")):
+        ACT(R("sN", 8 * k, 8 * k + 8), G8, scale=R(s) if s else s)
+    blank(1)
     MS(R("C128"), 128.0)
     MS(R("OHW", 0, 64), 0.0)
     MS(R("sO"), 0.0)
     MS(R("cK"), 0.0)
+    MS(R("CLP"), CLIP)
+    MS(R("LFT"), LIFT)
+    MS(R("AVG"), 1.0 / 128)
+    for n, offs in (("OFV", (15.0 / 32, -1.0 / 8)), ("OFS", (-15.0 / 32, -3.0 / 8))):
+        for w in range(2):
+            MS(X(T[n][:, :, w], n, w, w + 1), offs[w])
     for lo, hi in ((8, 32), (40, 48)):
         MS(R("cK", lo, hi), 4113.0 / 128)
-    TS(R("P15i"), R("PI"), 15, None, AND)
-    TC(R("P15"), R("P15i"))
-    TS(R("SLO"), R("P15"), 8.0, None, A.is_lt)
-    TS(R("SHI"), R("P15"), 8.0, None, ge)
-    TS(R("S2L"), R("SLO"), 2.0, None, mul)
-    TS(R("S2H"), R("SHI"), 2.0, None, mul)
-    TS(R("BIA"), R("SLO"), 17.0, None, mul)
-    TS(R("BIB"), R("SHI"), 17.0, None, mul)
-    TS(R("R2B"), R("SLO"), 2.0 * (JO - 2048) - 1, 1.0, mul, add)
-    TS(R("C2B"), R("SHI"), -4097.0, 1.0, mul, add)
-    for n, r in (("CKR", 8.0), ("CKC", 0.0)):
-        TS(R("T1"), R("P15"), r, 512.0, eq, mul)
-        TS(R("T2"), R("P15"), r + 1, 2.125, eq, mul)
-        TT(R(n), R("T1"), R("T2"), add)
-    TS(R("QA"), R("SHI"), -50.0, R("P15"), mul, add)
-    TS(R("QB8"), R("SLO"), -50.0, R("P15"), mul, add)
-    TS(R("QB"), R("QB8"), -8.0, None, add)
-    for a in range(1, 4):
-        TS(R("QJ%d" % a), R("QA"), -2.0 * a, None, add)
-    TS(R("OFF"), R("BB"), -999.0, 999.0, mul, add)
-    for n in ("C16", "C8", "CAL"):
-        TT(R(n), R(n), R("OFF"), add)
-    TS(R("sA"), R("C16"), R("QA"), R("CKR"), eq, add)
-    TS(R("sB"), R("C16"), R("QB8"), None, eq)
-    TS(R("sI"), R("C8"), R("QB"), R("CKC"), eq, add)
-    for a in range(4):
-        TS(R("sJ%d" % a), R("CAL"), R("QJ%d" % a if a else "QA"), R("CKR"), eq, add)
-    TC(R("XY0", 0, 8), R("prowI"))
-    TS(R("XY0", 8, 16), R("pcolI"), float(JO), None, add)
+    for w in range(2):
+        TS(R("MKB", 128 * w, 128 * w + 128), ALL("C16"), R("P15"), 4096.0, A.not_equal, mul)
+    TS(R("DM"), X(T.C16[:, :, NV:16], "C16"), R("P15"), None, eq)
+    TS(R("OHB"), R("C8", 0, 64), R("QB"), None, eq)
+    TS(R("sO", 0, 8), G8, R("T0"), 1.0 / 512, mul, mul)
+    TS(R("sO", 32, 40), G8, R("T8"), 1.0 / 512, mul, mul)
     ACT(R("Z0"), R("Zin"), F.Copy, bias=-128.0, scale=-1.0)
-    TC(R("repU", 0, 8 * NV), R("repI", 0, 8 * NV))
-    TS(R("P7"), R("SHI"), -8.0, R("P15"), mul, add)
-    TS(R("P7"), R("P7"), 5.0 * NV, None, mul)
-    TS(R("FUa"), R("FU", 0, 2 * NPER, 2), R("SLO"), R("P7"), mul, add)
-    TS(R("FUb"), R("FU", 1, 2 * NPER, 2), R("SHI"), None, mul)
-    TT(R("FUa"), R("FUa"), R("FUb"), add)
-    TC(R("perU", 0, NPER), R("FUa"))
-    G8 = R("BB", 0, 128, 16)
-    TC(R("ST1"), G8)
-    for n, c in (("IDb", 1.0), ("IDh", 1.0), ("I15", 2.0 ** 15), ("I16", 1.0 / 16), ("SELI", 2048.0), ("NIDf", -1.0)):
-        TS(R(n), R("IDf"), c, None, mul)
-    TC(ALL("BBb"), R("BB"))
-    for c in range(8):
-        TS(R("CD", c, 128, 8), R("BB", 16 * c, 16 * c + 16), -1.0 / 16, None, mul)
-    for n in ("KV", "KS"):
-        TS(ALL(n), R("IOTA", 0, 640), 0.0, None, mul)
-    TS(R("PK0"), R("BB"), R("SHI"), None, mul)
-    TS(R("PK1"), R("BB"), R("SLO"), None, mul)
-    TS(R("T1"), R("P15"), 0.0, None, eq)
-    TS(R("T2"), R("P15"), 8.0, None, eq)
-    TS(R("sO", 0, 8), G8, R("T1"), None, mul)
-    TS(R("sO", 32, 40), G8, R("T2"), None, mul)
-    for k, s in enumerate((0.0, "S2H", "S2H", "S2L", 0.0, "S2L", "SHI")):
-        TS(R("sN", 8 * k, 8 * k + 8), G8, R(s) if s else s, None, mul)
 
-    def late_constants():
+    def late_constants(part):
+        if part == 0:
+            ACT(R("repU", 0, 8 * NV), R("repI", 0, 8 * NV))
+            TS(R("FUa"), R("FU", 0, 2 * NPER, 2), R("SLO"), R("P45"), mul, add)
+            TS(R("FUb"), R("FU", 1, 2 * NPER, 2), R("SHI"), None, mul)
+            TT(R("FUa"), R("FUa"), R("FUb"), add)
+            TC(R("perU", 0, NPER), R("FUa"))
+            return
         AFF(R("RST"), R("NEG"), [[0, 8], [1, 64]], A.not_equal, 1e9, 0, 0)
         AFF(R("RS16"), R("NEG", 0, 256), [[0, 16], [1, 16]], A.not_equal, 1e9, 0, 0)
         for n1, n2, sc, se in (("SELa", "SELb", 16, 1), ("SELc", "SELd", 1, 8)):
             for h in range(2):
                 AFF(X(T[n1][:, :, h, :], n1, h, h + 1), R("ZEb", 0, 256), [[-sc, 8], [0, 8], [-2 * se, 4]], A.not_equal, 2048.0, -h * se, 1)
+            for h in range(2):
                 AFF(X(T[n2][:, :, h, :], n2, h, h + 1), X(T[n1][:, :, h, :], n1, h, h + 1), [[-sc, 8], [-se, 8], [0, 4]], A.not_equal, 2048.0, -8 * se, 1)
         AFF(R("SELe"), R("ZEb", 0, 128), [[-1, 8], [-8, 16]], A.not_equal, 2048.0, 0, 1)
-        IOTA(ALL("HIO"), [[0, 12], [-16, 2], [1, 32]], 0, 0)
-        IOTA(R("LIO"), [[1, 256]], 0, 0)
-        IOTA(R("NIO"), [[-1, 256]], 0, 0)
-        TC(R("repU", 8 * NV, 8 * NV + 48), R("repI", 8 * NV, 8 * NV + 48))
-        TS(R("DM"), R("DM"), R("P15"), None, eq)
-        TS(ALL("MKB"), R("MKI"), R("P15"), 4096.0, A.not_equal, mul)
+        for n, c in (("IDb", 1.0), ("I15", BIGA), ("I11", BIG0), ("I16", 1.0 / 16), ("SELI", 2048.0), ("NIDf", -1.0)):
+            ACT(R(n), R("IDf"), scale=c)
+        for n in ("KV", "KS"):
+            TS(ALL(n), R("IOTA", 0, 640), 0.0, None, mul)
+        ACT(R("repU", 8 * NV, 8 * NV + 48), R("repI", 8 * NV, 8 * NV + 48))
         TS(R("OHA"), R("OHA"), R("P15"), None, eq)
-        TS(R("OHB"), R("OHB"), R("P15"), None, eq)
+        ACT(R("KJ"), R("KJ"), bias=R("P15"))
         TT(R("OHW", 64, 128), R("OHA"), R("OHB"), add)
-        TS(R("KJ"), R("KJ"), R("P15"), None, add)
-    late_constants()
-    figs = R("MW", 0, W)[1]
-    dma("y", R("B16"), X(T.MW[0::16, 0:W], "MW", 0, W))
-    dma("g", R("WF", ROT, W), (T.fig[:, 0:W - ROT], EXT), figs)
-    dma("g", R("WF", 0, ROT), (T.fig[:, W - ROT:W], EXT), figs)
-    mates(1, "yy", figs)
+        figs = R("MW", 0, W)[1]
+        for h in range(2):
+            dma("y", R("B32", 128 * h, 128 * h + 128), X(T.MW[64 * h:64 * h + 64:16, 0:W], "MW", 0, W))
+        mates(1, "yy", figs)
+        IOTA(ALL("HIO"), [[0, 24], [1, 32]], 0, 0)
+        IOTA(R("LIO"), [[1, 128]], 0, 0)
+        IOTA(R("NIO"), [[-1, 128]], 0, 0)
 
-    def suppress(ns, between):
-        first = 24 - ns
+    def suppress(between):
+        first = 24 - NSE
+        order = list(range(first - NSE - 2)) + [e for k in range(NSE) for e in (first + k, first - NSE - 2 + k)] + [first - 2, first - 1]
 
         def count_in(e):
-            q = 32 * (e % 8 // 2)
-            MM([(X(T.pH[q:q + 32, 0:256], "pH"), R("HOH", 32 * e, 32 * e + 32), X(T.LOH[:, e, :], "LOH", e, e + 1), False, e > 16 and e % 2 == 1)])
-        for k in range(ns):
-            ACT(X(T.AB[:, k, :], "AB", k, k + 1), R("LIO"), F.Abs, bias=R("nlo", first + k, first + k + 1))
-        for k in range(ns):
-            e = first + k
-            ACT(X(T.LOH[:, e, :], "LOH", e, e + 1), X(T.AB[:, k, :], "AB", k, k + 1), F.Relu, bias=R("val", e % 8, e % 8 + 1), scale=-1.0)
+            q, h = 32 * (e % 4), 128 * (e % 8 // 4)
+            last = not any(f % 4 == e % 4 for f in order[order.index(e) + 1:])
+            MM([(X(T.pH[q:q + 32, h:h + 128], "pH"), R("HOH", 32 * e, 32 * e + 32), X(T.LOH[:, e, :], "LOH", e, e + 1), False, last)])
+        for k in range(NSE + 1):
+            if k < NSE:
+                ACT(X(T.AB[:, k, :], "AB", k, k + 1), R("LIO"), F.Abs, bias=R("nlo", first + k, first + k + 1))
+            if k:
+                e = first + k - 1
+                ACT(X(T.LOH[:, e, :], "LOH", e, e + 1), X(T.AB[:, k - 1, :], "AB", k - 1, k), F.Relu, bias=R("val", e % 8, e % 8 + 1), scale=-1.0)
         TT(ALL("HOH"), IND(R("hiI"), R("repU", 8 * NV, 8 * NV + 48)), ALL("HIO"), eq)
-        for e in range(first):
-            TS(X(T.LOH[:, e, :], "LOH", e, e + 1), R("NIO"), R("nlo", e, e + 1), R("val", e % 8, e % 8 + 1), eq, mul)
-            count_in(e)
-        for e in range(first, 24):
+        for e in order:
+            if e < first:
+                TS(X(T.LOH[:, e, :], "LOH", e, e + 1), R("NIO"), R("nlo", e, e + 1), R("val", e % 8, e % 8 + 1), eq, mul)
             count_in(e)
         between()
 
-    for t in range(ROUNDS):
-        xy, z = "XY%d" % t, "Z%d" % t
-        win = "WF" if t else "MW"
+    def row0(src):
+        for h in range(2):
+            dma("y", X(T.MW[64 * h:64 * h + 64:16, 0:W], "MW", 0, W), R(src, 128 * h, 128 * h + 128), skip=h == 1)
+
+    def mates_names(t):
+        xy = "XY%d" % t
         LX, LY = R(xy, 0, 8), R(xy, 8, 16)
         XM = R("XM%d" % (t % 2))
         TS(R("C2"), IND(XM, LY), R("S2H"), R("C2B"), mul, add)
         TS(R("R2"), IND(XM, LX), R("S2L"), R("R2B"), mul, add)
-        ACT(R("U"), IND(R("IOTA"), LX), F.Identity, bias=R("BIA"), scale=R("S2L"))
-        ACT(R("WN"), IND(R("IOTA"), LY), F.Identity, bias=R("BIB"), scale=R("S2H"))
-        TS(R("mo"), R(xy), -2048.0, None, add)
+        ACT(R("U"), IND(R("IOTA"), LX), bias=R("BIA"), scale=R("S2L"))
+        ACT(R("WN"), IND(R("IOTA"), LY), bias=R("BIB"), scale=R("S2H"))
         ACC(R("pM", 256, 384), [(R("sI"), R("C2"))])
-        ACT(R("IPs"), R("pM", 256, 384), F.Copy)
-        JP = [R("pJ", 128 * a, 128 * a + 128) for a in range(4)]
-        MM([(JP[a], R("sJ%d" % a), R("R2"), True, True) for a in range(4)])
-        ACC(R("pM", 128, 256), [(R("IDf"), R("U")), (R("IDf"), R("WN"))])
-        ACT(R("OT"), R("pM", 128, 256), F.Copy)
+        MM([(R("pJ", 128 * a, 128 * a + 128), R("sJ%d" % a), R("R2"), True, True) for a in range(4)])
+        ACT(R("IPs"), R("pM", 256, 384))
+
+    mates_names(0)
+    for t in range(ROUNDS):
+        xy, z = "XY%d" % t, "Z%d" % t
+        win = "MW"
+        ACC(R("pM", 128, 256), [(R("IDh"), R("U")), (R("IDh"), R("WN"))])
         ACC(R("pM", 0, 128), [(R("sA"), R("R2")), (R("sB"), R("C2"))])
+        ACT(R("OT"), R("pM", 128, 256), F.Copy, bias=4113.0)
         for a in range(4):
-            TT(X(T.Fq[:, :, :, 1 + a], "Fq", 1 + a, 2 + a), JP[a], R("IPs"), mul)
+            TT(X(T.Fq[:, :, :, 1 + a], "Fq", 1 + a, 2 + a), R("pJ", 128 * a, 128 * a + 128), R("IPs"), mul)
         TT(X(T.Fq[:, :, :, 0], "Fq", 0, 1), R("pM", 0, 128), R("OT"), mul)
-        ACT(R("NZf"), R(z), F.Copy, bias=128.0 + EPS)
-        ACT(R("Zr"), IND(R(z), R("repU", 0, 8 * NV)), F.Copy, bias=-128.0 - EPS, scale=-1.0)
-        ACT(R("MT"), R("pM", 0, 128), F.Copy, bias=-2056.5, scale=0.5)
+        if t == 0:
+            late_constants(0)
+        ACT(R("Zr"), IND(R(z), R("repU", 0, 8 * NV)), bias=R("EZ"), scale=-1.0)
+        ACT(R("NZf"), R(z), bias=R("EN"))
         TS(ALL("FiS"), X(T.Fq[:, :, NV:16, :], "Fq"), 5, W - 1, SHR, AND)
         TS(R("FiV"), X(T.Fq[:, :, 0:NV, :], "Fq"), 5, W - 1, SHR, AND)
         TC(X(T.FS[:, :, :, 0:5], "FS"), ALL("FiS"))
         TC(R("FV"), IND(R("FiV"), R("perU", 0, NPER)))
+        ACT(R("MT"), R("pM", 0, 128), F.Copy, bias=-2056.5, scale=0.5)
+        ACT(R("mo"), R(xy), F.Copy, bias=-2048.0)
+        if t == 0:
+            late_constants(1)
         bs = X(T.BBb[:, :, NV:16], "BBb")
         ACC(R("pM", 0, 8 * NS), [(R(z), bs), (R("C128"), bs)])
         TT(ALL("RZ"), R("pM", 0, 8 * NS), R("DM"), mul)
         ACC(R("pM", 0, 56), [(R("OT"), R("sO")), (R("ONE"), R("cK"))], True, False)
-        if t == 0:
-            TC(R("SEL0"), ALL("SELb"))
-            TC(R("SEL1"), ALL("SELd"))
-            TC(R("SELJ"), R("SELe"))
-            TS(R("BP"), R("B16"), SIG, None, add)
-        ACC(R("pH", 0, 256), [(R("IDf"), R("W0")) if t else (R("IDb"), R("B16"))], True, False)
         ACC(ALL("pE"), [(R("IDb"), R("RHO"))], True, False)
-        MM([(R("pJ", 0, 256), R("IDh"), R("MKB"), True, False), (R("pJ", 256, 272), R("IDh"), R("mo"), False, False)])
+        MM([(R("pJ", 0, 256), R("IDh"), R("MKB"), True, False), (R("pJ", 256, 272), R("IDh"), R("mo"), False, False),
+            (R("pJ", 272, 280), R("IDf"), R("KJ"), False, False)])
 
         def rectangles(kp, xs, sel0, sel):
             reg = (lambda x: (x, x + 1)) if kp == "KV" else (lambda x: (0, NS))
@@ -442,129 +468,148 @@ def rank_program(g, core, T, topo):
 
         def step(s):
             k = s[2:]
+            if s[1] == "v":
+                x, p0, p1 = (int(k), 0, NV) if k < "4" else (4, 0, CUT) if k == "4" else (4, CUT, NV)
+                ev = [X(T.EV[:, x, 128 * p:128 * p + 128], "EV", NV * x + p, NV * x + p + 1) for p in range(NV)]
             if s[:2] == "gv":
-                x = int(k)
-                TT(X(T.EV[:, x], "EV", x, x + 1), IND(R(win, 0, W), R("FV", 8 * NV * x, 8 * NV * (x + 1))), R("Zr"), A.max)
+                TT(X(T.EV[:, x, 128 * p0:128 * p1], "EV", NV * x + p0, NV * x + p1),
+                   IND(R(win, 0, W), R("FV", 8 * (NV * x + p0), 8 * (NV * x + p1))), R("Zr", 128 * p0, 128 * p1), A.max)
             elif s[:2] == "gs":
                 q = int(k)
                 for c in range(8):
                     j = 16 * c + NV + q
                     ACT(X(T.ES[:, q, c:640:8], "ES", 8 * q + c, 8 * q + c + 1), IND(R(win, 0, W), X(T.FS[:, c, q, 0:5], "FS")), F.Relu, bias=R("NZf", j, j + 1))
             elif s[:2] == "mv":
-                x = int(k)
                 b, lo, hi = [c for n, c in CHUNKS.items() if n[0] == "V" and c[1] <= x < c[2]][0]
-                MM([(X(T[b][:, x - lo, 0, :, p], b), X(T.EV[:, x, 128 * p:128 * p + 128], "EV", x, x + 1), R("ST1"), x == lo and p == 0,
-                     x == hi - 1 and p == NV - 1) for p in range(NV)])
+                if x == lo and p0 == 0:
+                    ACC(X(T[b][:, 0:hi - lo, :, :, 0:NV], b), [(R("AVG"), X(T.OFV[:, 0:hi - lo], "OFV"))], True, False)
+                MM([(X(T[b][:, x - lo, :, :, p], b), ev[p], R("ST1"), False, x == hi - 1 and p == NV - 1) for p in range(p0, p1)])
             elif s[:2] == "ms":
                 q = int(k)
                 b, lo, hi = [c for n, c in CHUNKS.items() if n[0] == "S" and c[1] <= q < c[2]][0]
-                MM([(X(T[b][:, x, 0, :, q - lo], b), X(T.ES[:, q, 128 * x:128 * x + 128], "ES", 8 * q, 8 * q + 8), R("ST1"), q == lo and x == 0,
+                if q == lo:
+                    ACC(X(T[b][:, 0:5, :, :, 0:hi - lo], b), [(R("AVG"), X(T.OFS[:, :, :, :, 0:hi - lo], "OFS"))], True, False)
+                MM([(X(T[b][:, x, :, :, q - lo], b), X(T.ES[:, q, 128 * x:128 * x + 128], "ES", 8 * q, 8 * q + 8), R("ST1"), False,
                      q == hi - 1 and x == 4) for x in range(5)])
             else:
                 b, lo, hi = CHUNKS[s[1:]]
                 if s[1] == "V":
-                    part = [X(T[b][:, 0:hi - lo, w, :, 0:NV], b) for w in range(2)]
-                    rb = R("RB", 8 * NV * lo, 8 * NV * hi)
+                    nx, n = hi - lo, NV
                     kp = X(T.KV[:, lo:hi, :, 0:NV], "KV", lo, hi)
+                    again = [(X(T[b][:, x - lo, 0, :, p], b), X(T.EV[:, x, 128 * p:128 * p + 128], "EV", NV * x + p, NV * x + p + 1), R("ST2"))
+                             for x in range(lo, hi) for p in range(NV)]
                 else:
-                    part = [X(T[b][:, 0:5, w, :, 0:hi - lo], b) for w in range(2)]
-                    rb = R("RB", 40 * (NV + lo), 40 * (NV + hi))
+                    nx, n = 5, hi - lo
                     kp = X(T.KS[:, :, :, NV + lo:NV + hi], "KS", lo, hi)
+                    again = [(X(T[b][:, x, 0, :, q - lo], b), X(T.ES[:, q, 128 * x:128 * x + 128], "ES", 8 * q, 8 * q + 8), R("ST2"))
+                             for x in range(5) for q in range(lo, hi)]
+                key = X(T[b][:, 0:nx, 0, :, 0:n], b)
                 if s[0] == "r":
-                    TS(rb, part[0], MAGIC, -MAGIC, add, add)
-                elif s[0] == "d":
-                    db = R("DB", *rb[1][0][1:])
-                    TT(db, rb, part[0], A.subtract)
-                    more = [(X(T[b][:, x, 1, :, 0:hi - lo], b), R("CD"), X(T.RZ[:, :, lo:hi], "RZ"), False, False) for x in range(5)] if s[1] == "S" else []
-                    MM([(part[1], R("I16"), rb, True, False)] + more + [(part[1], R("I15"), db, False, True)])
+                    rn = "R" + s[1:]
+                    TS(ALL(rn), X(T[b][:, 0:nx, :, :, 0:n], b), MAGIC, -MAGIC, add, add)
+                    r = [X(T[rn][:, :, w, :], rn) for w in range(2)]
+                    run = [(key, R("I15"), r[0])] + again + [(key, R("I11"), r[1]), (key, R("I16"), r[0]), (key, R("I16"), r[1])]
+                    if s[1] == "S":
+                        run += [(X(T[b][:, x, 0, :, 0:n], b), R("CD"), X(T.RZ[:, :, lo:hi], "RZ")) for x in range(5)]
+                    MM([it + (k == 0, k == len(run) - 1) for k, it in enumerate(run)])
                 elif s[0] == "e":
                     rectangles("KV", range(lo, hi), "SEL0", "SELI")
+                elif s[0] == "K":
+                    ACT(kp, key, F.Relu, bias=R("LFT") if s[1] == "S" else 0.0)
                 else:
-                    TS(kp, part[1], 8192.0 if s[1] == "S" else 0.0, 0.0, add, A.max)
+                    TS(kp, key, LIFT if s[1] == "S" else 0.0, 0.0, add, A.max)
+            if s == "gs2":
+                if t == 0:
+                    ACT(R("SEL0"), ALL("SELb"))
+                    ACT(R("SEL1"), ALL("SELd"))
+                    ACT(R("SELJ"), R("SELe"))
+                    ACT(R("BP"), R("B32"), F.Copy, bias=SIG)
+            if s == "mv1":
+                ACC(R("pH", 0, 256), [(R("IDb"), R("W0" if t else "B32"))], True, False)
         for s in ORDER:
             step(s)
-        ACT(R(win, W, W + 128), R(z), F.Copy, bias=-256.0, scale=-2.0)
+        ACT(R(win, W, W + 128), R(z), F.Copy, bias=-255.0, scale=-2.0)
         rectangles("KS", range(5), "SEL1", "SELJ")
         SCAN(R("M1"), R("RST"), ALL("pE"), 0.0, A.max, A.min)
         mk = R("mki", 8 * t, 8 * t + 8)
         TS(mk, R("M1", 63, 512, 64), CLIP, -CLIP, A.min, add)
-        TS(R("mkf"), R("M1", 63, 512, 64), CLIP, -CLIP, A.min, add)
+        ACT(R("nm"), R("M1", 63, 512, 64), F.Relu, bias=R("CLP"), scale=-1.0)
         TS(R("rhoI"), mk, 127, None, AND)
-        MM([(R("pJ", 256 + 8 * w, 264 + 8 * w), R("NIDf"), R("mkf"), False, False) for w in range(2)])
+        MM([(R("pJ", 256 + 8 * w, 264 + 8 * w), R("NIDf" if w == 2 else "IDf"), R("nm"), False, False) for w in range(3)])
         TC(R("rhoU"), R("rhoI"))
         TT(R("NM"), IND(R("OHW"), R("rhoU")), R("MT"), mul)
         MM([(R("pJ", 128 * w, 128 * w + 128), R("PK%d" % w), R("NM"), False, w == 1) for w in range(2)])
         ACC(R("pM", 0, 56), [(R("NM"), R("sN"))], False)
-        TT(R("kj"), R("KJ"), R("mkf"), add)
         NEW = R("NEW")
+        last = t == ROUNDS - 1
+        if last:
+            TS(R("cI"), R("mki"), 7, None, SHR)
+        ACT(R("Asb"), R("pM", 0, 24))
+        ACT(R("val"), R("pM", 48, 56), F.Sign, scale=-1.0)
 
         def pass_names():
             SCAN(R("NSC"), R("RS16"), R("pJ", 0, 256), 0.0, A.max, A.min)
             TT(NEW, R("pJ", 256, 272), R("NSC", 15, 256, 16), A.min)
-            TS(R("XYs"), NEW, 2048.0, None, add)
+            ACT(R("XYs"), NEW, F.Copy, bias=2048.0)
             remote(t, "n", "XY%d" % (t + 1), R("XYs"))
+            ACT(R("UW"), NEW, F.Copy, bias=4113.0, scale=2.0)
 
         def corners():
-            TC(R("Asb"), R("pM", 0, 24))
-            TS(R("val"), R("pM", 48, 56), 0.0, SIG, A.not_equal, mul)
             TT(R("QC"), R("pM", 24, 48), R("Asb"), mul)
-            TS(R("loI"), R("QC"), 5, 255, SHR, AND)
-            TS(R("hiI"), R("QC"), 13, 15, SHR, AND)
+            TS(R("loI"), R("QC"), 5, 127, SHR, AND)
+            TS(R("hiI"), R("QC"), 12, 31, SHR, AND)
             TS(R("nlo"), R("loI"), -1.0, None, mul)
 
         def pass_needs():
-            TS(R("UW"), NEW, 2.0, 4113.0, mul, add)
             TT(R("q3"), R("UW", 0, 8), R("UW", 8, 16), mul)
             TS(R("FC"), R("q3"), 5, W - 1, SHR, AND)
-            TT(R("far"), R("FC"), R("kj"), A.max)
+            TT(R("far"), R("pJ", 272, 280), R("FC"), A.max)
             TC(R("farU"), R("far"))
-            ACT(R("Zs"), IND(R(win), R("farU")), F.Copy, bias=-127.8, scale=-0.5)
+            ACT(R("Zs"), IND(R(win), R("farU")), F.Copy, bias=-127.6, scale=-0.5)
             remote(t, "z", "Z%d" % (t + 1), R("Zs"))
-        if t < ROUNDS - 1:
+        if not last:
             pass_names()
+            corners()
             pass_needs()
-            corners()
-            suppress(NSE[t], lambda: None)
+            suppress(lambda: None)
             TT(R("W0"), R("pH", 0, 256), R("BP"), A.min)
-            dma("y", X(T.WF[0::16, 0:W], "WF", 0, W), R("W0"))
+            row0("W0")
+            mates_names(t + 1)
             if t == 0:
-                IOTA(ALL("ONEb"), [[0, 2048]], 1, 0)
-                AFF(ALL("EXPM"), ALL("ONEb"), [[-1, 16], [-16, 8], [0, 16]], eq, 0.0, 0, 1)
+                IOTA(ALL("EXPM"), [[0, 2048]], 1, 0)
+                AFF(ALL("EXPM"), ALL("EXPM"), [[-1, 32], [-32, 4], [0, 16]], eq, 0.0, 0, 1)
         else:
+            row0("B32")
             corners()
-            suppress(NSE[t], pass_names)
-            TT(R("FL"), R("pH", 0, 256), R("B16"), A.is_gt)
+            suppress(pass_names)
+            TT(R("FL"), R("pH", 0, 256), R("B32"), A.is_gt)
+            TS(R("cn"), R("cI"), 0.0, -6146.0, eq, mul)
             TS(R("SG"), R("FL"), -2.0, 1.0, mul, add)
             pass_needs()
 
     e = ROUNDS
     banks = ("pA", "pB", "pC", "pD")
-    half = {"pA": 1, "pB": 1, "pC": 4, "pD": 4}
     for k in range(8):
         nm = banks[k % 4]
-        MM([(X(T[nm][:, half[nm] * x:half[nm] * (x + 1)], nm), X(T.EXPM[:, 2 * k + x, :], "EXPM"), R("SG"), True, True) for x in range(2)])
+        MM([(X(T[nm][64 * h:64 * h + 64, x // 2, x % 2] if k % 4 < 2 else T[nm][64 * h:64 * h + 64, 2 * x:2 * x + 2], nm),
+             X(T.EXPM[:, 4 * k + x, :], "EXPM"), R("SG", 128 * h, 128 * h + 128), True, True) for x in range(4) for h in range(2)])
         TT(R("YF", 512 * k, 512 * k + 512), R("MW", 512 * k, 512 * k + 512), ALL(nm), mul)
         if k == 0:
             dma("s", (T.yf[:, 0:512 - ROT], EXT), R("YF", ROT, 512))
             dma("y", (T.yf[:, W - ROT:W], EXT), R("YF", 0, ROT))
-            TS(R("cI"), R("mki"), 64.0, None, add)
-            TS(R("G"), R("mki"), 0.0, None, A.is_lt)
-            TS(R("cI"), R("cI"), 7, None, SHR)
-            TS(R("cf"), R("cI"), 6145.0, None, add)
-            TT(R("cst"), R("cf"), R("G"), mul)
-            ACC(X(T.pM[0:32, 0:128], "pM"), [(R("cst"), R("IDf"))])
-            ACT(X(T.CT[0:32, :], "CT"), X(T.pM[0:32, 0:128], "pM"), F.Copy, bias=-1.0)
+        else:
+            dma(("s", "y")[k % 2], (T.yf[:, 512 * k - ROT:512 * (k + 1) - ROT], EXT), R("YF", 512 * k, 512 * (k + 1)))
+        if k == 3:
+            ACT(R("cf"), R("cI"))
+            ACC(X(T.pM[0:32, 0:128], "pM"), [(R("cf"), R("IDf")), (R("cn"), R("IDf"))])
+            ACT(X(T.CT[0:32, :], "CT"), X(T.pM[0:32, 0:128], "pM"), F.Copy, bias=6145.0)
             for x in range(8):
-                dma(("s", "y")[x % 2], (T.yc[x:x + 1, :], EXT), X(T.CT[0:32, 16 * x:16 * x + 16], "CT"))
-        elif k % 2 == 0:
-            dma(("s", "y")[k // 2 % 2], (T.yf[:, 512 * (k - 1) - ROT:512 * (k + 1) - ROT], EXT), R("YF", 512 * (k - 1), 512 * (k + 1)))
-        if k == 5:
-            TC(R("YP", 0, 8), R("XY%d" % e, 0, 8))
-            TS(R("YP", 8, 16), R("XY%d" % e, 8, 16), -float(JO), None, add)
-            dma("y", (T.yp[:], EXT), R("YP"))
-    dma("s", (T.yf[:, 3584 - ROT:W - ROT], EXT), R("YF", 3584, W))
+                dma("s", (T.yc[x:x + 1, :], EXT), X(T.CT[0:32, 16 * x:16 * x + 16], "CT"))
+    ACT(R("YP", 0, 8), R("XY%d" % e, 0, 8))
+    ACT(R("YP", 8, 16), R("XY%d" % e, 8, 16), F.Copy, bias=-float(JO))
+    dma("s", (T.yp[:], EXT), R("YP"))
     ACT(R("YZ"), R("Z%d" % e), F.Copy, bias=-128.0, scale=-1.0)
-    dma("y", (T.yz[:], EXT), R("YZ"))
+    dma("s", (T.yz[:], EXT), R("YZ"))
     for s, n in sorted(count.items()):
         if known["g"].get(s, 0) < n:
             g.wait_ge(T.sem[s], n)

@@ -12,11 +12,16 @@ ROUNDS = 4
 NV = 9
 NS = 16 - NV
 NPER = (40 * NV + 15) // 16
-NSE = 7
-CUT = 5
+NSE = [7, 7, 7, 8]
+OUTS = (1, 3, 5, 7, 0)
+HALF = 9
+PIECES = [(0, 0, 9), (1, 0, 9), (2, 0, 9), (3, 0, 9), (4, 0, 5), (4, 5, 9)]
 CHUNKS = {"VA": ("pA", 0, 2), "VB": ("pB", 2, 4), "VC": ("pA", 4, 5), "SA": ("pC", 0, 4), "SB": ("pD", 4, 6), "SC": ("pC", 6, 7)}
-ORDER = ("gs0 gs1 gs2 ms0 gv0 mv0 ms1 gv1 mv1 ms2 gv2 gs3 rVA mv2 ms3 gv3 gs4 KVA rSA eVA mv3 ms4 gv4 gs5 KSA rVB mv4 gv5 ms5 mv5 "
-         "gs6 rSB rVC kVB eVB ms6 kSB rSC kVC eVC kSC").split()
+KEYS = {"VA": "pJ", "SA": "pH", "VB": "pM", "SB": "pH", "VC": "pJ", "SC": "pM"}
+ORDER = ("gs0 gs1 gv0 gs2 gv1 ms0 mv0 ms1 aVA ms2 gv2 gs3 mv1 rVA KVA eVA ms3 gv3 aSA rSA gs4 mv2 gs5 kSA aSB mv3 ms4 aVB gs6 rVB gv4 gv5 "
+         "mv4 kVB ms5 rSB mv5 aVC ms6 KSB rVC eVB kVC aSC rSC eVC kSC").split()
+GATHER, WAKE, HOLD = 1.3, 60.0, 2.0
+STEP = 100.0
 
 SB = {}
 POOL = {}
@@ -48,11 +53,12 @@ _small("sO cK", 56)
 _small("DM", 8 * NS)
 _small("FU", 2 * NPER)
 _small("FUa FUb", NPER)
-_small("P15 SLO SHI S2L S2H R2B C2B BIA BIB CKR CKC T0 T1 T8 T9 QA QB QB8 QJ1 QJ2 QJ3 P7 P45 CLP LFT R0 RA WX EN EZ", 1)
+_small("P15 SLO SHI S2L S2H R2B C2B BIA BIB CKR CKC T0 T1 T8 T9 QA QB QB8 QJ1 QJ2 QJ3 P7 P16 P45 LFT R0 RA WX EN EZ", 1)
 _sb("poolF", [USED["poolF"]])
 _sb("poolI", [USED["poolI"]], "int32")
 _sb("prowI pcolI", [8], "int32")
-_sb("rhoU farU", [8], "uint16")
+_sb("smallU", [16], "uint16")
+POOL["rhoU"], POOL["farU"] = ("smallU", 0, 8), ("smallU", 8, 8)
 for _t in range(ROUNDS + 1):
     _sb("XY%d" % _t, [16], "uint16")
     _sb("Z%d" % _t, [128], "bfloat16")
@@ -66,14 +72,14 @@ _sb("ST2", [8], "float16")
 _sb("BBb", [8, 16], "bfloat16")
 _sb("XM0 XM1", [NI], "int32")
 _sb("MW", [W + 128], "bfloat16")
-_sb("YF", [W], "bfloat16")
+_sb("YF", [W + ROT], "bfloat16")
 _sb("IOTA", [NI])
 _sb("C16", [8, 16])
 _sb("ONE BB OFF C16m C8 C8m CAL IDf NIDf OHW OT IPs MT NZf CT", [128])
 _sb("sJ0 sJ1 sJ2 sJ3 sA sB sI PK0 PK1 IDh I15 I11 I16 SELI SELJ CD R2 C2 NM U WN", [128], "float16")
 _sb("sN", [56], "float16")
 _sb("mo", [16], "float16")
-_sb("RZ", [8, NS], "float16")
+_sb("RZ", [5, 8, NS], "float16")
 _sb("SEL0 SEL1", [512], "float16")
 _sb("MKB", [256], "float16")
 for _n, (_b, _lo, _hi) in CHUNKS.items():
@@ -83,13 +89,14 @@ _sb("RHO ZEb", [512], "bfloat16")
 _sb("SELa SELb SELc SELd", [8, 2, 32], "bfloat16")
 _sb("SELe LIO NIO", [128], "bfloat16")
 _sb("EXPM", [32, 64], "bfloat16")
-_sb("NEG RST M1", [512])
+_sb("NEG RST", [512])
+_sb("M1", [512], "int32")
 _sb("RS16 NSC", [256])
 _sb("OHA OHB", [64])
 _sb("SG FL B32 BP W0", [256], "bfloat16")
 _sb("HIO HOH", [768], "bfloat16")
 _sb("LOH", [24, 128], "bfloat16")
-_sb("AB", [NSE, 128], "bfloat16")
+_sb("AB", [max(NSE), 128], "bfloat16")
 _sb("Fq", [8, 16, 5], "int32")
 _sb("FiS", [8, NS, 5], "int32")
 _sb("FiV", [40 * NV], "int32")
@@ -161,22 +168,108 @@ def rank_program(g, core, T, topo):
                 out += r[1]
         return out
 
-    def emit(q, call, reads, writes):
-        sem = "q" + q
-        need_waits(q, reads, writes, False)
-        inst = call()
-        count[sem] = count.get(sem, 0) + 1
-        inst.then_inc(T.sem[sem], 1)
-        note(q, sem, count[sem], reads, writes, dict(known[q]))
+    calls = []
 
-    def dma(q, out, in_, after=(), skip=False):
-        ndma[0] += 0 if skip else 1
-        sem = "d%d" % (ndma[0] - 1)
-        if not skip:
-            need_waits(q, in_[1] + list(after), out[1], True)
-        queues[q].dma_start(out[0], in_[0]).then_inc(T.sem[sem], 16)
-        count[sem] = count.get(sem, 0) + 16
-        note(sem, sem, count[sem], in_[1], out[1], dict(known[q]))
+    def size(ap):
+        n = 1
+        for k in list(ap.shape)[1:]:
+            n *= k
+        return n
+
+    def narrow(ref):
+        return SB[ref[1][0][0]][2] in ("bfloat16", "float16", "uint16")
+
+    def emit(q, call, reads, writes, ns):
+        def issue():
+            sem = "q" + q
+            need_waits(q, reads, writes, False)
+            inst = call()
+            count[sem] = count.get(sem, 0) + 1
+            inst.then_inc(T.sem[sem], 1)
+            note(q, sem, count[sem], reads, writes, dict(known[q]))
+        calls.append((q, issue, reads, writes, ns, 0.0, 60.0 if q == "t" else 0.0))
+
+    def dma(q, out, in_, after=(), more=()):
+        pairs = [(out, in_)] + list(more)
+        reads, writes = regs_of(*[p[1] for p in pairs]), regs_of(*[p[0] for p in pairs])
+
+        def issue():
+            sem = "d%d" % ndma[0]
+            ndma[0] += 1
+            need_waits(q, reads + list(after), writes, True)
+            for o, i in pairs:
+                queues[q].dma_start(o[0], i[0]).then_inc(T.sem[sem], 16)
+            count[sem] = 16 * len(pairs)
+            note(sem, sem, count[sem], reads, writes, dict(known[q]))
+        side = out if out[1] else in_
+        nbytes = len(pairs) * side[0].shape[0] * size(side[0]) * (2 if narrow(side) else 4)
+        calls.append((q, issue, reads + list(after), writes, 60.0 * len(pairs), 60.0 + nbytes / 190.0, 1700.0))
+
+    def cost_v(out, *ins):
+        n = size(out[0])
+        if len(ins) and len(ins[0]) == 3:
+            return 50 + GATHER * n
+        r = 0.5 if all(narrow(a) for a in (out,) + ins) else 1.0
+        if len(ins) == 2 and not any(a[1][0][0] in PSUMS for a in ins):
+            r *= 2
+        return 45 + 0.83 * max(64, r * n)
+
+    def arrange():
+        seen, before, after = {}, [], [[] for _ in calls]
+        for k, (q, _, reads, writes, _, _, _) in enumerate(calls):
+            deps = set()
+            for regs, w in ((reads, False), (writes, True)):
+                for (n, lo, hi) in regs:
+                    for (plo, phi, pw, pq, j) in seen.get(n, ()):
+                        if (pw or w or pq != q) if n in PSUMS else (phi > lo and plo < hi and (pw or w)):
+                            deps.add(j)
+            for regs, w in ((reads, False), (writes, True)):
+                for (n, lo, hi) in regs:
+                    lst = seen.setdefault(n, [])
+                    if w:
+                        lst[:] = [p for p in lst if not (n in PSUMS or (lo <= p[0] and p[1] <= hi))]
+                    lst.append((lo, hi, w, q, k))
+            before.append(deps)
+            for j in deps:
+                after[j].append(k)
+        way = [-STEP * k for k in range(len(calls))]
+
+        def sweep(before, after, way):
+            left = [len(d) for d in before]
+            ready = {k: 0.0 for k in range(len(calls)) if not left[k]}
+            free = {q: 0.0 for q in queues}
+            engines, order, soon, end = 0.0, [], {}, [0.0] * len(calls)
+            while ready:
+                start = {k: max(t, free[calls[k][0]]) for k, t in ready.items()}
+                first = min(start, key=lambda k: (start[k], -way[k], k))
+                q, t0 = calls[first][0], start[first]
+                mine = [k for k in ready if calls[k][0] == q]
+                k = max(mine, key=lambda k: (way[k] - HOLD * (start[k] - t0), -k))
+                if len(order) < loads:
+                    k = len(order)
+                    q = calls[k][0]
+                elif start[k] > t0:
+                    fits = [m for m in mine if start[m] == t0 and t0 + calls[m][4] <= start[k]]
+                    if not fits:
+                        free[q] = min(start[k], t0 + WAKE)
+                        continue
+                    k = max(fits, key=lambda m: (way[m], -m))
+                free[q] = done = start[k] + calls[k][4]
+                if calls[k][5]:
+                    engines = max(done + 0.7 * calls[k][6], engines) + calls[k][5]
+                    done = engines + 0.3 * calls[k][6]
+                else:
+                    done += calls[k][6]
+                del ready[k]
+                order.append(k)
+                end[k] = done
+                for j in after[k]:
+                    left[j] -= 1
+                    soon[j] = max(soon.get(j, 0.0), done + WAKE)
+                    if not left[j]:
+                        ready[j] = soon[j]
+            return order, end
+        return sweep(before, after, way)[0]
 
     def R(n, lo=0, hi=None, step=1):
         if n in POOL:
@@ -194,31 +287,33 @@ def rank_program(g, core, T, topo):
         return X(T[n][:], n)
 
     def IND(win, offs):
-        return (win[0].indirect(offs[0]), win[1] + offs[1])
+        return (win[0].indirect(offs[0]), win[1] + offs[1], True)
 
     def val(x):
         return x[0] if isinstance(x, tuple) else x
 
     def TT(out, a, b, op):
-        emit("v", lambda: g.vector.tensor_tensor(out[0], a[0], b[0], op), regs_of(a, b), out[1])
+        emit("v", lambda: g.vector.tensor_tensor(out[0], a[0], b[0], op), regs_of(a, b), out[1], cost_v(out, a, b))
 
     def TS(out, a, s1, s2, op0, op1=None):
         if op1 is None:
-            emit("v", lambda: g.vector.tensor_scalar(out[0], a[0], val(s1), None, op0), regs_of(a, s1), out[1])
+            emit("v", lambda: g.vector.tensor_scalar(out[0], a[0], val(s1), None, op0), regs_of(a, s1), out[1], cost_v(out, a))
         else:
-            emit("v", lambda: g.vector.tensor_scalar(out[0], a[0], val(s1), val(s2), op0, op1), regs_of(a, s1, s2), out[1])
+            emit("v", lambda: g.vector.tensor_scalar(out[0], a[0], val(s1), val(s2), op0, op1), regs_of(a, s1, s2), out[1], cost_v(out, a))
 
     def TC(out, a):
-        emit("v", lambda: g.vector.tensor_copy(out[0], a[0]), regs_of(a), out[1])
+        emit("v", lambda: g.vector.tensor_copy(out[0], a[0]), regs_of(a), out[1], cost_v(out, a))
 
     def MS(out, c):
-        emit("v", lambda: g.vector.memset(out[0], c), [], out[1])
+        emit("v", lambda: g.vector.memset(out[0], c), [], out[1], cost_v(out))
 
     def SCAN(out, d0, d1, init, op0, op1):
-        emit("v", lambda: g.vector.tensor_tensor_scan(out[0], d0[0], d1[0], init, op0, op1), regs_of(d0, d1), out[1])
+        emit("v", lambda: g.vector.tensor_tensor_scan(out[0], d0[0], d1[0], init, op0, op1), regs_of(d0, d1), out[1], cost_v(out, d0))
 
     def ACT(out, a, func=F.Identity, bias=0.0, scale=1.0):
-        emit("s", lambda: g.scalar.activation(out[0], a[0], func, bias=val(bias), scale=val(scale)), regs_of(a, bias, scale), out[1])
+        n = size(out[0])
+        emit("s", lambda: g.scalar.activation(out[0], a[0], func, bias=val(bias), scale=val(scale)), regs_of(a, bias, scale), out[1],
+             65 + (GATHER * n if len(a) == 3 else 0.83 * max(64, n)))
 
     def MM(items):
         def go():
@@ -226,32 +321,37 @@ def rank_program(g, core, T, topo):
             for (o, l, r, st, sp) in items:
                 inst = g.tensor.matmul(o[0], l[0], r[0], st, sp)
             return inst
-        emit("t", go, regs_of(*[r for it in items for r in it[1:3]]), regs_of(*[it[0] for it in items]))
+        emit("t", go, regs_of(*[r for it in items for r in it[1:3]]), regs_of(*[it[0] for it in items]),
+             sum(0.42 * (1 if narrow(it[1]) else 4) * max(min(64, size(it[1][0])), size(it[2][0])) for it in items))
 
     def ACC(out, pairs, start=True, stop=True):
         MM([(out, l, r, start and k == 0, stop and k == len(pairs) - 1) for k, (l, r) in enumerate(pairs)])
 
-    def IOTA(out, pattern, base, cm, f=True):
+    def IOTA(out, pattern, base, cm, f=True, after=()):
         if f:
-            emit("g", lambda: g.iota(out[0], pattern, base, cm, allow_small_or_imprecise_dtypes=True), [], out[1])
+            emit("g", lambda: g.iota(out[0], pattern, base, cm, allow_small_or_imprecise_dtypes=True), list(after), out[1], 130 + 1.66 * size(out[0]))
         else:
-            emit("g", lambda: g.iota(out[0], pattern, base, cm), [], out[1])
+            emit("g", lambda: g.iota(out[0], pattern, base, cm), [], out[1], 130 + 1.66 * size(out[0]))
 
     def AFF(out, in_, pattern, op, fill, base, cm):
-        emit("g", lambda: g.affine_select(out[0], in_[0], pattern, op, fill, base, cm), in_[1], out[1])
+        emit("g", lambda: g.affine_select(out[0], in_[0], pattern, op, fill, base, cm), in_[1], out[1], 170 + 1.66 * size(out[0]))
 
     def remote(t, kind, dst, src):
         sh = 1 + t % 3
         to = T.cores[(rank + sh) % 4]
         rid, pid, _ = topo.addr(to)
         ls, rs = "l%s%d" % (kind, t), "r%s%d" % (kind, t)
-        need_waits("g", src[1], [], True)
-        g.remote_dma(T[dst][:], src[0], T.sem[rs], T.sem[ls], pid, rid, topo.mask(core, to))
-        count[ls] = len(topo.engines(core, to))
-        note(ls, ls, count[ls], src[1], [], dict(known["g"]))
         frm = T.cores[(rank - sh) % 4]
-        count[rs] = len(topo.engines(frm, core))
-        note(rs, rs, count[rs], [], [(dst, 0, SB[dst][1][1])], {})
+        lands = [(dst, 0, SB[dst][1][1])]
+
+        def issue():
+            need_waits("g", src[1], [], True)
+            g.remote_dma(T[dst][:], src[0], T.sem[rs], T.sem[ls], pid, rid, topo.mask(core, to))
+            count[ls] = len(topo.engines(core, to))
+            note(ls, ls, count[ls], src[1], [], dict(known["g"]))
+            count[rs] = len(topo.engines(frm, core))
+            note(rs, rs, count[rs], [], lands, {})
+        calls.append(("g", issue, src[1], lands, 2900.0 if ls == "ln0" else 900.0, 0.0, 2850.0 + 5.3 * size(src[0])))
 
     eq, ge, SHR, AND, mul, add = A.is_equal, A.is_ge, A.arith_shift_right, A.bitwise_and, A.mult, A.add
     EXT = []
@@ -274,6 +374,7 @@ def rank_program(g, core, T, topo):
     dma("s", R("Zin"), (T.need[:], EXT))
     dma("y", R("MW", ROT, W), (T.fig[:, 0:W - ROT], EXT))
     dma("s", R("MW", 0, ROT), (T.fig[:, W - ROT:W], EXT))
+    loads = len(calls)
 
     MS(R("ONE"), 1.0)
     MS(R("FU"), 0.0)
@@ -283,10 +384,10 @@ def rank_program(g, core, T, topo):
     IOTA(ALL("C16"), [[0, 8], [1, 16]], 0, 0)
     IOTA(R("C8"), [[0, 16], [1, 8]], 0, 0)
     IOTA(R("CAL"), [[0, 8], [1, 2], [0, 8]], 0, 0)
-    IOTA(R("IOTA"), [[1, NI]], 0, 0)
-    AFF(R("IDf"), R("ONE"), [[-1, 128]], eq, 0.0, 0, 1)
-    IOTA(R("repI", 0, 8 * NV), [[1, NV], [16, 8]], 0, 0, False)
     IOTA(R("FU", 0, 5 * NV), [[1, 5], [5, NV]], 0, 0)
+    AFF(R("IDf"), R("ONE"), [[-1, 128]], eq, 0.0, 0, 1)
+    IOTA(R("IOTA"), [[1, NI]], 0, 0)
+    IOTA(R("repI", 0, 8 * NV), [[1, NV], [16, 8]], 0, 0, False)
     IOTA(R("OHA"), [[1, 8], [0, 8]], 0, 0)
     IOTA(R("repI", 8 * NV, 8 * NV + 48), [[1, 24], [0, 2]], 0, 0, False)
     IOTA(R("RHO"), [[0, 8], [1, 16], [16, 4]], 0, 0)
@@ -344,10 +445,9 @@ def rank_program(g, core, T, topo):
         ACT(R("sN", 8 * k, 8 * k + 8), G8, scale=R(s) if s else s)
     blank(1)
     MS(R("C128"), 128.0)
-    MS(R("OHW", 0, 64), 0.0)
+    MS(R("OHW", 64, 128), 0.0)
     MS(R("sO"), 0.0)
     MS(R("cK"), 0.0)
-    MS(R("CLP"), CLIP)
     MS(R("LFT"), LIFT)
     MS(R("AVG"), 1.0 / 128)
     for n, offs in (("OFV", (15.0 / 32, -1.0 / 8)), ("OFS", (-15.0 / 32, -3.0 / 8))):
@@ -361,17 +461,15 @@ def rank_program(g, core, T, topo):
     TS(R("OHB"), R("C8", 0, 64), R("QB"), None, eq)
     TS(R("sO", 0, 8), G8, R("T0"), 1.0 / 512, mul, mul)
     TS(R("sO", 32, 40), G8, R("T8"), 1.0 / 512, mul, mul)
+    TS(R("FUa"), R("FU", 0, 2 * NPER, 2), R("SLO"), R("P45"), mul, add)
+    TS(R("FUb"), R("FU", 1, 2 * NPER, 2), R("SHI"), None, mul)
+    TT(R("FUa"), R("FUa"), R("FUb"), add)
+    TC(R("perU", 0, NPER), R("FUa"))
+    ACT(R("repU", 0, 8 * NV), R("repI", 0, 8 * NV))
     ACT(R("Z0"), R("Zin"), F.Copy, bias=-128.0, scale=-1.0)
 
-    def late_constants(part):
-        if part == 0:
-            ACT(R("repU", 0, 8 * NV), R("repI", 0, 8 * NV))
-            TS(R("FUa"), R("FU", 0, 2 * NPER, 2), R("SLO"), R("P45"), mul, add)
-            TS(R("FUb"), R("FU", 1, 2 * NPER, 2), R("SHI"), None, mul)
-            TT(R("FUa"), R("FUa"), R("FUb"), add)
-            TC(R("perU", 0, NPER), R("FUa"))
-            return
-        AFF(R("RST"), R("NEG"), [[0, 8], [1, 64]], A.not_equal, 1e9, 0, 0)
+    def late_constants():
+        AFF(R("RST"), R("NEG"), [[0, 8], [1, 64]], A.not_equal, CLIP, 0, 0)
         AFF(R("RS16"), R("NEG", 0, 256), [[0, 16], [1, 16]], A.not_equal, 1e9, 0, 0)
         for n1, n2, sc, se in (("SELa", "SELb", 16, 1), ("SELc", "SELd", 1, 8)):
             for h in range(2):
@@ -386,7 +484,7 @@ def rank_program(g, core, T, topo):
         ACT(R("repU", 8 * NV, 8 * NV + 48), R("repI", 8 * NV, 8 * NV + 48))
         TS(R("OHA"), R("OHA"), R("P15"), None, eq)
         ACT(R("KJ"), R("KJ"), bias=R("P15"))
-        TT(R("OHW", 64, 128), R("OHA"), R("OHB"), add)
+        TT(R("OHW", 0, 64), R("OHA"), R("OHB"), add)
         figs = R("MW", 0, W)[1]
         for h in range(2):
             dma("y", R("B32", 128 * h, 128 * h + 128), X(T.MW[64 * h:64 * h + 64:16, 0:W], "MW", 0, W))
@@ -395,30 +493,28 @@ def rank_program(g, core, T, topo):
         IOTA(R("LIO"), [[1, 128]], 0, 0)
         IOTA(R("NIO"), [[-1, 128]], 0, 0)
 
-    def suppress(between):
-        first = 24 - NSE
-        order = list(range(first - NSE - 2)) + [e for k in range(NSE) for e in (first + k, first - NSE - 2 + k)] + [first - 2, first - 1]
-
-        def count_in(e):
-            q, h = 32 * (e % 4), 128 * (e % 8 // 4)
-            last = not any(f % 4 == e % 4 for f in order[order.index(e) + 1:])
-            MM([(X(T.pH[q:q + 32, h:h + 128], "pH"), R("HOH", 32 * e, 32 * e + 32), X(T.LOH[:, e, :], "LOH", e, e + 1), False, last)])
-        for k in range(NSE + 1):
-            if k < NSE:
+    def suppress(ns):
+        first = 24 - ns
+        for k in range(ns + 1):
+            if k < ns:
                 ACT(X(T.AB[:, k, :], "AB", k, k + 1), R("LIO"), F.Abs, bias=R("nlo", first + k, first + k + 1))
             if k:
                 e = first + k - 1
                 ACT(X(T.LOH[:, e, :], "LOH", e, e + 1), X(T.AB[:, k - 1, :], "AB", k - 1, k), F.Relu, bias=R("val", e % 8, e % 8 + 1), scale=-1.0)
         TT(ALL("HOH"), IND(R("hiI"), R("repU", 8 * NV, 8 * NV + 48)), ALL("HIO"), eq)
-        for e in order:
-            if e < first:
-                TS(X(T.LOH[:, e, :], "LOH", e, e + 1), R("NIO"), R("nlo", e, e + 1), R("val", e % 8, e % 8 + 1), eq, mul)
-            count_in(e)
-        between()
+        cuts = (0, 3, 6, 8, 9, 10)
+        runs = [list(range(first * a // 10, first * b // 10)) + list(range(first + ns * a // 10, first + ns * b // 10)) for a, b in zip(cuts, cuts[1:])]
+        order = sum(runs, [])
+        for run in runs:
+            for e in run:
+                if e < first:
+                    TS(X(T.LOH[:, e, :], "LOH", e, e + 1), R("NIO"), R("nlo", e, e + 1), R("val", e % 8, e % 8 + 1), eq, mul)
+            MM([(X(T.pH[32 * (e % 4):32 * (e % 4) + 32, 128 * (e % 8 // 4):128 * (e % 8 // 4) + 128], "pH"), R("HOH", 32 * e, 32 * e + 32),
+                 X(T.LOH[:, e, :], "LOH", e, e + 1), False, not any(f % 4 == e % 4 for f in order[order.index(e) + 1:])) for e in run])
 
     def row0(src):
-        for h in range(2):
-            dma("y", X(T.MW[64 * h:64 * h + 64:16, 0:W], "MW", 0, W), R(src, 128 * h, 128 * h + 128), skip=h == 1)
+        halves = [(X(T.MW[64 * h:64 * h + 64:16, 0:W], "MW", 0, W), R(src, 128 * h, 128 * h + 128)) for h in range(2)]
+        dma("y", halves[0][0], halves[0][1], more=halves[1:])
 
     def mates_names(t):
         xy = "XY%d" % t
@@ -430,6 +526,7 @@ def rank_program(g, core, T, topo):
         ACT(R("WN"), IND(R("IOTA"), LY), bias=R("BIB"), scale=R("S2H"))
         ACC(R("pM", 256, 384), [(R("sI"), R("C2"))])
         MM([(R("pJ", 128 * a, 128 * a + 128), R("sJ%d" % a), R("R2"), True, True) for a in range(4)])
+        ACT(R("mo"), R(xy), F.Copy, bias=-2048.0)
         ACT(R("IPs"), R("pM", 256, 384))
 
     mates_names(0)
@@ -442,25 +539,21 @@ def rank_program(g, core, T, topo):
         for a in range(4):
             TT(X(T.Fq[:, :, :, 1 + a], "Fq", 1 + a, 2 + a), R("pJ", 128 * a, 128 * a + 128), R("IPs"), mul)
         TT(X(T.Fq[:, :, :, 0], "Fq", 0, 1), R("pM", 0, 128), R("OT"), mul)
-        if t == 0:
-            late_constants(0)
-        ACT(R("Zr"), IND(R(z), R("repU", 0, 8 * NV)), bias=R("EZ"), scale=-1.0)
+        TS(R("MT"), R("pM", 0, 128), 0.5, -2056.5, mul, add)
+        half = HALF if t else NV
         ACT(R("NZf"), R(z), bias=R("EN"))
+        ACT(R("Zr", 0, 128 * half), IND(R(z), R("repU", 0, 8 * half)), bias=R("EZ"), scale=-1.0)
         TS(ALL("FiS"), X(T.Fq[:, :, NV:16, :], "Fq"), 5, W - 1, SHR, AND)
         TS(R("FiV"), X(T.Fq[:, :, 0:NV, :], "Fq"), 5, W - 1, SHR, AND)
         TC(X(T.FS[:, :, :, 0:5], "FS"), ALL("FiS"))
         TC(R("FV"), IND(R("FiV"), R("perU", 0, NPER)))
-        ACT(R("MT"), R("pM", 0, 128), F.Copy, bias=-2056.5, scale=0.5)
-        ACT(R("mo"), R(xy), F.Copy, bias=-2048.0)
+        if half < NV:
+            TS(R("Zr", 128 * half, 128 * NV), IND(R(z), R("repU", 8 * half, 8 * NV)), -1.0, R("EZ"), mul, add)
         if t == 0:
-            late_constants(1)
+            late_constants()
         bs = X(T.BBb[:, :, NV:16], "BBb")
         ACC(R("pM", 0, 8 * NS), [(R(z), bs), (R("C128"), bs)])
-        TT(ALL("RZ"), R("pM", 0, 8 * NS), R("DM"), mul)
-        ACC(R("pM", 0, 56), [(R("OT"), R("sO")), (R("ONE"), R("cK"))], True, False)
         ACC(ALL("pE"), [(R("IDb"), R("RHO"))], True, False)
-        MM([(R("pJ", 0, 256), R("IDh"), R("MKB"), True, False), (R("pJ", 256, 272), R("IDh"), R("mo"), False, False),
-            (R("pJ", 272, 280), R("IDf"), R("KJ"), False, False)])
 
         def rectangles(kp, xs, sel0, sel):
             reg = (lambda x: (x, x + 1)) if kp == "KV" else (lambda x: (0, NS))
@@ -469,11 +562,12 @@ def rank_program(g, core, T, topo):
         def step(s):
             k = s[2:]
             if s[1] == "v":
-                x, p0, p1 = (int(k), 0, NV) if k < "4" else (4, 0, CUT) if k == "4" else (4, CUT, NV)
+                x, p0, p1 = PIECES[int(k)]
                 ev = [X(T.EV[:, x, 128 * p:128 * p + 128], "EV", NV * x + p, NV * x + p + 1) for p in range(NV)]
             if s[:2] == "gv":
                 TT(X(T.EV[:, x, 128 * p0:128 * p1], "EV", NV * x + p0, NV * x + p1),
-                   IND(R(win, 0, W), R("FV", 8 * (NV * x + p0), 8 * (NV * x + p1))), R("Zr", 128 * p0, 128 * p1), A.max)
+                   IND(R(win, 0, W), R("FV", 8 * (NV * x + p0), 8 * (NV * x + p1))),
+                   R("Zr", 128 * p0, 128 * p1), A.max)
             elif s[:2] == "gs":
                 q = int(k)
                 for c in range(8):
@@ -481,9 +575,10 @@ def rank_program(g, core, T, topo):
                     ACT(X(T.ES[:, q, c:640:8], "ES", 8 * q + c, 8 * q + c + 1), IND(R(win, 0, W), X(T.FS[:, c, q, 0:5], "FS")), F.Relu, bias=R("NZf", j, j + 1))
             elif s[:2] == "mv":
                 b, lo, hi = [c for n, c in CHUNKS.items() if n[0] == "V" and c[1] <= x < c[2]][0]
-                if x == lo and p0 == 0:
+                mine = [n for n, pc in enumerate(PIECES) if lo <= pc[0] < hi]
+                if int(k) == mine[0]:
                     ACC(X(T[b][:, 0:hi - lo, :, :, 0:NV], b), [(R("AVG"), X(T.OFV[:, 0:hi - lo], "OFV"))], True, False)
-                MM([(X(T[b][:, x - lo, :, :, p], b), ev[p], R("ST1"), False, x == hi - 1 and p == NV - 1) for p in range(p0, p1)])
+                MM([(X(T[b][:, x - lo, :, :, p], b), ev[p], R("ST1"), False, int(k) == mine[-1] and p == p1 - 1) for p in range(p0, p1)])
             elif s[:2] == "ms":
                 q = int(k)
                 b, lo, hi = [c for n, c in CHUNKS.items() if n[0] == "S" and c[1] <= q < c[2]][0]
@@ -496,22 +591,23 @@ def rank_program(g, core, T, topo):
                 if s[1] == "V":
                     nx, n = hi - lo, NV
                     kp = X(T.KV[:, lo:hi, :, 0:NV], "KV", lo, hi)
-                    again = [(X(T[b][:, x - lo, 0, :, p], b), X(T.EV[:, x, 128 * p:128 * p + 128], "EV", NV * x + p, NV * x + p + 1), R("ST2"))
-                             for x in range(lo, hi) for p in range(NV)]
+                    data = [X(T.EV[:, x, 128 * p:128 * p + 128], "EV", NV * x + p, NV * x + p + 1) for x in range(lo, hi) for p in range(NV)]
                 else:
                     nx, n = 5, hi - lo
                     kp = X(T.KS[:, :, :, NV + lo:NV + hi], "KS", lo, hi)
-                    again = [(X(T[b][:, x, 0, :, q - lo], b), X(T.ES[:, q, 128 * x:128 * x + 128], "ES", 8 * q, 8 * q + 8), R("ST2"))
-                             for x in range(5) for q in range(lo, hi)]
-                key = X(T[b][:, 0:nx, 0, :, 0:n], b)
-                if s[0] == "r":
+                    data = [X(T.ES[:, q, 128 * x:128 * x + 128], "ES", 8 * q, 8 * q + 8) for x in range(5) for q in range(lo, hi)]
+                kb = KEYS[s[1:]]
+                key = R(kb, 0, 8 * nx * n)
+                if s[0] == "a":
+                    MM([(R(kb, 8 * n * (k // n) + k % n, 8 * n * (k // n + 1), n), d, R("ST2"), k == 0, False) for k, d in enumerate(data)])
+                elif s[0] == "r":
                     rn = "R" + s[1:]
                     TS(ALL(rn), X(T[b][:, 0:nx, :, :, 0:n], b), MAGIC, -MAGIC, add, add)
                     r = [X(T[rn][:, :, w, :], rn) for w in range(2)]
-                    run = [(key, R("I15"), r[0])] + again + [(key, R("I11"), r[1]), (key, R("I16"), r[0]), (key, R("I16"), r[1])]
+                    run = [(key, R("I15"), r[0]), (key, R("I11"), r[1]), (key, R("I16"), r[0]), (key, R("I16"), r[1])]
                     if s[1] == "S":
-                        run += [(X(T[b][:, x, 0, :, 0:n], b), R("CD"), X(T.RZ[:, :, lo:hi], "RZ")) for x in range(5)]
-                    MM([it + (k == 0, k == len(run) - 1) for k, it in enumerate(run)])
+                        run += [(key, R("CD"), X(T.RZ[:, :, :, lo:hi], "RZ"))]
+                    MM([it + (False, k == len(run) - 1) for k, it in enumerate(run)])
                 elif s[0] == "e":
                     rectangles("KV", range(lo, hi), "SEL0", "SELI")
                 elif s[0] == "K":
@@ -524,26 +620,39 @@ def rank_program(g, core, T, topo):
                     ACT(R("SEL1"), ALL("SELd"))
                     ACT(R("SELJ"), R("SELe"))
                     ACT(R("BP"), R("B32"), F.Copy, bias=SIG)
-            if s == "mv1":
-                ACC(R("pH", 0, 256), [(R("IDb"), R("W0" if t else "B32"))], True, False)
+                if t == 1:
+                    IOTA(X(T.EXPM[:], "EXPM") if True else 0, [[0, 2048]], 1, 0, True, R("FV")[1])
+                if t == 2:
+                    AFF((T.EXPM[:], [("EXPM", 0, 1)]), (T.EXPM[:], [("EXPM", 0, 1)] + R("FV")[1]), [[-1, 32], [-32, 4], [0, 16]], eq, 0.0, 0, 1)
+            if s == "gv0":
+                TT(X(T.RZ[:, 0], "RZ", 0, 1), R("pM", 0, 8 * NS), R("DM"), mul)
+                for x in range(1, 5):
+                    AFF(X(T.RZ[:, x], "RZ", x, x + 1), X(T.RZ[:, 0], "RZ", 0, 1), [[0, 8 * NS]], ge, 0.0, 0, 0)
         for s in ORDER:
             step(s)
         ACT(R(win, W, W + 128), R(z), F.Copy, bias=-255.0, scale=-2.0)
         rectangles("KS", range(5), "SEL1", "SELJ")
         SCAN(R("M1"), R("RST"), ALL("pE"), 0.0, A.max, A.min)
-        mk = R("mki", 8 * t, 8 * t + 8)
-        TS(mk, R("M1", 63, 512, 64), CLIP, -CLIP, A.min, add)
-        ACT(R("nm"), R("M1", 63, 512, 64), F.Relu, bias=R("CLP"), scale=-1.0)
+        MM([(R("pJ", 0, 256), R("IDh"), R("MKB"), True, False), (R("pJ", 256, 272), R("IDh"), R("mo"), False, False),
+            (R("pJ", 272, 280), R("IDf"), R("KJ"), False, False)])
+        ACC(R("pM", 0, 56), [(R("OT"), R("sO")), (R("ONE"), R("cK"))], True, False)
+        mk = R("M1", 63, 512, 64)
         TS(R("rhoI"), mk, 127, None, AND)
+        ACT(R("nm"), mk, F.Copy, bias=CLIP, scale=-1.0)
+        ACT(R("mki", 8 * t, 8 * t + 8), mk)
         MM([(R("pJ", 256 + 8 * w, 264 + 8 * w), R("NIDf" if w == 2 else "IDf"), R("nm"), False, False) for w in range(3)])
         TC(R("rhoU"), R("rhoI"))
         TT(R("NM"), IND(R("OHW"), R("rhoU")), R("MT"), mul)
         MM([(R("pJ", 128 * w, 128 * w + 128), R("PK%d" % w), R("NM"), False, w == 1) for w in range(2)])
         ACC(R("pM", 0, 56), [(R("NM"), R("sN"))], False)
+        ACC(R("pH", 0, 256), [(R("IDb"), R("W0" if t else "B32"))], True, False)
         NEW = R("NEW")
         last = t == ROUNDS - 1
-        if last:
+
+        def costs():
             TS(R("cI"), R("mki"), 7, None, SHR)
+            TS(R("cn"), R("mki"), CLIP, -6145.0, eq, mul)
+            ACT(R("cf"), R("cI"))
         ACT(R("Asb"), R("pM", 0, 24))
         ACT(R("val"), R("pM", 48, 56), F.Sign, scale=-1.0)
 
@@ -571,45 +680,50 @@ def rank_program(g, core, T, topo):
             pass_names()
             corners()
             pass_needs()
-            suppress(lambda: None)
+            suppress(NSE[t])
             TT(R("W0"), R("pH", 0, 256), R("BP"), A.min)
             row0("W0")
             mates_names(t + 1)
-            if t == 0:
-                IOTA(ALL("EXPM"), [[0, 2048]], 1, 0)
-                AFF(ALL("EXPM"), ALL("EXPM"), [[-1, 32], [-32, 4], [0, 16]], eq, 0.0, 0, 1)
         else:
             row0("B32")
             corners()
-            suppress(pass_names)
+            suppress(NSE[t])
+            pass_names()
             TT(R("FL"), R("pH", 0, 256), R("B32"), A.is_gt)
-            TS(R("cn"), R("cI"), 0.0, -6146.0, eq, mul)
             TS(R("SG"), R("FL"), -2.0, 1.0, mul, add)
             pass_needs()
 
     e = ROUNDS
-    banks = ("pA", "pB", "pC", "pD")
-    for k in range(8):
-        nm = banks[k % 4]
-        MM([(X(T[nm][64 * h:64 * h + 64, x // 2, x % 2] if k % 4 < 2 else T[nm][64 * h:64 * h + 64, 2 * x:2 * x + 2], nm),
-             X(T.EXPM[:, 4 * k + x, :], "EXPM"), R("SG", 128 * h, 128 * h + 128), True, True) for x in range(4) for h in range(2)])
-        TT(R("YF", 512 * k, 512 * k + 512), R("MW", 512 * k, 512 * k + 512), ALL(nm), mul)
-        if k == 0:
-            dma("s", (T.yf[:, 0:512 - ROT], EXT), R("YF", ROT, 512))
-            dma("y", (T.yf[:, W - ROT:W], EXT), R("YF", 0, ROT))
+    block = {"pA": lambda r, x: T.pA[r, x // 2, x % 2], "pB": lambda r, x: T.pB[r, x // 2, x % 2], "pC": lambda r, x: T.pC[r, 2 * x:2 * x + 2],
+             "pD": lambda r, x: T.pD[r, 2 * x:2 * x + 2], "pE": lambda r, x: T.pE[r, 128 * x:128 * x + 128]}
+    sent = 512
+    for k, nm in ((1, "pA"), (2, "pB"), (3, "pC"), (4, "pD"), (5, "pA"), (6, "pB"), (7, "pC"), (0, "pE")):
+        MM([(X(block[nm](slice(64 * h, 64 * h + 64), x), nm), X(T.EXPM[:, 4 * k + x, :], "EXPM"), R("SG", 128 * h, 128 * h + 128), True, True)
+            for x in range(4) for h in range(2)])
+        if k:
+            TT(R("YF", 512 * k, 512 * k + 512), R("MW", 512 * k, 512 * k + 512), ALL(nm), mul)
         else:
-            dma(("s", "y")[k % 2], (T.yf[:, 512 * k - ROT:512 * (k + 1) - ROT], EXT), R("YF", 512 * k, 512 * (k + 1)))
-        if k == 3:
-            ACT(R("cf"), R("cI"))
+            TT(R("YF", ROT, 512), R("MW", ROT, 512), R(nm, ROT, 512), mul)
+            dma("s", (T.yf[:, 0:512 - ROT], EXT), R("YF", ROT, 512))
+            TT(R("YF", W, W + ROT), R("MW", 0, ROT), R(nm, 0, ROT), mul)
+        if k in OUTS:
+            upto = 512 * k + 512 if k else W + ROT
+            dma("y", (T.yf[:, sent - ROT:upto - ROT], EXT), R("YF", sent, upto))
+            sent = upto
+        if k == 2:
+            costs()
+        if k == 5:
             ACC(X(T.pM[0:32, 0:128], "pM"), [(R("cf"), R("IDf")), (R("cn"), R("IDf"))])
-            ACT(X(T.CT[0:32, :], "CT"), X(T.pM[0:32, 0:128], "pM"), F.Copy, bias=6145.0)
+            ACT(X(T.CT[0:32, :], "CT"), X(T.pM[0:32, 0:128], "pM"))
             for x in range(8):
                 dma("s", (T.yc[x:x + 1, :], EXT), X(T.CT[0:32, 16 * x:16 * x + 16], "CT"))
-    ACT(R("YP", 0, 8), R("XY%d" % e, 0, 8))
-    ACT(R("YP", 8, 16), R("XY%d" % e, 8, 16), F.Copy, bias=-float(JO))
-    dma("s", (T.yp[:], EXT), R("YP"))
+            ACT(R("YP", 0, 8), R("XY%d" % e, 0, 8))
+            ACT(R("YP", 8, 16), R("XY%d" % e, 8, 16), F.Copy, bias=-float(JO))
+            dma("s", (T.yp[:], EXT), R("YP"))
     ACT(R("YZ"), R("Z%d" % e), F.Copy, bias=-128.0, scale=-1.0)
     dma("s", (T.yz[:], EXT), R("YZ"))
+    for k in arrange():
+        calls[k][1]()
     for s, n in sorted(count.items()):
         if known["g"].get(s, 0) < n:
             g.wait_ge(T.sem[s], n)

@@ -12,16 +12,23 @@ ROUNDS = 4
 NV = 9
 NS = 16 - NV
 NPER = (40 * NV + 15) // 16
-NSE = [7, 7, 7, 8]
-OUTS = (1, 3, 5, 7, 0)
-HALF = 9
+NSE = [11, 11, 11, 11]
+FIRST = 2
+OUTS = (2, 4, 6, 0)
+ZS = 2
 PIECES = [(0, 0, 9), (1, 0, 9), (2, 0, 9), (3, 0, 9), (4, 0, 5), (4, 5, 9)]
 CHUNKS = {"VA": ("pA", 0, 2), "VB": ("pB", 2, 4), "VC": ("pA", 4, 5), "SA": ("pC", 0, 4), "SB": ("pD", 4, 6), "SC": ("pC", 6, 7)}
+ON_SCALAR = "Asb C2 FS MT OT UW WN ext farU mo nlo nm".split()
 KEYS = {"VA": "pJ", "SA": "pH", "VB": "pM", "SB": "pH", "VC": "pJ", "SC": "pM"}
-ORDER = ("gs0 gs1 gv0 gs2 gv1 ms0 mv0 ms1 aVA ms2 gv2 gs3 mv1 rVA KVA eVA ms3 gv3 aSA rSA gs4 mv2 gs5 kSA aSB mv3 ms4 aVB gs6 rVB gv4 gv5 "
-         "mv4 kVB ms5 rSB mv5 aVC ms6 KSB rVC eVB kVC aSC rSC eVC kSC").split()
+ORDER = ("gs0 ms0 gs1 gs2 gv0 gs3 gv1 mv0 aVA mv1 gv2 ms1 ms2 ms3 rVA gv3 KVA aSA gs4 mv2 rSA mv3 aVB kSA eVA gv4 mv4 ms4 rVB gs5 gv5 mv5 "
+         "ms5 aSB gs6 ms6 aVC rVC KVB aSC kVC rSC rSB eVC eVB kSB kSC eSC").split()
 GATHER, WAKE, HOLD = 1.3, 60.0, 2.0
 STEP = 100.0
+SHIFT = {}
+ZG = 1
+RATE = 280.0
+SHARE = {6: 2}
+YS = ()
 
 SB = {}
 POOL = {}
@@ -44,7 +51,8 @@ _small("hiI loI QC", 24, "int32")
 _small("rhoI q3 FC far", 8, "int32")
 _small("mki cI", 8 * ROUNDS, "int32")
 _small("repI", 8 * NV + 48, "int32")
-_small("PI P15i", 1, "int32")
+_small("PI P15i P12i", 1, "int32")
+
 _small("KJ nm val", 8)
 _small("cf cn", 8 * ROUNDS)
 _small("UW YP NEW", 16)
@@ -53,7 +61,7 @@ _small("sO cK", 56)
 _small("DM", 8 * NS)
 _small("FU", 2 * NPER)
 _small("FUa FUb", NPER)
-_small("P15 SLO SHI S2L S2H R2B C2B BIA BIB CKR CKC T0 T1 T8 T9 QA QB QB8 QJ1 QJ2 QJ3 P7 P16 P45 LFT R0 RA WX EN EZ", 1)
+_small("P15 SLO SHI S2L S2H R2B C2B BIA BIB CKR CKC T0 T1 T8 T9 QA QB QB8 QJ1 QJ2 QJ3 P7 P16 P45 LFT QRT R0 RA WX EN EZ", 1)
 _sb("poolF", [USED["poolF"]])
 _sb("poolI", [USED["poolI"]], "int32")
 _sb("prowI pcolI", [8], "int32")
@@ -64,7 +72,8 @@ for _t in range(ROUNDS + 1):
     _sb("Z%d" % _t, [128], "bfloat16")
 _sb("XYs", [16], "uint16")
 _sb("repU", [8 * NV + 48], "uint16")
-_sb("Zs Zin YZ IDb C128 AVG", [128], "bfloat16")
+_sb("Zs Zin IDb NIDb I128 C128 AVG", [128], "bfloat16")
+_sb("YT", [512], "bfloat16")
 _sb("OFV", [2, 2, 8, NV], "bfloat16")
 _sb("OFS", [5, 2, 8, 4], "bfloat16")
 _sb("ST1", [16], "float16")
@@ -80,30 +89,31 @@ _sb("sJ0 sJ1 sJ2 sJ3 sA sB sI PK0 PK1 IDh I15 I11 I16 SELI SELJ CD R2 C2 NM U WN
 _sb("sN", [56], "float16")
 _sb("mo", [16], "float16")
 _sb("RZ", [5, 8, NS], "float16")
-_sb("SEL0 SEL1", [512], "float16")
+_sb("SEL0 SEL1", [8, 2, 32], "float16")
 _sb("MKB", [256], "float16")
 for _n, (_b, _lo, _hi) in CHUNKS.items():
     _sb("R" + _n, [_hi - _lo, 2, 8 * NV] if _n[0] == "V" else [5, 2, 8 * (_hi - _lo)], "float16")
 _sb("KV KS", [5, 8, 16], "float16")
 _sb("RHO ZEb", [512], "bfloat16")
-_sb("SELa SELb SELc SELd", [8, 2, 32], "bfloat16")
-_sb("SELe LIO NIO", [128], "bfloat16")
+_sb("NIO", [128], "bfloat16")
 _sb("EXPM", [32, 64], "bfloat16")
-_sb("NEG RST", [512])
+_sb("RST", [512])
 _sb("M1", [512], "int32")
 _sb("RS16 NSC", [256])
 _sb("OHA OHB", [64])
-_sb("SG FL B32 BP W0", [256], "bfloat16")
-_sb("HIO HOH", [768], "bfloat16")
-_sb("LOH", [24, 128], "bfloat16")
-_sb("AB", [max(NSE), 128], "bfloat16")
+_sb("SG B32 BP W0", [256], "bfloat16")
+_sb("HOH NHO", [768], "bfloat16")
+_sb("HIO", [384], "bfloat16")
+_sb("LOH", [24, 130], "bfloat16")
+_sb("LIO", [129])
 _sb("Fq", [8, 16, 5], "int32")
 _sb("FiS", [8, NS, 5], "int32")
 _sb("FiV", [40 * NV], "int32")
 _sb("perU", [NPER + NPER % 2], "uint16")
 _sb("FS", [8, NS, 6], "uint16")
 _sb("FV", [16 * NPER], "uint16")
-_sb("Zr", [128 * NV])
+_sb("Zr", [128 * NV], "float16")
+_sb("Z4x", [32 * NV], "float16")
 _sb("EV", [5, 128 * NV], "float16")
 _sb("ES", [NS, 640], "float16")
 for _n, _s in (("pA", [2, 2, 8, 16]), ("pB", [2, 2, 8, 16]), ("pC", [8, 2, 8, 4]), ("pD", [8, 2, 8, 4]), ("pE", [512]),
@@ -203,7 +213,7 @@ def rank_program(g, core, T, topo):
             note(sem, sem, count[sem], reads, writes, dict(known[q]))
         side = out if out[1] else in_
         nbytes = len(pairs) * side[0].shape[0] * size(side[0]) * (2 if narrow(side) else 4)
-        calls.append((q, issue, reads + list(after), writes, 60.0 * len(pairs), 60.0 + nbytes / 190.0, 1700.0))
+        calls.append((q, issue, reads + list(after), writes, 60.0 * len(pairs), 60.0 + nbytes / RATE, 1700.0))
 
     def cost_v(out, *ins):
         n = size(out[0])
@@ -232,7 +242,9 @@ def rank_program(g, core, T, topo):
             before.append(deps)
             for j in deps:
                 after[j].append(k)
-        way = [-STEP * k for k in range(len(calls))]
+        def written(n, lo, hi):
+            return ([m for m, (p, base, width) in POOL.items() if p == n and base <= lo < base + width] + [n.rstrip("0123456789")])[0]
+        way = [-STEP * (k + (SHIFT.get(written(*c[3][0]), 0) if c[3] else 0)) for k, c in enumerate(calls)]
 
         def sweep(before, after, way):
             left = [len(d) for d in before]
@@ -278,7 +290,8 @@ def rank_program(g, core, T, topo):
             n, lo, hi = p, base + lo, base + hi
         elif hi is None:
             hi = SB[n][1][1]
-        return (T[n][:, lo:hi:step] if step > 1 else T[n][:, lo:hi], [(n, lo, hi)])
+        rows = [(n, -2, 0)] if n == "MW" and lo < W else []
+        return (T[n][:, lo:hi:step] if step > 1 else T[n][:, lo:hi], [(n, lo, hi)] + rows)
 
     def X(ap, n, lo=0, hi=1 << 20):
         return (ap, [(n, lo, hi)])
@@ -314,6 +327,12 @@ def rank_program(g, core, T, topo):
         n = size(out[0])
         emit("s", lambda: g.scalar.activation(out[0], a[0], func, bias=val(bias), scale=val(scale)), regs_of(a, bias, scale), out[1],
              65 + (GATHER * n if len(a) == 3 else 0.83 * max(64, n)))
+
+    def AFFINE(name, out, a, scale=1.0, bias=0.0):
+        if name in ON_SCALAR:
+            ACT(out, a, F.Identity if isinstance(bias, tuple) else F.Copy, bias=bias, scale=scale)
+        else:
+            TS(out, a, scale, bias, A.mult, A.add)
 
     def MM(items):
         def go():
@@ -351,7 +370,7 @@ def rank_program(g, core, T, topo):
             note(ls, ls, count[ls], src[1], [], dict(known["g"]))
             count[rs] = len(topo.engines(frm, core))
             note(rs, rs, count[rs], [], lands, {})
-        calls.append(("g", issue, src[1], lands, 2900.0 if ls == "ln0" else 900.0, 0.0, 2850.0 + 5.3 * size(src[0])))
+        calls.append(("g", issue, src[1], lands, 2900.0 if ls == "ln0" else 900.0, 0.0, 3300.0 + 5.3 * size(src[0])))
 
     eq, ge, SHR, AND, mul, add = A.is_equal, A.is_ge, A.arith_shift_right, A.bitwise_and, A.mult, A.add
     EXT = []
@@ -372,8 +391,8 @@ def rank_program(g, core, T, topo):
     dma("s", R("pcolI"), (T.pcol[:], EXT))
     mates(0, "ys")
     dma("s", R("Zin"), (T.need[:], EXT))
-    dma("y", R("MW", ROT, W), (T.fig[:, 0:W - ROT], EXT))
-    dma("s", R("MW", 0, ROT), (T.fig[:, W - ROT:W], EXT))
+    dma("y", X(T.MW[:, ROT:W], "MW", ROT, W), (T.fig[:, 0:W - ROT], EXT))
+    dma("s", X(T.MW[:, 0:ROT], "MW", 0, ROT), (T.fig[:, W - ROT:W], EXT))
     loads = len(calls)
 
     MS(R("ONE"), 1.0)
@@ -384,45 +403,31 @@ def rank_program(g, core, T, topo):
     IOTA(ALL("C16"), [[0, 8], [1, 16]], 0, 0)
     IOTA(R("C8"), [[0, 16], [1, 8]], 0, 0)
     IOTA(R("CAL"), [[0, 8], [1, 2], [0, 8]], 0, 0)
+    IOTA(R("IOTA", 0, NI // 2), [[1, NI // 2]], 0, 0)
+    AFF(R("IDh"), R("ONE"), [[-1, 128]], eq, 0.0, 0, 1)
     IOTA(R("FU", 0, 5 * NV), [[1, 5], [5, NV]], 0, 0)
-    AFF(R("IDf"), R("ONE"), [[-1, 128]], eq, 0.0, 0, 1)
-    IOTA(R("IOTA"), [[1, NI]], 0, 0)
-    IOTA(R("repI", 0, 8 * NV), [[1, NV], [16, 8]], 0, 0, False)
-    IOTA(R("OHA"), [[1, 8], [0, 8]], 0, 0)
-    IOTA(R("repI", 8 * NV, 8 * NV + 48), [[1, 24], [0, 2]], 0, 0, False)
-    IOTA(R("RHO"), [[0, 8], [1, 16], [16, 4]], 0, 0)
-    IOTA(R("KJ"), [[16, 8]], W, 0)
+    IOTA(R("repI", 0, 2 * NV), [[1, NV], [64, 2]], 0, 0, False)
 
+    def LIN(n, m, scale, bias):
+        ACT(R(n), R(m), F.Identity if isinstance(bias, tuple) else F.Copy, bias=bias, scale=scale)
     TS(R("P15i"), R("PI"), 15, None, AND)
-    MS(R("NEG"), -1e9)
+    TS(R("P12i"), R("PI"), 12, None, AND)
     TC(R("P15"), R("P15i"))
-    MS(R("ZEb"), 0.0)
     TS(R("SLO"), R("P15"), 8.0, None, A.is_lt)
     TS(R("SHI"), R("P15"), 8.0, None, ge)
-    TS(R("S2L"), R("P15"), 8.0, 2.0, A.is_lt, mul)
-    TS(R("S2H"), R("P15"), 8.0, 2.0, ge, mul)
-    TS(R("BIA"), R("P15"), 8.0, -4096.0, A.is_lt, mul)
-    TS(R("BIB"), R("P15"), 8.0, -4096.0, ge, mul)
     TS(R("R0"), R("P15"), 0.0, None, eq)
-    TS(R("RA"), R("P15"), 0.0, None, A.is_gt)
-    TS(R("WX"), R("R0"), BIGA - BIG0, -BIGA, mul, add)
-    TS(R("EN"), R("R0"), EPS0 - EPS, 128.0 + EPS, mul, add)
-    TS(R("EZ"), R("R0"), EPS - EPS0, -128.0 - EPS, mul, add)
     for n, r, c in (("T0", 0.0, 512.0), ("T1", 1.0, 2.125), ("T8", 8.0, 512.0), ("T9", 9.0, 2.125)):
         TS(R(n), R("P15"), r, c, eq, mul)
-    TS(R("R2B"), R("SLO"), 2.0 * (JO - 2048) - 1, 1.0, mul, add)
-    TS(R("C2B"), R("SHI"), -4097.0, 1.0, mul, add)
     TS(R("QA"), R("SHI"), -50.0, R("P15"), mul, add)
     TS(R("QB8"), R("SLO"), -50.0, R("P15"), mul, add)
-    TS(R("P7"), R("SHI"), -8.0, R("P15"), mul, add)
-    TT(R("CKR"), R("T8"), R("T9"), add)
-    TT(R("CKC"), R("T0"), R("T1"), add)
+    for n, m, scale, bias in (("CKC", "T0", 1.0, R("T1")), ("CKR", "T8", 1.0, R("T9")), ("QB", "QB8", 1.0, -8.0), ("QJ1", "QA", 1.0, -2.0),
+                              ("QJ2", "QA", 1.0, -4.0), ("QJ3", "QA", 1.0, -6.0), ("S2H", "SHI", 2.0, 0.0), ("C2B", "SHI", -4097.0, 1.0),
+                              ("S2L", "SLO", 2.0, 0.0), ("R2B", "SLO", 2.0 * (JO - 2048) - 1, 1.0), ("BIA", "SLO", -4096.0, 0.0),
+                              ("BIB", "SHI", -4096.0, 0.0), ("P7", "SHI", -8.0, R("P15")), ("P45", "P7", 5.0 * NV, 0.0),
+                              ("EZ", "R0", EPS - EPS0, -128.0 - EPS), ("EN", "R0", EPS0 - EPS, 128.0 + EPS), ("P16", "P12i", 4.0, 0.0)):
+        LIN(n, m, scale, bias)
     TS(R("OFF"), R("BB"), -999.0, 999.0, mul, add)
-    TS(R("QB"), R("QB8"), -8.0, None, add)
-    for a in range(1, 4):
-        TS(R("QJ%d" % a), R("QA"), -2.0 * a, None, add)
-    TS(R("P45"), R("P7"), 5.0 * NV, None, mul)
-    for n, m in (("C16m", "C16"), ("C8m", "C8"), ("CAL", "CAL")):
+    for n, m in (("C8m", "C8"), ("CAL", "CAL"), ("C16m", "C16")):
         TT(R(n), ALL(m), R("OFF"), add)
     TS(R("sI"), R("C8m"), R("QB"), R("CKC"), eq, add)
     for a in range(4):
@@ -431,103 +436,119 @@ def rank_program(g, core, T, topo):
     TS(R("sB"), R("C16m"), R("QB8"), None, eq)
     ACT(R("XY0", 0, 8), R("prowI"))
     ACT(R("XY0", 8, 16), R("pcolI"), F.Copy, bias=float(JO))
-    G8 = R("BB", 0, 128, 16)
-    ACT(R("ST1", 0, 8), G8, scale=R("RA"))
-    ACT(R("ST1", 8, 16), G8, scale=R("R0"))
-    ACT(R("ST2"), G8, scale=R("WX"))
-    ACT(R("IDh"), R("IDf"))
-    ACT(ALL("BBb"), R("BB"))
-    for w, s in enumerate(("SHI", "SLO")):
-        ACT(R("PK%d" % w), R("BB"), scale=R(s))
-    for c in range(8):
-        ACT(R("CD", c, 128, 8), R("BB", 16 * c, 16 * c + 16), scale=-1.0 / 16)
-    for k, s in enumerate((0.0, "S2H", "S2H", "S2L", 0.0, "S2L", "SHI")):
-        ACT(R("sN", 8 * k, 8 * k + 8), G8, scale=R(s) if s else s)
-    blank(1)
-    MS(R("C128"), 128.0)
-    MS(R("OHW", 64, 128), 0.0)
-    MS(R("sO"), 0.0)
-    MS(R("cK"), 0.0)
-    MS(R("LFT"), LIFT)
-    MS(R("AVG"), 1.0 / 128)
-    for n, offs in (("OFV", (15.0 / 32, -1.0 / 8)), ("OFS", (-15.0 / 32, -3.0 / 8))):
-        for w in range(2):
-            MS(X(T[n][:, :, w], n, w, w + 1), offs[w])
-    for lo, hi in ((8, 32), (40, 48)):
-        MS(R("cK", lo, hi), 4113.0 / 128)
-    for w in range(2):
-        TS(R("MKB", 128 * w, 128 * w + 128), ALL("C16"), R("P15"), 4096.0, A.not_equal, mul)
-    TS(R("DM"), X(T.C16[:, :, NV:16], "C16"), R("P15"), None, eq)
-    TS(R("OHB"), R("C8", 0, 64), R("QB"), None, eq)
-    TS(R("sO", 0, 8), G8, R("T0"), 1.0 / 512, mul, mul)
-    TS(R("sO", 32, 40), G8, R("T8"), 1.0 / 512, mul, mul)
+    ACT(R("IOTA", NI // 2, NI), R("IOTA", 0, NI // 2), F.Copy, bias=float(NI // 2))
     TS(R("FUa"), R("FU", 0, 2 * NPER, 2), R("SLO"), R("P45"), mul, add)
     TS(R("FUb"), R("FU", 1, 2 * NPER, 2), R("SHI"), None, mul)
     TT(R("FUa"), R("FUa"), R("FUb"), add)
     TC(R("perU", 0, NPER), R("FUa"))
-    ACT(R("repU", 0, 8 * NV), R("repI", 0, 8 * NV))
+    ACT(R("repU", 0, 2 * NV), R("repI", 0, 2 * NV), bias=R("P16"))
     ACT(R("Z0"), R("Zin"), F.Copy, bias=-128.0, scale=-1.0)
 
     def late_constants():
-        AFF(R("RST"), R("NEG"), [[0, 8], [1, 64]], A.not_equal, CLIP, 0, 0)
-        AFF(R("RS16"), R("NEG", 0, 256), [[0, 16], [1, 16]], A.not_equal, 1e9, 0, 0)
-        for n1, n2, sc, se in (("SELa", "SELb", 16, 1), ("SELc", "SELd", 1, 8)):
-            for h in range(2):
-                AFF(X(T[n1][:, :, h, :], n1, h, h + 1), R("ZEb", 0, 256), [[-sc, 8], [0, 8], [-2 * se, 4]], A.not_equal, 2048.0, -h * se, 1)
-            for h in range(2):
-                AFF(X(T[n2][:, :, h, :], n2, h, h + 1), X(T[n1][:, :, h, :], n1, h, h + 1), [[-sc, 8], [-se, 8], [0, 4]], A.not_equal, 2048.0, -8 * se, 1)
-        AFF(R("SELe"), R("ZEb", 0, 128), [[-1, 8], [-8, 16]], A.not_equal, 2048.0, 0, 1)
-        for n, c in (("IDb", 1.0), ("I15", BIGA), ("I11", BIG0), ("I16", 1.0 / 16), ("SELI", 2048.0), ("NIDf", -1.0)):
-            ACT(R(n), R("IDf"), scale=c)
-        for n in ("KV", "KS"):
-            TS(ALL(n), R("IOTA", 0, 640), 0.0, None, mul)
-        ACT(R("repU", 8 * NV, 8 * NV + 48), R("repI", 8 * NV, 8 * NV + 48))
-        TS(R("OHA"), R("OHA"), R("P15"), None, eq)
-        ACT(R("KJ"), R("KJ"), bias=R("P15"))
-        TT(R("OHW", 0, 64), R("OHA"), R("OHB"), add)
+        G8 = R("BB", 0, 128, 16)
+        MS(R("AVG"), 1.0 / 128)
+        for n, offs in (("OFV", (15.0 / 32, -1.0 / 8)), ("OFS", (-15.0 / 32, -3.0 / 8))):
+            for w in range(2):
+                MS(X(T[n][:, :, w], n, w, w + 1), offs[w])
+        MS(R("C128"), 128.0)
+        MS(R("ZEb"), 0.0)
+        LIN("RA", "R0", -1.0, 1.0)
+        LIN("WX", "R0", BIGA - BIG0, -BIGA)
+        ACT(R("ST1", 0, 8), G8, scale=R("RA"))
+        ACT(R("ST1", 8, 16), G8, scale=R("R0"))
+        ACT(R("ST2"), G8, scale=R("WX"))
+        ACT(ALL("BBb"), R("BB"))
+        TS(R("DM"), X(T.C16[:, :, NV:16], "C16"), R("P15"), None, eq)
+        IOTA(R("RHO"), [[0, 8], [1, 16], [16, 4]], 0, 0)
+        for n, c in (("IDb", 1.0), ("I15", BIGA), ("I11", BIG0), ("I16", 1.0 / 16), ("SELI", 2048.0)):
+            ACT(R(n), R("IDh"), scale=c)
+        MS(R("LFT"), LIFT)
+        AFF(R("CD"), R("AVG"), [[0, 16], [-16, 8]], ge, 0.0, 0, 1)
+        AFF(R("CD"), R("CD"), [[0, 16], [16, 8]], ge, 0.0, 15, -1)
+        ACT(R("CD"), R("CD"), scale=-8.0)
+        blank(1)
         figs = R("MW", 0, W)[1]
         for h in range(2):
-            dma("y", R("B32", 128 * h, 128 * h + 128), X(T.MW[64 * h:64 * h + 64:16, 0:W], "MW", 0, W))
+            dma("y", R("B32", 128 * h, 128 * h + 128), X(T.MW[64 * h:64 * h + 64:16, 0:W], "MW", -2, W))
         mates(1, "yy", figs)
-        IOTA(ALL("HIO"), [[0, 24], [1, 32]], 0, 0)
-        IOTA(R("LIO"), [[1, 128]], 0, 0)
+
+    def key_constants():
+        for n, kp, lo, hi, sc, se in (("SEL0", "KV", NV, 16, 16, 1), ("SEL1", "KS", 0, NV, 1, 8)):
+            AFF(X(T[kp][:, :, :, lo:hi], kp, 9, 10), R("ZEb", 0, 40 * (hi - lo)), [[0, 40 * (hi - lo)]], ge, 0.0, 0, 0)
+            for h in range(2):
+                AFF(X(T[n][:, :, h, :], n, h, h + 1), R("ZEb", 0, 256), [[-sc, 8], [0, 8], [-2 * se, 4]], A.not_equal, 2048.0, -h * se, 1)
+            for h in range(2):
+                AFF(X(T[n][:, :, h, :], n, h, h + 1), X(T[n][:, :, h, :], n, h, h + 1), [[-sc, 8], [-se, 8], [0, 4]], A.not_equal, 2048.0, -8 * se, 1)
+        AFF(R("SELJ"), R("ZEb", 0, 128), [[-1, 8], [-8, 16]], A.not_equal, 2048.0, 0, 1)
+        IOTA(R("OHA"), [[1, 8], [0, 8]], 0, 0)
+        IOTA(R("KJ"), [[16, 8]], W, 0)
+        AFF(R("RST"), R("ZEb"), [[0, 8], [1, 64]], A.not_equal, CLIP, 0, 0)
+        IOTA(R("RS16"), [[0, 16], [-16384, 16]], 8192, 0)
+        for h in range(2):
+            IOTA(R("repI", 8 * NV + 24 * h, 8 * NV + 24 * h + 24), [[8, 3], [1, 4], [0, 2]], 4 * h, 0, False)
+        IOTA(ALL("HIO"), [[0, 12], [1, 32]], 0, 0)
         IOTA(R("NIO"), [[-1, 128]], 0, 0)
 
-    def suppress(ns):
-        first = 24 - ns
-        for k in range(ns + 1):
-            if k < ns:
-                ACT(X(T.AB[:, k, :], "AB", k, k + 1), R("LIO"), F.Abs, bias=R("nlo", first + k, first + k + 1))
-            if k:
-                e = first + k - 1
-                ACT(X(T.LOH[:, e, :], "LOH", e, e + 1), X(T.AB[:, k - 1, :], "AB", k - 1, k), F.Relu, bias=R("val", e % 8, e % 8 + 1), scale=-1.0)
-        TT(ALL("HOH"), IND(R("hiI"), R("repU", 8 * NV, 8 * NV + 48)), ALL("HIO"), eq)
-        cuts = (0, 3, 6, 8, 9, 10)
-        runs = [list(range(first * a // 10, first * b // 10)) + list(range(first + ns * a // 10, first + ns * b // 10)) for a, b in zip(cuts, cuts[1:])]
-        order = sum(runs, [])
-        for run in runs:
-            for e in run:
-                if e < first:
-                    TS(X(T.LOH[:, e, :], "LOH", e, e + 1), R("NIO"), R("nlo", e, e + 1), R("val", e % 8, e % 8 + 1), eq, mul)
-            MM([(X(T.pH[32 * (e % 4):32 * (e % 4) + 32, 128 * (e % 8 // 4):128 * (e % 8 // 4) + 128], "pH"), R("HOH", 32 * e, 32 * e + 32),
-                 X(T.LOH[:, e, :], "LOH", e, e + 1), False, not any(f % 4 == e % 4 for f in order[order.index(e) + 1:])) for e in run])
+    def last_constants():
+        G8 = R("BB", 0, 128, 16)
+        for w in range(2):
+            TS(R("MKB", 128 * w, 128 * w + 128), ALL("C16"), R("P15"), 4096.0, A.not_equal, mul)
+        ACT(R("KJ"), R("KJ"), bias=R("P15"))
+        for n, c in (("IDf", 1.0), ("NIDf", -1.0)):
+            ACT(R(n), R("IDh"), scale=c)
+        MS(R("OHW", 64, 128), 0.0)
+        TS(R("OHB"), R("C8", 0, 64), R("QB"), None, eq)
+        TS(R("OHA"), R("OHA"), R("P15"), None, eq)
+        TT(R("OHW", 0, 64), R("OHA"), R("OHB"), add)
+        for w, s in enumerate(("SHI", "SLO")):
+            ACT(R("PK%d" % w), R("BB"), scale=R(s))
+        MS(R("sO"), 0.0)
+        MS(R("cK"), 4113.0 / 128)
+        for lo, hi in ((0, 8), (32, 40), (48, 56)):
+            AFF(R("cK", lo, hi), R("cK", lo, hi), [[0, 8]], A.is_gt, 0.0, 0, 0)
+        TS(R("sO", 0, 8), G8, R("T0"), 1.0 / 512, mul, mul)
+        TS(R("sO", 32, 40), G8, R("T8"), 1.0 / 512, mul, mul)
+        for k, s in enumerate((0.0, "S2H", "S2H", "S2L", 0.0, "S2L", "SHI")):
+            ACT(R("sN", 8 * k, 8 * k + 8), G8, scale=R(s) if s else s)
+        ACT(R("repU", 8 * NV, 8 * NV + 48), R("repI", 8 * NV, 8 * NV + 48))
+        ACT(R("LIO"), R("IOTA", 0, 129), F.Copy, bias=-0.5)
 
-    def row0(src):
-        halves = [(X(T.MW[64 * h:64 * h + 64:16, 0:W], "MW", 0, W), R(src, 128 * h, 128 * h + 128)) for h in range(2)]
-        dma("y", halves[0][0], halves[0][1], more=halves[1:])
+    def suppress(ns, then):
+        for h, bank in enumerate(("pH", "pE")):
+            n0, n1 = 12 * h, 12 * h + (ns + 1 - h) // 2
+            col = {n: 8 * (n % 12 // 4) + 4 * h + n % 4 for n in range(n0, n0 + 12)}
+            for n in range(n0, n1):
+                ACT(X(T.LOH[:, n, 0:129], "LOH", n, n + 1), R("LIO"), F.Sign, bias=R("nlo", col[n], col[n] + 1), scale=R("val", col[n] % 8, col[n] % 8 + 1))
+            for a, b in ((n0, n1), (n1, n0 + 12)):
+                TT(R("HOH", 32 * a, 32 * b), IND(R("hiI"), R("repU", 8 * NV + 2 * a, 8 * NV + 2 * b)), R("HIO", 0, 32 * (b - a)), eq)
+                if a == n0:
+                    TS(R("NHO", 32 * n0, 32 * n1), R("HOH", 32 * n0, 32 * n1), -1.0, None, mul)
+            mine, theirs = list(range(n1, n0 + 12)), list(range(n0, n1))
+            runs = [theirs[:3], theirs[3:] + mine[:2], mine[2:-1], mine[-1:]]
+            order = sum(runs, [])
+            for run in runs:
+                for n in run:
+                    if n >= n1:
+                        TS(X(T.LOH[:, n, 1:129], "LOH", n, n + 1), R("NIO"), R("nlo", col[n], col[n] + 1), R("val", col[n] % 8, col[n] % 8 + 1), eq, mul)
+                MM([(X(T[bank][32 * (n % 4):32 * (n % 4) + 32, 0:128], bank), R(side, 32 * n, 32 * n + 32), X(T.LOH[:, n, k:k + 128], "LOH", n, n + 1),
+                     False, k == 1 and not any(f % 4 == n % 4 for f in order[order.index(n) + 1:]))
+                    for n in run for k, side in enumerate(("NHO", "HOH")) if k or n < n1])
+            then(h, R(bank, 0, 128))
+
+    def row0(src, h):
+        dma("y", X(T.MW[64 * h:64 * h + 64:16, 0:W], "MW", -2 + h, -1 + h), R(src, 128 * h, 128 * h + 128))
 
     def mates_names(t):
         xy = "XY%d" % t
         LX, LY = R(xy, 0, 8), R(xy, 8, 16)
         XM = R("XM%d" % (t % 2))
-        TS(R("C2"), IND(XM, LY), R("S2H"), R("C2B"), mul, add)
-        TS(R("R2"), IND(XM, LX), R("S2L"), R("R2B"), mul, add)
-        ACT(R("U"), IND(R("IOTA"), LX), bias=R("BIA"), scale=R("S2L"))
-        ACT(R("WN"), IND(R("IOTA"), LY), bias=R("BIB"), scale=R("S2H"))
+        AFFINE("C2", R("C2"), IND(XM, LY), R("S2H"), R("C2B"))
+        AFFINE("R2", R("R2"), IND(XM, LX), R("S2L"), R("R2B"))
+        AFFINE("U", R("U"), IND(R("IOTA"), LX), R("S2L"), R("BIA"))
+        AFFINE("WN", R("WN"), IND(R("IOTA"), LY), R("S2H"), R("BIB"))
         ACC(R("pM", 256, 384), [(R("sI"), R("C2"))])
         MM([(R("pJ", 128 * a, 128 * a + 128), R("sJ%d" % a), R("R2"), True, True) for a in range(4)])
-        ACT(R("mo"), R(xy), F.Copy, bias=-2048.0)
-        ACT(R("IPs"), R("pM", 256, 384))
+        AFFINE("IPs", R("IPs"), R("pM", 256, 384))
 
     mates_names(0)
     for t in range(ROUNDS):
@@ -535,29 +556,30 @@ def rank_program(g, core, T, topo):
         win = "MW"
         ACC(R("pM", 128, 256), [(R("IDh"), R("U")), (R("IDh"), R("WN"))])
         ACC(R("pM", 0, 128), [(R("sA"), R("R2")), (R("sB"), R("C2"))])
-        ACT(R("OT"), R("pM", 128, 256), F.Copy, bias=4113.0)
+        AFFINE("OT", R("OT"), R("pM", 128, 256), 1.0, 4113.0)
         for a in range(4):
             TT(X(T.Fq[:, :, :, 1 + a], "Fq", 1 + a, 2 + a), R("pJ", 128 * a, 128 * a + 128), R("IPs"), mul)
         TT(X(T.Fq[:, :, :, 0], "Fq", 0, 1), R("pM", 0, 128), R("OT"), mul)
-        TS(R("MT"), R("pM", 0, 128), 0.5, -2056.5, mul, add)
-        half = HALF if t else NV
-        ACT(R("NZf"), R(z), bias=R("EN"))
-        ACT(R("Zr", 0, 128 * half), IND(R(z), R("repU", 0, 8 * half)), bias=R("EZ"), scale=-1.0)
+        ACT(R("Z4x"), IND(R(z), R("repU", 0, 2 * NV)), bias=R("EZ"), scale=-1.0)
         TS(ALL("FiS"), X(T.Fq[:, :, NV:16, :], "Fq"), 5, W - 1, SHR, AND)
         TS(R("FiV"), X(T.Fq[:, :, 0:NV, :], "Fq"), 5, W - 1, SHR, AND)
-        TC(X(T.FS[:, :, :, 0:5], "FS"), ALL("FiS"))
-        TC(R("FV"), IND(R("FiV"), R("perU", 0, NPER)))
-        if half < NV:
-            TS(R("Zr", 128 * half, 128 * NV), IND(R(z), R("repU", 8 * half, 8 * NV)), -1.0, R("EZ"), mul, add)
+        AFFINE("NZf", R("NZf"), R(z), 1.0, R("EN"))
+        AFFINE("FS", X(T.FS[:, :, :, 0:5], "FS"), ALL("FiS"))
+        AFFINE("FV", R("FV"), IND(R("FiV"), R("perU", 0, NPER)))
+        for k in range(4):
+            zr = X(T.Zr[:, k:128 * NV:4], "Zr", k, k + 1)
+            if k >= 4 - ZG and t:
+                AFF(zr, R("Z4x"), [[0, 32 * NV]], ge, 0.0, 0, 0)
+            else:
+                (ACT if k < ZS else TC)(zr, R("Z4x"))
         if t == 0:
             late_constants()
         bs = X(T.BBb[:, :, NV:16], "BBb")
-        ACC(R("pM", 0, 8 * NS), [(R(z), bs), (R("C128"), bs)])
-        ACC(ALL("pE"), [(R("IDb"), R("RHO"))], True, False)
+        ACC(R("pE", 0, 8 * NS), [(R(z), bs), (R("C128"), bs)])
 
-        def rectangles(kp, xs, sel0, sel):
+        def rectangles(kp, xs, sel0, sel, stop):
             reg = (lambda x: (x, x + 1)) if kp == "KV" else (lambda x: (0, NS))
-            MM([(R("pE", x - 1, 512, 4) if x else ALL("pE"), X(T[kp][:, x], kp, *reg(x)), R(sel if x else sel0), False, kp == "KS" and x == 4) for x in xs])
+            MM([(R("pE", x - 1, 512, 4) if x else ALL("pE"), (T[kp][:, x], [(kp,) + reg(x), (kp, 9, 10)]), ALL(sel if x else sel0), False, stop and x == xs[-1]) for x in xs])
 
         def step(s):
             k = s[2:]
@@ -567,12 +589,16 @@ def rank_program(g, core, T, topo):
             if s[:2] == "gv":
                 TT(X(T.EV[:, x, 128 * p0:128 * p1], "EV", NV * x + p0, NV * x + p1),
                    IND(R(win, 0, W), R("FV", 8 * (NV * x + p0), 8 * (NV * x + p1))),
-                   R("Zr", 128 * p0, 128 * p1), A.max)
+                   X(T.Zr[:, 128 * p0:128 * p1], "Zr"), A.max)
             elif s[:2] == "gs":
                 q = int(k)
                 for c in range(8):
                     j = 16 * c + NV + q
-                    ACT(X(T.ES[:, q, c:640:8], "ES", 8 * q + c, 8 * q + c + 1), IND(R(win, 0, W), X(T.FS[:, c, q, 0:5], "FS")), F.Relu, bias=R("NZf", j, j + 1))
+                    out, figs = X(T.ES[:, q, c:640:8], "ES", 8 * q + c, 8 * q + c + 1), IND(R(win, 0, W), X(T.FS[:, c, q, 0:5], "FS"))
+                    if c < SHARE.get(q, 0) and (t or q > 1):
+                        TS(out, figs, R("NZf", j, j + 1), 0.0, add, A.max)
+                    else:
+                        ACT(out, figs, F.Relu, bias=R("NZf", j, j + 1))
             elif s[:2] == "mv":
                 b, lo, hi = [c for n, c in CHUNKS.items() if n[0] == "V" and c[1] <= x < c[2]][0]
                 mine = [n for n, pc in enumerate(PIECES) if lo <= pc[0] < hi]
@@ -609,98 +635,123 @@ def rank_program(g, core, T, topo):
                         run += [(key, R("CD"), X(T.RZ[:, :, :, lo:hi], "RZ"))]
                     MM([it + (False, k == len(run) - 1) for k, it in enumerate(run)])
                 elif s[0] == "e":
-                    rectangles("KV", range(lo, hi), "SEL0", "SELI")
+                    stop = s == [n for n in ORDER if n[0] == "e"][-1]
+                    if s[1] == "V":
+                        rectangles("KV", range(lo, hi), "SEL0", "SELI", stop)
+                    else:
+                        rectangles("KS", range(5), "SEL1", "SELJ", stop)
                 elif s[0] == "K":
                     ACT(kp, key, F.Relu, bias=R("LFT") if s[1] == "S" else 0.0)
                 else:
                     TS(kp, key, LIFT if s[1] == "S" else 0.0, 0.0, add, A.max)
-            if s == "gs2":
-                if t == 0:
-                    ACT(R("SEL0"), ALL("SELb"))
-                    ACT(R("SEL1"), ALL("SELd"))
-                    ACT(R("SELJ"), R("SELe"))
-                    ACT(R("BP"), R("B32"), F.Copy, bias=SIG)
+            if s == "gv1":
                 if t == 1:
-                    IOTA(X(T.EXPM[:], "EXPM") if True else 0, [[0, 2048]], 1, 0, True, R("FV")[1])
+                    IOTA(X(T.EXPM[:], "EXPM") if True else 0, [[0, 2048]], 1, 0, True, [("RZ", 0, 5)])
                 if t == 2:
-                    AFF((T.EXPM[:], [("EXPM", 0, 1)]), (T.EXPM[:], [("EXPM", 0, 1)] + R("FV")[1]), [[-1, 32], [-32, 4], [0, 16]], eq, 0.0, 0, 1)
+                    AFF((T.EXPM[:], [("EXPM", 0, 1)]), (T.EXPM[:], [("EXPM", 0, 1), ("RZ", 0, 5)]), [[-1, 32], [-32, 4], [0, 16]], eq, 0.0, 0, 1)
             if s == "gv0":
-                TT(X(T.RZ[:, 0], "RZ", 0, 1), R("pM", 0, 8 * NS), R("DM"), mul)
+                TT(X(T.RZ[:, 0], "RZ", 0, 1), R("pE", 0, 8 * NS), R("DM"), mul)
+                ACC(ALL("pE"), [(R("IDb"), R("RHO"))], True, False)
                 for x in range(1, 5):
                     AFF(X(T.RZ[:, x], "RZ", x, x + 1), X(T.RZ[:, 0], "RZ", 0, 1), [[0, 8 * NS]], ge, 0.0, 0, 0)
+                if t == 0:
+                    key_constants()
         for s in ORDER:
             step(s)
-        ACT(R(win, W, W + 128), R(z), F.Copy, bias=-255.0, scale=-2.0)
-        rectangles("KS", range(5), "SEL1", "SELJ")
+        AFFINE("mo", R("mo"), (R(xy)[0], R(xy)[1] + [("ES", 8 * NS - 1, 8 * NS)]), 1.0, -2048.0)
+        AFFINE("ext", R(win, W, W + 128), (R(z)[0], R(z)[1] + [("ES", 8 * NS - 1, 8 * NS)]), -2.0, -255.0)
+        if t == 1:
+            MS(R("QRT"), -0.25)
+            ACT(R("NIDb"), R("IDh"), scale=-1.0)
+        if t == 0:
+            last_constants()
+            ACT(R("BP"), (R("B32")[0], R("B32")[1] + [("ES", 8 * NS - 1, 8 * NS)]), F.Copy, bias=SIG)
         SCAN(R("M1"), R("RST"), ALL("pE"), 0.0, A.max, A.min)
         MM([(R("pJ", 0, 256), R("IDh"), R("MKB"), True, False), (R("pJ", 256, 272), R("IDh"), R("mo"), False, False),
             (R("pJ", 272, 280), R("IDf"), R("KJ"), False, False)])
         ACC(R("pM", 0, 56), [(R("OT"), R("sO")), (R("ONE"), R("cK"))], True, False)
+        ACC(X(T.pD[:, 0:2], "pD"), [(R("sA"), R("R2")), (R("sB"), R("C2"))])
+        AFFINE("MT", R("MT"), X(T.pD[:, 0:2], "pD"), 0.5, -2056.5)
         mk = R("M1", 63, 512, 64)
         TS(R("rhoI"), mk, 127, None, AND)
-        ACT(R("nm"), mk, F.Copy, bias=CLIP, scale=-1.0)
+        AFFINE("nm", R("nm"), mk, -1.0, CLIP)
         ACT(R("mki", 8 * t, 8 * t + 8), mk)
         MM([(R("pJ", 256 + 8 * w, 264 + 8 * w), R("NIDf" if w == 2 else "IDf"), R("nm"), False, False) for w in range(3)])
-        TC(R("rhoU"), R("rhoI"))
+        AFFINE("rhoU", R("rhoU"), R("rhoI"))
         TT(R("NM"), IND(R("OHW"), R("rhoU")), R("MT"), mul)
         MM([(R("pJ", 128 * w, 128 * w + 128), R("PK%d" % w), R("NM"), False, w == 1) for w in range(2)])
         ACC(R("pM", 0, 56), [(R("NM"), R("sN"))], False)
-        ACC(R("pH", 0, 256), [(R("IDb"), R("W0" if t else "B32"))], True, False)
-        NEW = R("NEW")
         last = t == ROUNDS - 1
+        for h, bank in enumerate(("pH", "pE")):
+            ACC(R(bank, 0, 128), [(R("IDb"), R("W0" if t else "B32", 128 * h, 128 * h + 128))] +
+                ([(R("NIDb"), R("BP", 128 * h, 128 * h + 128))] if last else []), True, False)
+        NEW = R("NEW")
 
         def costs():
             TS(R("cI"), R("mki"), 7, None, SHR)
             TS(R("cn"), R("mki"), CLIP, -6145.0, eq, mul)
             ACT(R("cf"), R("cI"))
-        ACT(R("Asb"), R("pM", 0, 24))
+        AFFINE("Asb", R("Asb"), R("pM", 0, 24))
         ACT(R("val"), R("pM", 48, 56), F.Sign, scale=-1.0)
 
         def pass_names():
             SCAN(R("NSC"), R("RS16"), R("pJ", 0, 256), 0.0, A.max, A.min)
             TT(NEW, R("pJ", 256, 272), R("NSC", 15, 256, 16), A.min)
-            ACT(R("XYs"), NEW, F.Copy, bias=2048.0)
+            AFFINE("XYs", R("XYs"), NEW, 1.0, 2048.0)
             remote(t, "n", "XY%d" % (t + 1), R("XYs"))
-            ACT(R("UW"), NEW, F.Copy, bias=4113.0, scale=2.0)
+            AFFINE("UW", R("UW"), NEW, 2.0, 4113.0)
 
         def corners():
             TT(R("QC"), R("pM", 24, 48), R("Asb"), mul)
             TS(R("loI"), R("QC"), 5, 127, SHR, AND)
             TS(R("hiI"), R("QC"), 12, 31, SHR, AND)
-            TS(R("nlo"), R("loI"), -1.0, None, mul)
+            AFFINE("nlo", R("nlo"), R("loI"), -1.0)
 
         def pass_needs():
             TT(R("q3"), R("UW", 0, 8), R("UW", 8, 16), mul)
             TS(R("FC"), R("q3"), 5, W - 1, SHR, AND)
             TT(R("far"), R("pJ", 272, 280), R("FC"), A.max)
-            TC(R("farU"), R("far"))
+            AFFINE("farU", R("farU"), R("far"))
             ACT(R("Zs"), IND(R(win), R("farU")), F.Copy, bias=-127.6, scale=-0.5)
             remote(t, "z", "Z%d" % (t + 1), R("Zs"))
         if not last:
             pass_names()
-            corners()
             pass_needs()
-            suppress(NSE[t])
-            TT(R("W0"), R("pH", 0, 256), R("BP"), A.min)
-            row0("W0")
+            corners()
+            def flags(h, counts):
+                TT(R("W0", 128 * h, 128 * h + 128), counts, R("BP", 128 * h, 128 * h + 128), A.min)
+                row0("W0", h)
+            suppress(NSE[t], flags)
             mates_names(t + 1)
         else:
-            row0("B32")
+            row0("B32", 0)
+            row0("B32", 1)
             corners()
-            suppress(NSE[t])
+            suppress(NSE[t], lambda h, counts: ACT(R("SG", 128 * h, 128 * h + 128), counts, F.Sign, bias=R("QRT"), scale=-1.0))
             pass_names()
-            TT(R("FL"), R("pH", 0, 256), R("B32"), A.is_gt)
-            TS(R("SG"), R("FL"), -2.0, 1.0, mul, add)
             pass_needs()
 
     e = ROUNDS
     block = {"pA": lambda r, x: T.pA[r, x // 2, x % 2], "pB": lambda r, x: T.pB[r, x // 2, x % 2], "pC": lambda r, x: T.pC[r, 2 * x:2 * x + 2],
-             "pD": lambda r, x: T.pD[r, 2 * x:2 * x + 2], "pE": lambda r, x: T.pE[r, 128 * x:128 * x + 128]}
+             "pD": lambda r, x: T.pD[r, 2 * x:2 * x + 2], "pE": lambda r, x: T.pE[r, 128 * x:128 * x + 128],
+             "pJ": lambda r, x: T.pJ[r, 128 * x:128 * x + 128]}
     sent = 512
-    for k, nm in ((1, "pA"), (2, "pB"), (3, "pC"), (4, "pD"), (5, "pA"), (6, "pB"), (7, "pC"), (0, "pE")):
-        MM([(X(block[nm](slice(64 * h, 64 * h + 64), x), nm), X(T.EXPM[:, 4 * k + x, :], "EXPM"), R("SG", 128 * h, 128 * h + 128), True, True)
-            for x in range(4) for h in range(2)])
-        if k:
+    for k, nm in ((1, "pE"), (2, "pB"), (3, "pC"), (4, "pD"), (5, "pA"), (6, "pB"), (7, "pC"), (0, "pE")):
+        if k in YS:
+            ACC(ALL(nm), [(R("I128"), R("MW", 512 * k, 512 * k + 512))], True, False)
+        for bank, xs in ((("pA", range(2)), (nm, range(2, 4))) if k == 1 else ((nm, range(4)),)):
+            MM([(X(block[bank](slice(64 * h, 64 * h + 64), x), bank), X(T.EXPM[:, 4 * k + x, :], "EXPM"), R("SG", 128 * h, 128 * h + 128),
+                 k not in YS, k not in YS or x == 3) for x in xs for h in range(2)])
+        if k in YS:
+            ACT(R("YT"), ALL(nm), F.Abs, scale=128.0)
+            ACT(R("YF", 512 * k, 512 * k + 512), R("YT"), F.Copy, bias=-128.0)
+        elif k == 1:
+            cut = 256
+            TT(R("YF", 512, 512 + cut), R("MW", 512, 512 + cut), X(T.pA[:, 0], "pA"), mul)
+            dma("y", (T.yf[:, 512 - ROT:512 + cut - ROT], EXT), R("YF", 512, 512 + cut))
+            sent += cut
+            TT(R("YF", 512 + cut, 1024), R("MW", 512 + cut, 1024), R(nm, cut, 512), mul)
+        elif k:
             TT(R("YF", 512 * k, 512 * k + 512), R("MW", 512 * k, 512 * k + 512), ALL(nm), mul)
         else:
             TT(R("YF", ROT, 512), R("MW", ROT, 512), R(nm, ROT, 512), mul)
@@ -720,8 +771,8 @@ def rank_program(g, core, T, topo):
             ACT(R("YP", 0, 8), R("XY%d" % e, 0, 8))
             ACT(R("YP", 8, 16), R("XY%d" % e, 8, 16), F.Copy, bias=-float(JO))
             dma("s", (T.yp[:], EXT), R("YP"))
-    ACT(R("YZ"), R("Z%d" % e), F.Copy, bias=-128.0, scale=-1.0)
-    dma("s", (T.yz[:], EXT), R("YZ"))
+    ACT(R("Zin"), R("Z%d" % e), F.Copy, bias=-128.0, scale=-1.0)
+    dma("s", (T.yz[:], EXT), R("Zin"))
     for k in arrange():
         calls[k][1]()
     for s, n in sorted(count.items()):

from concourse.mybir import AluOpType as A, ActivationFunctionType as F

ROT = 315
W, NI, NJ = 4096, 2048, 1536
JO = 288
EPS, EPS0, SIG = 1.0 / 16, 1.0 / 4, 1.0 / 2
BIGA, BIG0 = 2.0 ** 15, 2.0 ** 11
LIFT = BIGA * 15 * EPS + BIG0 * EPS0
MAGIC = 1.5 * 2 ** 23
CLIP = float(128 * 6144 + 64)
ROUNDS = 4
NV = 9
NS = 16 - NV
NPER = (40 * NV + 15) // 16
NSE = [11, 11, 11, 11]
FIRST = 2
OUTS = (2, 4, 6, 0)
ZS = 2
PIECES = [(0, 0, 9), (1, 0, 9), (2, 0, 9), (3, 0, 9), (4, 0, 5), (4, 5, 9)]
CHUNKS = {"VA": ("pA", 0, 2), "VB": ("pB", 2, 4), "VC": ("pA", 4, 5), "SA": ("pC", 0, 4), "SB": ("pD", 4, 6), "SC": ("pC", 6, 7)}
ON_SCALAR = "Asb C2 FS MT OT UW WN ext farU mo nlo nm".split()
KEYS = {"VA": "pJ", "SA": "pH", "VB": "pM", "SB": "pH", "VC": "pJ", "SC": "pM"}
ORDER = ("gs0 ms0 gs1 gs2 gv0 gs3 gv1 mv0 aVA mv1 gv2 ms1 ms2 ms3 rVA gv3 KVA aSA gs4 mv2 rSA mv3 aVB kSA eVA gv4 mv4 ms4 rVB gs5 gv5 mv5 "
         "ms5 aSB gs6 ms6 aVC rVC KVB aSC kVC rSC rSB eVC eVB kSB kSC eSC").split()
GATHER, WAKE, HOLD = 1.3, 60.0, 2.0
STEP = 100.0
SHIFT = {}
ZG = 1
RATE = 280.0
SHARE = {6: 2}
YS = ()

SB = {}
POOL = {}
USED = {"poolF": 0, "poolI": 0}


def _sb(names, shape, dtype="float32"):
    for n in names.split():
        SB[n] = ("sbuf", [128] + shape, dtype)


def _small(names, width, dtype="float32"):
    p = "poolF" if dtype == "float32" else "poolI"
    for n in names.split():
        POOL[n] = (p, USED[p], width)
        USED[p] += width


_small("hiI loI QC", 24, "int32")
_small("rhoI q3 FC far", 8, "int32")
_small("mki cI", 8 * ROUNDS, "int32")
_small("repI", 8 * NV + 48, "int32")
_small("PI P15i P12i", 1, "int32")

_small("KJ nm val", 8)
_small("cf cn", 8 * ROUNDS)
_small("UW YP NEW", 16)
_small("Asb nlo", 24)
_small("sO cK", 56)
_small("DM", 8 * NS)
_small("FU", 2 * NPER)
_small("FUa FUb", NPER)
_small("P15 SLO SHI S2L S2H R2B C2B BIA BIB CKR CKC T0 T1 T8 T9 QA QB QB8 QJ1 QJ2 QJ3 P7 P16 P45 LFT QRT R0 RA WX EN EZ", 1)
_sb("poolF", [USED["poolF"]])
_sb("poolI", [USED["poolI"]], "int32")
_sb("prowI pcolI", [8], "int32")
_sb("smallU", [16], "uint16")
POOL["rhoU"], POOL["farU"] = ("smallU", 0, 8), ("smallU", 8, 8)
for _t in range(ROUNDS + 1):
    _sb("XY%d" % _t, [16], "uint16")
    _sb("Z%d" % _t, [128], "bfloat16")
_sb("XYs", [16], "uint16")
_sb("repU", [8 * NV + 48], "uint16")
_sb("Zs Zin IDb NIDb I128 C128 AVG", [128], "bfloat16")
_sb("YT", [512], "bfloat16")
_sb("OFV", [2, 2, 8, NV], "bfloat16")
_sb("OFS", [5, 2, 8, 4], "bfloat16")
_sb("ST1", [16], "float16")
_sb("ST2", [8], "float16")
_sb("BBb", [8, 16], "bfloat16")
_sb("XM0 XM1", [NI], "int32")
_sb("MW", [W + 128], "bfloat16")
_sb("YF", [W + ROT], "bfloat16")
_sb("IOTA", [NI])
_sb("C16", [8, 16])
_sb("ONE BB OFF C16m C8 C8m CAL IDf NIDf OHW OT IPs MT NZf CT", [128])
_sb("sJ0 sJ1 sJ2 sJ3 sA sB sI PK0 PK1 IDh I15 I11 I16 SELI SELJ CD R2 C2 NM U WN", [128], "float16")
_sb("sN", [56], "float16")
_sb("mo", [16], "float16")
_sb("RZ", [5, 8, NS], "float16")
_sb("SEL0 SEL1", [8, 2, 32], "float16")
_sb("MKB", [256], "float16")
for _n, (_b, _lo, _hi) in CHUNKS.items():
    _sb("R" + _n, [_hi - _lo, 2, 8 * NV] if _n[0] == "V" else [5, 2, 8 * (_hi - _lo)], "float16")
_sb("KV KS", [5, 8, 16], "float16")
_sb("RHO ZEb", [512], "bfloat16")
_sb("NIO", [128], "bfloat16")
_sb("EXPM", [32, 64], "bfloat16")
_sb("RST", [512])
_sb("M1", [512], "int32")
_sb("RS16 NSC", [256])
_sb("OHA OHB", [64])
_sb("SG B32 BP W0", [256], "bfloat16")
_sb("HOH NHO", [768], "bfloat16")
_sb("HIO", [384], "bfloat16")
_sb("LOH", [24, 130], "bfloat16")
_sb("LIO", [129])
_sb("Fq", [8, 16, 5], "int32")
_sb("FiS", [8, NS, 5], "int32")
_sb("FiV", [40 * NV], "int32")
_sb("perU", [NPER + NPER % 2], "uint16")
_sb("FS", [8, NS, 6], "uint16")
_sb("FV", [16 * NPER], "uint16")
_sb("Zr", [128 * NV], "float16")
_sb("Z4x", [32 * NV], "float16")
_sb("EV", [5, 128 * NV], "float16")
_sb("ES", [NS, 640], "float16")
for _n, _s in (("pA", [2, 2, 8, 16]), ("pB", [2, 2, 8, 16]), ("pC", [8, 2, 8, 4]), ("pD", [8, 2, 8, 4]), ("pE", [512]),
               ("pH", [512]), ("pJ", [512]), ("pM", [512])):
    SB[_n] = ("psum", [128] + _s, "float32")
PSUMS = ("pA", "pB", "pC", "pD", "pE", "pH", "pJ", "pM")
SCRATCH = SB
NDMA = 70
SEMAPHORES = ["qv", "qt", "qs", "qg"] + ["d%d" % k for k in range(NDMA)] + \
    [p + "%d" % k for p in ("rn", "rz", "ln", "lz") for k in range(ROUNDS)]


def rank_program(g, core, T, topo):
    rank = T.rank_of(core)
    if rank is None:
        return
    queues = {"v": g.vector, "t": g.tensor, "s": g.scalar, "g": g, "y": g.sync}
    count = {}
    known = {q: {} for q in queues}
    past = {}
    ndma = [0]

    def need_waits(q, reads, writes, is_dma):
        deps = []
        for regs, w in ((reads, False), (writes, True)):
            for (n, lo, hi) in regs:
                bank = n in PSUMS
                for (plo, phi, pw, pq, sem, val, kn) in past.get(n, ()):
                    same = pq == q and not is_dma
                    if bank:
                        if same and not (pw or w):
                            continue
                    elif phi <= lo or plo >= hi or not (pw or w):
                        continue
                    if same and q == "t":
                        continue
                    deps.append((sem, val, kn))
        for sem, val, kn in sorted(deps, key=lambda d: -d[1]):
            if known[q].get(sem, 0) < val:
                queues[q].wait_ge(T.sem[sem], val)
                known[q][sem] = val
                for s2, v2 in kn.items():
                    if known[q].get(s2, 0) < v2:
                        known[q][s2] = v2

    def note(q, sem, val, reads, writes, kn):
        for regs, w in ((reads, False), (writes, True)):
            for (n, lo, hi) in regs:
                lst = past.setdefault(n, [])
                if n in PSUMS:
                    lst[:] = [p for p in lst if p[3] != q or (p[2] and not w)]
                elif w:
                    lst[:] = [p for p in lst if not (lo <= p[0] and p[1] <= hi)]
                else:
                    lst[:] = [p for p in lst if not (p[3] == q and not p[2] and lo <= p[0] and p[1] <= hi)]
                lst.append((lo, hi, w, q, sem, val, kn))

    def regs_of(*refs):
        out = []
        for r in refs:
            if isinstance(r, tuple):
                out += r[1]
        return out

    calls = []

    def size(ap):
        n = 1
        for k in list(ap.shape)[1:]:
            n *= k
        return n

    def narrow(ref):
        return SB[ref[1][0][0]][2] in ("bfloat16", "float16", "uint16")

    def emit(q, call, reads, writes, ns):
        def issue():
            sem = "q" + q
            need_waits(q, reads, writes, False)
            inst = call()
            count[sem] = count.get(sem, 0) + 1
            inst.then_inc(T.sem[sem], 1)
            note(q, sem, count[sem], reads, writes, dict(known[q]))
        calls.append((q, issue, reads, writes, ns, 0.0, 60.0 if q == "t" else 0.0))

    def dma(q, out, in_, after=(), more=()):
        pairs = [(out, in_)] + list(more)
        reads, writes = regs_of(*[p[1] for p in pairs]), regs_of(*[p[0] for p in pairs])

        def issue():
            sem = "d%d" % ndma[0]
            ndma[0] += 1
            need_waits(q, reads + list(after), writes, True)
            for o, i in pairs:
                queues[q].dma_start(o[0], i[0]).then_inc(T.sem[sem], 16)
            count[sem] = 16 * len(pairs)
            note(sem, sem, count[sem], reads, writes, dict(known[q]))
        side = out if out[1] else in_
        nbytes = len(pairs) * side[0].shape[0] * size(side[0]) * (2 if narrow(side) else 4)
        calls.append((q, issue, reads + list(after), writes, 60.0 * len(pairs), 60.0 + nbytes / RATE, 1700.0))

    def cost_v(out, *ins):
        n = size(out[0])
        if len(ins) and len(ins[0]) == 3:
            return 50 + GATHER * n
        r = 0.5 if all(narrow(a) for a in (out,) + ins) else 1.0
        if len(ins) == 2 and not any(a[1][0][0] in PSUMS for a in ins):
            r *= 2
        return 45 + 0.83 * max(64, r * n)

    def arrange():
        seen, before, after = {}, [], [[] for _ in calls]
        for k, (q, _, reads, writes, _, _, _) in enumerate(calls):
            deps = set()
            for regs, w in ((reads, False), (writes, True)):
                for (n, lo, hi) in regs:
                    for (plo, phi, pw, pq, j) in seen.get(n, ()):
                        if (pw or w or pq != q) if n in PSUMS else (phi > lo and plo < hi and (pw or w)):
                            deps.add(j)
            for regs, w in ((reads, False), (writes, True)):
                for (n, lo, hi) in regs:
                    lst = seen.setdefault(n, [])
                    if w:
                        lst[:] = [p for p in lst if not (n in PSUMS or (lo <= p[0] and p[1] <= hi))]
                    lst.append((lo, hi, w, q, k))
            before.append(deps)
            for j in deps:
                after[j].append(k)
        def written(n, lo, hi):
            return ([m for m, (p, base, width) in POOL.items() if p == n and base <= lo < base + width] + [n.rstrip("0123456789")])[0]
        way = [-STEP * (k + (SHIFT.get(written(*c[3][0]), 0) if c[3] else 0)) for k, c in enumerate(calls)]

        def sweep(before, after, way):
            left = [len(d) for d in before]
            ready = {k: 0.0 for k in range(len(calls)) if not left[k]}
            free = {q: 0.0 for q in queues}
            engines, order, soon, end = 0.0, [], {}, [0.0] * len(calls)
            while ready:
                start = {k: max(t, free[calls[k][0]]) for k, t in ready.items()}
                first = min(start, key=lambda k: (start[k], -way[k], k))
                q, t0 = calls[first][0], start[first]
                mine = [k for k in ready if calls[k][0] == q]
                k = max(mine, key=lambda k: (way[k] - HOLD * (start[k] - t0), -k))
                if len(order) < loads:
                    k = len(order)
                    q = calls[k][0]
                elif start[k] > t0:
                    fits = [m for m in mine if start[m] == t0 and t0 + calls[m][4] <= start[k]]
                    if not fits:
                        free[q] = min(start[k], t0 + WAKE)
                        continue
                    k = max(fits, key=lambda m: (way[m], -m))
                free[q] = done = start[k] + calls[k][4]
                if calls[k][5]:
                    engines = max(done + 0.7 * calls[k][6], engines) + calls[k][5]
                    done = engines + 0.3 * calls[k][6]
                else:
                    done += calls[k][6]
                del ready[k]
                order.append(k)
                end[k] = done
                for j in after[k]:
                    left[j] -= 1
                    soon[j] = max(soon.get(j, 0.0), done + WAKE)
                    if not left[j]:
                        ready[j] = soon[j]
            return order, end
        return sweep(before, after, way)[0]

    def R(n, lo=0, hi=None, step=1):
        if n in POOL:
            p, base, width = POOL[n]
            hi = width if hi is None else hi
            n, lo, hi = p, base + lo, base + hi
        elif hi is None:
            hi = SB[n][1][1]
        rows = [(n, -2, 0)] if n == "MW" and lo < W else []
        return (T[n][:, lo:hi:step] if step > 1 else T[n][:, lo:hi], [(n, lo, hi)] + rows)

    def X(ap, n, lo=0, hi=1 << 20):
        return (ap, [(n, lo, hi)])

    def ALL(n):
        return X(T[n][:], n)

    def IND(win, offs):
        return (win[0].indirect(offs[0]), win[1] + offs[1], True)

    def val(x):
        return x[0] if isinstance(x, tuple) else x

    def TT(out, a, b, op):
        emit("v", lambda: g.vector.tensor_tensor(out[0], a[0], b[0], op), regs_of(a, b), out[1], cost_v(out, a, b))

    def TS(out, a, s1, s2, op0, op1=None):
        if op1 is None:
            emit("v", lambda: g.vector.tensor_scalar(out[0], a[0], val(s1), None, op0), regs_of(a, s1), out[1], cost_v(out, a))
        else:
            emit("v", lambda: g.vector.tensor_scalar(out[0], a[0], val(s1), val(s2), op0, op1), regs_of(a, s1, s2), out[1], cost_v(out, a))

    def TC(out, a):
        emit("v", lambda: g.vector.tensor_copy(out[0], a[0]), regs_of(a), out[1], cost_v(out, a))

    def MS(out, c):
        emit("v", lambda: g.vector.memset(out[0], c), [], out[1], cost_v(out))

    def SCAN(out, d0, d1, init, op0, op1):
        emit("v", lambda: g.vector.tensor_tensor_scan(out[0], d0[0], d1[0], init, op0, op1), regs_of(d0, d1), out[1], cost_v(out, d0))

    def ACT(out, a, func=F.Identity, bias=0.0, scale=1.0):
        n = size(out[0])
        emit("s", lambda: g.scalar.activation(out[0], a[0], func, bias=val(bias), scale=val(scale)), regs_of(a, bias, scale), out[1],
             65 + (GATHER * n if len(a) == 3 else 0.83 * max(64, n)))

    def AFFINE(name, out, a, scale=1.0, bias=0.0):
        if name in ON_SCALAR:
            ACT(out, a, F.Identity if isinstance(bias, tuple) else F.Copy, bias=bias, scale=scale)
        else:
            TS(out, a, scale, bias, A.mult, A.add)

    def MM(items):
        def go():
            inst = None
            for (o, l, r, st, sp) in items:
                inst = g.tensor.matmul(o[0], l[0], r[0], st, sp)
            return inst
        emit("t", go, regs_of(*[r for it in items for r in it[1:3]]), regs_of(*[it[0] for it in items]),
             sum(0.42 * (1 if narrow(it[1]) else 4) * max(min(64, size(it[1][0])), size(it[2][0])) for it in items))

    def ACC(out, pairs, start=True, stop=True):
        MM([(out, l, r, start and k == 0, stop and k == len(pairs) - 1) for k, (l, r) in enumerate(pairs)])

    def IOTA(out, pattern, base, cm, f=True, after=()):
        if f:
            emit("g", lambda: g.iota(out[0], pattern, base, cm, allow_small_or_imprecise_dtypes=True), list(after), out[1], 130 + 1.66 * size(out[0]))
        else:
            emit("g", lambda: g.iota(out[0], pattern, base, cm), [], out[1], 130 + 1.66 * size(out[0]))

    def AFF(out, in_, pattern, op, fill, base, cm):
        emit("g", lambda: g.affine_select(out[0], in_[0], pattern, op, fill, base, cm), in_[1], out[1], 170 + 1.66 * size(out[0]))

    def remote(t, kind, dst, src):
        sh = 1 + t % 3
        to = T.cores[(rank + sh) % 4]
        rid, pid, _ = topo.addr(to)
        ls, rs = "l%s%d" % (kind, t), "r%s%d" % (kind, t)
        frm = T.cores[(rank - sh) % 4]
        lands = [(dst, 0, SB[dst][1][1])]

        def issue():
            need_waits("g", src[1], [], True)
            g.remote_dma(T[dst][:], src[0], T.sem[rs], T.sem[ls], pid, rid, topo.mask(core, to))
            count[ls] = len(topo.engines(core, to))
            note(ls, ls, count[ls], src[1], [], dict(known["g"]))
            count[rs] = len(topo.engines(frm, core))
            note(rs, rs, count[rs], [], lands, {})
        calls.append(("g", issue, src[1], lands, 2900.0 if ls == "ln0" else 900.0, 0.0, 3300.0 + 5.3 * size(src[0])))

    eq, ge, SHR, AND, mul, add = A.is_equal, A.is_ge, A.arith_shift_right, A.bitwise_and, A.mult, A.add
    EXT = []

    def blank(h):
        n = "XM%d" % h
        MS(X(T[n][:, 0:JO], n, 0, 8), 0)
        MS(X(T[n][:, JO + NJ:NI], n, 0, 8), 0)

    def mates(h, qs, after=()):
        n = "XM%d" % h
        for k in range(8):
            dma(qs[k % 2], X(T[n][16 * k + 8:16 * k + 16, JO:JO + NJ], n, 8 + k, 9 + k), (T.cmate[16 * k + 8 * h:16 * k + 8 * h + 8, :], EXT), after)
        for k in range(8):
            dma(qs[k % 2], X(T[n][16 * k:16 * k + 8, 0:NI], n, k, k + 1), (T.rmate[16 * k + 8 * h:16 * k + 8 * h + 8, :], EXT), after)
    blank(0)
    dma("y", R("prowI"), (T.prow[:], EXT))
    dma("s", R("pcolI"), (T.pcol[:], EXT))
    mates(0, "ys")
    dma("s", R("Zin"), (T.need[:], EXT))
    dma("y", X(T.MW[:, ROT:W], "MW", ROT, W), (T.fig[:, 0:W - ROT], EXT))
    dma("s", X(T.MW[:, 0:ROT], "MW", 0, ROT), (T.fig[:, W - ROT:W], EXT))
    loads = len(calls)

    MS(R("ONE"), 1.0)
    MS(R("FU"), 0.0)
    IOTA(R("PI"), [[1, 1]], 0, 1, False)
    AFF(R("BB"), R("ONE"), [[-16, 8], [0, 16]], ge, 0.0, 0, 1)
    AFF(R("BB"), R("BB"), [[16, 8], [0, 16]], ge, 0.0, 15, -1)
    IOTA(ALL("C16"), [[0, 8], [1, 16]], 0, 0)
    IOTA(R("C8"), [[0, 16], [1, 8]], 0, 0)
    IOTA(R("CAL"), [[0, 8], [1, 2], [0, 8]], 0, 0)
    IOTA(R("IOTA", 0, NI // 2), [[1, NI // 2]], 0, 0)
    AFF(R("IDh"), R("ONE"), [[-1, 128]], eq, 0.0, 0, 1)
    IOTA(R("FU", 0, 5 * NV), [[1, 5], [5, NV]], 0, 0)
    IOTA(R("repI", 0, 2 * NV), [[1, NV], [64, 2]], 0, 0, False)

    def LIN(n, m, scale, bias):
        ACT(R(n), R(m), F.Identity if isinstance(bias, tuple) else F.Copy, bias=bias, scale=scale)
    TS(R("P15i"), R("PI"), 15, None, AND)
    TS(R("P12i"), R("PI"), 12, None, AND)
    TC(R("P15"), R("P15i"))
    TS(R("SLO"), R("P15"), 8.0, None, A.is_lt)
    TS(R("SHI"), R("P15"), 8.0, None, ge)
    TS(R("R0"), R("P15"), 0.0, None, eq)
    for n, r, c in (("T0", 0.0, 512.0), ("T1", 1.0, 2.125), ("T8", 8.0, 512.0), ("T9", 9.0, 2.125)):
        TS(R(n), R("P15"), r, c, eq, mul)
    TS(R("QA"), R("SHI"), -50.0, R("P15"), mul, add)
    TS(R("QB8"), R("SLO"), -50.0, R("P15"), mul, add)
    for n, m, scale, bias in (("CKC", "T0", 1.0, R("T1")), ("CKR", "T8", 1.0, R("T9")), ("QB", "QB8", 1.0, -8.0), ("QJ1", "QA", 1.0, -2.0),
                              ("QJ2", "QA", 1.0, -4.0), ("QJ3", "QA", 1.0, -6.0), ("S2H", "SHI", 2.0, 0.0), ("C2B", "SHI", -4097.0, 1.0),
                              ("S2L", "SLO", 2.0, 0.0), ("R2B", "SLO", 2.0 * (JO - 2048) - 1, 1.0), ("BIA", "SLO", -4096.0, 0.0),
                              ("BIB", "SHI", -4096.0, 0.0), ("P7", "SHI", -8.0, R("P15")), ("P45", "P7", 5.0 * NV, 0.0),
                              ("EZ", "R0", EPS - EPS0, -128.0 - EPS), ("EN", "R0", EPS0 - EPS, 128.0 + EPS), ("P16", "P12i", 4.0, 0.0)):
        LIN(n, m, scale, bias)
    TS(R("OFF"), R("BB"), -999.0, 999.0, mul, add)
    for n, m in (("C8m", "C8"), ("CAL", "CAL"), ("C16m", "C16")):
        TT(R(n), ALL(m), R("OFF"), add)
    TS(R("sI"), R("C8m"), R("QB"), R("CKC"), eq, add)
    for a in range(4):
        TS(R("sJ%d" % a), R("CAL"), R("QJ%d" % a if a else "QA"), R("CKR"), eq, add)
    TS(R("sA"), R("C16m"), R("QA"), R("CKR"), eq, add)
    TS(R("sB"), R("C16m"), R("QB8"), None, eq)
    ACT(R("XY0", 0, 8), R("prowI"))
    ACT(R("XY0", 8, 16), R("pcolI"), F.Copy, bias=float(JO))
    ACT(R("IOTA", NI // 2, NI), R("IOTA", 0, NI // 2), F.Copy, bias=float(NI // 2))
    TS(R("FUa"), R("FU", 0, 2 * NPER, 2), R("SLO"), R("P45"), mul, add)
    TS(R("FUb"), R("FU", 1, 2 * NPER, 2), R("SHI"), None, mul)
    TT(R("FUa"), R("FUa"), R("FUb"), add)
    TC(R("perU", 0, NPER), R("FUa"))
    ACT(R("repU", 0, 2 * NV), R("repI", 0, 2 * NV), bias=R("P16"))
    ACT(R("Z0"), R("Zin"), F.Copy, bias=-128.0, scale=-1.0)

    def late_constants():
        G8 = R("BB", 0, 128, 16)
        MS(R("AVG"), 1.0 / 128)
        for n, offs in (("OFV", (15.0 / 32, -1.0 / 8)), ("OFS", (-15.0 / 32, -3.0 / 8))):
            for w in range(2):
                MS(X(T[n][:, :, w], n, w, w + 1), offs[w])
        MS(R("C128"), 128.0)
        MS(R("ZEb"), 0.0)
        LIN("RA", "R0", -1.0, 1.0)
        LIN("WX", "R0", BIGA - BIG0, -BIGA)
        ACT(R("ST1", 0, 8), G8, scale=R("RA"))
        ACT(R("ST1", 8, 16), G8, scale=R("R0"))
        ACT(R("ST2"), G8, scale=R("WX"))
        ACT(ALL("BBb"), R("BB"))
        TS(R("DM"), X(T.C16[:, :, NV:16], "C16"), R("P15"), None, eq)
        IOTA(R("RHO"), [[0, 8], [1, 16], [16, 4]], 0, 0)
        for n, c in (("IDb", 1.0), ("I15", BIGA), ("I11", BIG0), ("I16", 1.0 / 16), ("SELI", 2048.0)):
            ACT(R(n), R("IDh"), scale=c)
        MS(R("LFT"), LIFT)
        AFF(R("CD"), R("AVG"), [[0, 16], [-16, 8]], ge, 0.0, 0, 1)
        AFF(R("CD"), R("CD"), [[0, 16], [16, 8]], ge, 0.0, 15, -1)
        ACT(R("CD"), R("CD"), scale=-8.0)
        blank(1)
        figs = R("MW", 0, W)[1]
        for h in range(2):
            dma("y", R("B32", 128 * h, 128 * h + 128), X(T.MW[64 * h:64 * h + 64:16, 0:W], "MW", -2, W))
        mates(1, "yy", figs)

    def key_constants():
        for n, kp, lo, hi, sc, se in (("SEL0", "KV", NV, 16, 16, 1), ("SEL1", "KS", 0, NV, 1, 8)):
            AFF(X(T[kp][:, :, :, lo:hi], kp, 9, 10), R("ZEb", 0, 40 * (hi - lo)), [[0, 40 * (hi - lo)]], ge, 0.0, 0, 0)
            for h in range(2):
                AFF(X(T[n][:, :, h, :], n, h, h + 1), R("ZEb", 0, 256), [[-sc, 8], [0, 8], [-2 * se, 4]], A.not_equal, 2048.0, -h * se, 1)
            for h in range(2):
                AFF(X(T[n][:, :, h, :], n, h, h + 1), X(T[n][:, :, h, :], n, h, h + 1), [[-sc, 8], [-se, 8], [0, 4]], A.not_equal, 2048.0, -8 * se, 1)
        AFF(R("SELJ"), R("ZEb", 0, 128), [[-1, 8], [-8, 16]], A.not_equal, 2048.0, 0, 1)
        IOTA(R("OHA"), [[1, 8], [0, 8]], 0, 0)
        IOTA(R("KJ"), [[16, 8]], W, 0)
        AFF(R("RST"), R("ZEb"), [[0, 8], [1, 64]], A.not_equal, CLIP, 0, 0)
        IOTA(R("RS16"), [[0, 16], [-16384, 16]], 8192, 0)
        for h in range(2):
            IOTA(R("repI", 8 * NV + 24 * h, 8 * NV + 24 * h + 24), [[8, 3], [1, 4], [0, 2]], 4 * h, 0, False)
        IOTA(ALL("HIO"), [[0, 12], [1, 32]], 0, 0)
        IOTA(R("NIO"), [[-1, 128]], 0, 0)

    def last_constants():
        G8 = R("BB", 0, 128, 16)
        for w in range(2):
            TS(R("MKB", 128 * w, 128 * w + 128), ALL("C16"), R("P15"), 4096.0, A.not_equal, mul)
        ACT(R("KJ"), R("KJ"), bias=R("P15"))
        for n, c in (("IDf", 1.0), ("NIDf", -1.0)):
            ACT(R(n), R("IDh"), scale=c)
        MS(R("OHW", 64, 128), 0.0)
        TS(R("OHB"), R("C8", 0, 64), R("QB"), None, eq)
        TS(R("OHA"), R("OHA"), R("P15"), None, eq)
        TT(R("OHW", 0, 64), R("OHA"), R("OHB"), add)
        for w, s in enumerate(("SHI", "SLO")):
            ACT(R("PK%d" % w), R("BB"), scale=R(s))
        MS(R("sO"), 0.0)
        MS(R("cK"), 4113.0 / 128)
        for lo, hi in ((0, 8), (32, 40), (48, 56)):
            AFF(R("cK", lo, hi), R("cK", lo, hi), [[0, 8]], A.is_gt, 0.0, 0, 0)
        TS(R("sO", 0, 8), G8, R("T0"), 1.0 / 512, mul, mul)
        TS(R("sO", 32, 40), G8, R("T8"), 1.0 / 512, mul, mul)
        for k, s in enumerate((0.0, "S2H", "S2H", "S2L", 0.0, "S2L", "SHI")):
            ACT(R("sN", 8 * k, 8 * k + 8), G8, scale=R(s) if s else s)
        ACT(R("repU", 8 * NV, 8 * NV + 48), R("repI", 8 * NV, 8 * NV + 48))
        ACT(R("LIO"), R("IOTA", 0, 129), F.Copy, bias=-0.5)

    def suppress(ns, then):
        for h, bank in enumerate(("pH", "pE")):
            n0, n1 = 12 * h, 12 * h + (ns + 1 - h) // 2
            col = {n: 8 * (n % 12 // 4) + 4 * h + n % 4 for n in range(n0, n0 + 12)}
            for n in range(n0, n1):
                ACT(X(T.LOH[:, n, 0:129], "LOH", n, n + 1), R("LIO"), F.Sign, bias=R("nlo", col[n], col[n] + 1), scale=R("val", col[n] % 8, col[n] % 8 + 1))
            for a, b in ((n0, n1), (n1, n0 + 12)):
                TT(R("HOH", 32 * a, 32 * b), IND(R("hiI"), R("repU", 8 * NV + 2 * a, 8 * NV + 2 * b)), R("HIO", 0, 32 * (b - a)), eq)
                if a == n0:
                    TS(R("NHO", 32 * n0, 32 * n1), R("HOH", 32 * n0, 32 * n1), -1.0, None, mul)
            mine, theirs = list(range(n1, n0 + 12)), list(range(n0, n1))
            runs = [theirs[:3], theirs[3:] + mine[:2], mine[2:-1], mine[-1:]]
            order = sum(runs, [])
            for run in runs:
                for n in run:
                    if n >= n1:
                        TS(X(T.LOH[:, n, 1:129], "LOH", n, n + 1), R("NIO"), R("nlo", col[n], col[n] + 1), R("val", col[n] % 8, col[n] % 8 + 1), eq, mul)
                MM([(X(T[bank][32 * (n % 4):32 * (n % 4) + 32, 0:128], bank), R(side, 32 * n, 32 * n + 32), X(T.LOH[:, n, k:k + 128], "LOH", n, n + 1),
                     False, k == 1 and not any(f % 4 == n % 4 for f in order[order.index(n) + 1:]))
                    for n in run for k, side in enumerate(("NHO", "HOH")) if k or n < n1])
            then(h, R(bank, 0, 128))

    def row0(src, h):
        dma("y", X(T.MW[64 * h:64 * h + 64:16, 0:W], "MW", -2 + h, -1 + h), R(src, 128 * h, 128 * h + 128))

    def mates_names(t):
        xy = "XY%d" % t
        LX, LY = R(xy, 0, 8), R(xy, 8, 16)
        XM = R("XM%d" % (t % 2))
        AFFINE("C2", R("C2"), IND(XM, LY), R("S2H"), R("C2B"))
        AFFINE("R2", R("R2"), IND(XM, LX), R("S2L"), R("R2B"))
        AFFINE("U", R("U"), IND(R("IOTA"), LX), R("S2L"), R("BIA"))
        AFFINE("WN", R("WN"), IND(R("IOTA"), LY), R("S2H"), R("BIB"))
        ACC(R("pM", 256, 384), [(R("sI"), R("C2"))])
        MM([(R("pJ", 128 * a, 128 * a + 128), R("sJ%d" % a), R("R2"), True, True) for a in range(4)])
        AFFINE("IPs", R("IPs"), R("pM", 256, 384))

    mates_names(0)
    for t in range(ROUNDS):
        xy, z = "XY%d" % t, "Z%d" % t
        win = "MW"
        ACC(R("pM", 128, 256), [(R("IDh"), R("U")), (R("IDh"), R("WN"))])
        ACC(R("pM", 0, 128), [(R("sA"), R("R2")), (R("sB"), R("C2"))])
        AFFINE("OT", R("OT"), R("pM", 128, 256), 1.0, 4113.0)
        for a in range(4):
            TT(X(T.Fq[:, :, :, 1 + a], "Fq", 1 + a, 2 + a), R("pJ", 128 * a, 128 * a + 128), R("IPs"), mul)
        TT(X(T.Fq[:, :, :, 0], "Fq", 0, 1), R("pM", 0, 128), R("OT"), mul)
        ACT(R("Z4x"), IND(R(z), R("repU", 0, 2 * NV)), bias=R("EZ"), scale=-1.0)
        TS(ALL("FiS"), X(T.Fq[:, :, NV:16, :], "Fq"), 5, W - 1, SHR, AND)
        TS(R("FiV"), X(T.Fq[:, :, 0:NV, :], "Fq"), 5, W - 1, SHR, AND)
        AFFINE("NZf", R("NZf"), R(z), 1.0, R("EN"))
        AFFINE("FS", X(T.FS[:, :, :, 0:5], "FS"), ALL("FiS"))
        AFFINE("FV", R("FV"), IND(R("FiV"), R("perU", 0, NPER)))
        for k in range(4):
            zr = X(T.Zr[:, k:128 * NV:4], "Zr", k, k + 1)
            if k >= 4 - ZG and t:
                AFF(zr, R("Z4x"), [[0, 32 * NV]], ge, 0.0, 0, 0)
            else:
                (ACT if k < ZS else TC)(zr, R("Z4x"))
        if t == 0:
            late_constants()
        bs = X(T.BBb[:, :, NV:16], "BBb")
        ACC(R("pE", 0, 8 * NS), [(R(z), bs), (R("C128"), bs)])

        def rectangles(kp, xs, sel0, sel, stop):
            reg = (lambda x: (x, x + 1)) if kp == "KV" else (lambda x: (0, NS))
            MM([(R("pE", x - 1, 512, 4) if x else ALL("pE"), (T[kp][:, x], [(kp,) + reg(x), (kp, 9, 10)]), ALL(sel if x else sel0), False, stop and x == xs[-1]) for x in xs])

        def step(s):
            k = s[2:]
            if s[1] == "v":
                x, p0, p1 = PIECES[int(k)]
                ev = [X(T.EV[:, x, 128 * p:128 * p + 128], "EV", NV * x + p, NV * x + p + 1) for p in range(NV)]
            if s[:2] == "gv":
                TT(X(T.EV[:, x, 128 * p0:128 * p1], "EV", NV * x + p0, NV * x + p1),
                   IND(R(win, 0, W), R("FV", 8 * (NV * x + p0), 8 * (NV * x + p1))),
                   X(T.Zr[:, 128 * p0:128 * p1], "Zr"), A.max)
            elif s[:2] == "gs":
                q = int(k)
                for c in range(8):
                    j = 16 * c + NV + q
                    out, figs = X(T.ES[:, q, c:640:8], "ES", 8 * q + c, 8 * q + c + 1), IND(R(win, 0, W), X(T.FS[:, c, q, 0:5], "FS"))
                    if c < SHARE.get(q, 0) and (t or q > 1):
                        TS(out, figs, R("NZf", j, j + 1), 0.0, add, A.max)
                    else:
                        ACT(out, figs, F.Relu, bias=R("NZf", j, j + 1))
            elif s[:2] == "mv":
                b, lo, hi = [c for n, c in CHUNKS.items() if n[0] == "V" and c[1] <= x < c[2]][0]
                mine = [n for n, pc in enumerate(PIECES) if lo <= pc[0] < hi]
                if int(k) == mine[0]:
                    ACC(X(T[b][:, 0:hi - lo, :, :, 0:NV], b), [(R("AVG"), X(T.OFV[:, 0:hi - lo], "OFV"))], True, False)
                MM([(X(T[b][:, x - lo, :, :, p], b), ev[p], R("ST1"), False, int(k) == mine[-1] and p == p1 - 1) for p in range(p0, p1)])
            elif s[:2] == "ms":
                q = int(k)
                b, lo, hi = [c for n, c in CHUNKS.items() if n[0] == "S" and c[1] <= q < c[2]][0]
                if q == lo:
                    ACC(X(T[b][:, 0:5, :, :, 0:hi - lo], b), [(R("AVG"), X(T.OFS[:, :, :, :, 0:hi - lo], "OFS"))], True, False)
                MM([(X(T[b][:, x, :, :, q - lo], b), X(T.ES[:, q, 128 * x:128 * x + 128], "ES", 8 * q, 8 * q + 8), R("ST1"), False,
                     q == hi - 1 and x == 4) for x in range(5)])
            else:
                b, lo, hi = CHUNKS[s[1:]]
                if s[1] == "V":
                    nx, n = hi - lo, NV
                    kp = X(T.KV[:, lo:hi, :, 0:NV], "KV", lo, hi)
                    data = [X(T.EV[:, x, 128 * p:128 * p + 128], "EV", NV * x + p, NV * x + p + 1) for x in range(lo, hi) for p in range(NV)]
                else:
                    nx, n = 5, hi - lo
                    kp = X(T.KS[:, :, :, NV + lo:NV + hi], "KS", lo, hi)
                    data = [X(T.ES[:, q, 128 * x:128 * x + 128], "ES", 8 * q, 8 * q + 8) for x in range(5) for q in range(lo, hi)]
                kb = KEYS[s[1:]]
                key = R(kb, 0, 8 * nx * n)
                if s[0] == "a":
                    MM([(R(kb, 8 * n * (k // n) + k % n, 8 * n * (k // n + 1), n), d, R("ST2"), k == 0, False) for k, d in enumerate(data)])
                elif s[0] == "r":
                    rn = "R" + s[1:]
                    TS(ALL(rn), X(T[b][:, 0:nx, :, :, 0:n], b), MAGIC, -MAGIC, add, add)
                    r = [X(T[rn][:, :, w, :], rn) for w in range(2)]
                    run = [(key, R("I15"), r[0]), (key, R("I11"), r[1]), (key, R("I16"), r[0]), (key, R("I16"), r[1])]
                    if s[1] == "S":
                        run += [(key, R("CD"), X(T.RZ[:, :, :, lo:hi], "RZ"))]
                    MM([it + (False, k == len(run) - 1) for k, it in enumerate(run)])
                elif s[0] == "e":
                    stop = s == [n for n in ORDER if n[0] == "e"][-1]
                    if s[1] == "V":
                        rectangles("KV", range(lo, hi), "SEL0", "SELI", stop)
                    else:
                        rectangles("KS", range(5), "SEL1", "SELJ", stop)
                elif s[0] == "K":
                    ACT(kp, key, F.Relu, bias=R("LFT") if s[1] == "S" else 0.0)
                else:
                    TS(kp, key, LIFT if s[1] == "S" else 0.0, 0.0, add, A.max)
            if s == "gv1":
                if t == 1:
                    IOTA(X(T.EXPM[:], "EXPM") if True else 0, [[0, 2048]], 1, 0, True, [("RZ", 0, 5)])
                if t == 2:
                    AFF((T.EXPM[:], [("EXPM", 0, 1)]), (T.EXPM[:], [("EXPM", 0, 1), ("RZ", 0, 5)]), [[-1, 32], [-32, 4], [0, 16]], eq, 0.0, 0, 1)
            if s == "gv0":
                TT(X(T.RZ[:, 0], "RZ", 0, 1), R("pE", 0, 8 * NS), R("DM"), mul)
                ACC(ALL("pE"), [(R("IDb"), R("RHO"))], True, False)
                for x in range(1, 5):
                    AFF(X(T.RZ[:, x], "RZ", x, x + 1), X(T.RZ[:, 0], "RZ", 0, 1), [[0, 8 * NS]], ge, 0.0, 0, 0)
                if t == 0:
                    key_constants()
        for s in ORDER:
            step(s)
        AFFINE("mo", R("mo"), (R(xy)[0], R(xy)[1] + [("ES", 8 * NS - 1, 8 * NS)]), 1.0, -2048.0)
        AFFINE("ext", R(win, W, W + 128), (R(z)[0], R(z)[1] + [("ES", 8 * NS - 1, 8 * NS)]), -2.0, -255.0)
        if t == 1:
            MS(R("QRT"), -0.25)
            ACT(R("NIDb"), R("IDh"), scale=-1.0)
        if t == 0:
            last_constants()
            ACT(R("BP"), (R("B32")[0], R("B32")[1] + [("ES", 8 * NS - 1, 8 * NS)]), F.Copy, bias=SIG)
        SCAN(R("M1"), R("RST"), ALL("pE"), 0.0, A.max, A.min)
        MM([(R("pJ", 0, 256), R("IDh"), R("MKB"), True, False), (R("pJ", 256, 272), R("IDh"), R("mo"), False, False),
            (R("pJ", 272, 280), R("IDf"), R("KJ"), False, False)])
        ACC(R("pM", 0, 56), [(R("OT"), R("sO")), (R("ONE"), R("cK"))], True, False)
        ACC(X(T.pD[:, 0:2], "pD"), [(R("sA"), R("R2")), (R("sB"), R("C2"))])
        AFFINE("MT", R("MT"), X(T.pD[:, 0:2], "pD"), 0.5, -2056.5)
        mk = R("M1", 63, 512, 64)
        TS(R("rhoI"), mk, 127, None, AND)
        AFFINE("nm", R("nm"), mk, -1.0, CLIP)
        ACT(R("mki", 8 * t, 8 * t + 8), mk)
        MM([(R("pJ", 256 + 8 * w, 264 + 8 * w), R("NIDf" if w == 2 else "IDf"), R("nm"), False, False) for w in range(3)])
        AFFINE("rhoU", R("rhoU"), R("rhoI"))
        TT(R("NM"), IND(R("OHW"), R("rhoU")), R("MT"), mul)
        MM([(R("pJ", 128 * w, 128 * w + 128), R("PK%d" % w), R("NM"), False, w == 1) for w in range(2)])
        ACC(R("pM", 0, 56), [(R("NM"), R("sN"))], False)
        last = t == ROUNDS - 1
        for h, bank in enumerate(("pH", "pE")):
            ACC(R(bank, 0, 128), [(R("IDb"), R("W0" if t else "B32", 128 * h, 128 * h + 128))] +
                ([(R("NIDb"), R("BP", 128 * h, 128 * h + 128))] if last else []), True, False)
        NEW = R("NEW")

        def costs():
            TS(R("cI"), R("mki"), 7, None, SHR)
            TS(R("cn"), R("mki"), CLIP, -6145.0, eq, mul)
            ACT(R("cf"), R("cI"))
        AFFINE("Asb", R("Asb"), R("pM", 0, 24))
        ACT(R("val"), R("pM", 48, 56), F.Sign, scale=-1.0)

        def pass_names():
            SCAN(R("NSC"), R("RS16"), R("pJ", 0, 256), 0.0, A.max, A.min)
            TT(NEW, R("pJ", 256, 272), R("NSC", 15, 256, 16), A.min)
            AFFINE("XYs", R("XYs"), NEW, 1.0, 2048.0)
            remote(t, "n", "XY%d" % (t + 1), R("XYs"))
            AFFINE("UW", R("UW"), NEW, 2.0, 4113.0)

        def corners():
            TT(R("QC"), R("pM", 24, 48), R("Asb"), mul)
            TS(R("loI"), R("QC"), 5, 127, SHR, AND)
            TS(R("hiI"), R("QC"), 12, 31, SHR, AND)
            AFFINE("nlo", R("nlo"), R("loI"), -1.0)

        def pass_needs():
            TT(R("q3"), R("UW", 0, 8), R("UW", 8, 16), mul)
            TS(R("FC"), R("q3"), 5, W - 1, SHR, AND)
            TT(R("far"), R("pJ", 272, 280), R("FC"), A.max)
            AFFINE("farU", R("farU"), R("far"))
            ACT(R("Zs"), IND(R(win), R("farU")), F.Copy, bias=-127.6, scale=-0.5)
            remote(t, "z", "Z%d" % (t + 1), R("Zs"))
        if not last:
            pass_names()
            pass_needs()
            corners()
            def flags(h, counts):
                TT(R("W0", 128 * h, 128 * h + 128), counts, R("BP", 128 * h, 128 * h + 128), A.min)
                row0("W0", h)
            suppress(NSE[t], flags)
            mates_names(t + 1)
        else:
            row0("B32", 0)
            row0("B32", 1)
            corners()
            suppress(NSE[t], lambda h, counts: ACT(R("SG", 128 * h, 128 * h + 128), counts, F.Sign, bias=R("QRT"), scale=-1.0))
            pass_names()
            pass_needs()

    e = ROUNDS
    block = {"pA": lambda r, x: T.pA[r, x // 2, x % 2], "pB": lambda r, x: T.pB[r, x // 2, x % 2], "pC": lambda r, x: T.pC[r, 2 * x:2 * x + 2],
             "pD": lambda r, x: T.pD[r, 2 * x:2 * x + 2], "pE": lambda r, x: T.pE[r, 128 * x:128 * x + 128],
             "pJ": lambda r, x: T.pJ[r, 128 * x:128 * x + 128]}
    sent = 512
    for k, nm in ((1, "pE"), (2, "pB"), (3, "pC"), (4, "pD"), (5, "pA"), (6, "pB"), (7, "pC"), (0, "pE")):
        if k in YS:
            ACC(ALL(nm), [(R("I128"), R("MW", 512 * k, 512 * k + 512))], True, False)
        for bank, xs in ((("pA", range(2)), (nm, range(2, 4))) if k == 1 else ((nm, range(4)),)):
            MM([(X(block[bank](slice(64 * h, 64 * h + 64), x), bank), X(T.EXPM[:, 4 * k + x, :], "EXPM"), R("SG", 128 * h, 128 * h + 128),
                 k not in YS, k not in YS or x == 3) for x in xs for h in range(2)])
        if k in YS:
            ACT(R("YT"), ALL(nm), F.Abs, scale=128.0)
            ACT(R("YF", 512 * k, 512 * k + 512), R("YT"), F.Copy, bias=-128.0)
        elif k == 1:
            cut = 256
            TT(R("YF", 512, 512 + cut), R("MW", 512, 512 + cut), X(T.pA[:, 0], "pA"), mul)
            dma("y", (T.yf[:, 512 - ROT:512 + cut - ROT], EXT), R("YF", 512, 512 + cut))
            sent += cut
            TT(R("YF", 512 + cut, 1024), R("MW", 512 + cut, 1024), R(nm, cut, 512), mul)
        elif k:
            TT(R("YF", 512 * k, 512 * k + 512), R("MW", 512 * k, 512 * k + 512), ALL(nm), mul)
        else:
            TT(R("YF", ROT, 512), R("MW", ROT, 512), R(nm, ROT, 512), mul)
            dma("s", (T.yf[:, 0:512 - ROT], EXT), R("YF", ROT, 512))
            TT(R("YF", W, W + ROT), R("MW", 0, ROT), R(nm, 0, ROT), mul)
        if k in OUTS:
            upto = 512 * k + 512 if k else W + ROT
            dma("y", (T.yf[:, sent - ROT:upto - ROT], EXT), R("YF", sent, upto))
            sent = upto
        if k == 2:
            costs()
        if k == 5:
            ACC(X(T.pM[0:32, 0:128], "pM"), [(R("cf"), R("IDf")), (R("cn"), R("IDf"))])
            ACT(X(T.CT[0:32, :], "CT"), X(T.pM[0:32, 0:128], "pM"))
            for x in range(8):
                dma("s", (T.yc[x:x + 1, :], EXT), X(T.CT[0:32, 16 * x:16 * x + 16], "CT"))
            ACT(R("YP", 0, 8), R("XY%d" % e, 0, 8))
            ACT(R("YP", 8, 16), R("XY%d" % e, 8, 16), F.Copy, bias=-float(JO))
            dma("s", (T.yp[:], EXT), R("YP"))
    ACT(R("Zin"), R("Z%d" % e), F.Copy, bias=-128.0, scale=-1.0)
    dma("s", (T.yz[:], EXT), R("Zin"))
    for k in arrange():
        calls[k][1]()
    for s, n in sorted(count.items()):
        if known["g"].get(s, 0) < n:
            g.wait_ge(T.sem[s], n)
